import numpy as np
import ml_dtypes


def mxq(x, axis, fmt="e4m3"):
    dtype, down = {"e4m3": (ml_dtypes.float8_e4m3fn, 7), "e5m2": (ml_dtypes.float8_e5m2, 14)}[fmt]
    v = np.moveaxis(np.asarray(x, np.float32).astype(ml_dtypes.bfloat16).astype(np.float64), axis, -1)
    blocks = v.reshape(v.shape[:-1] + (-1, 32))
    amax = np.abs(blocks).max(-1, keepdims=True)
    byte = np.maximum(np.where(amax > 0, np.frexp(amax)[1] - 1 + 127, 0) - down, 1)
    scale = np.exp2(byte - 127.0)
    codes = (blocks / scale).astype(np.float32).astype(dtype).astype(np.float64)
    return np.moveaxis((codes * scale).reshape(v.shape), -1, axis)


WIDE = False


def mx_kscale(k):
    if not WIDE:
        return np.ones(k)
    levels = np.array([10, -10, 5, -5, 0])
    if k % 512:
        return np.exp2(np.random.permutation(np.resize(levels, k // 32))).repeat(32)
    a = np.empty((k // 512, 16))
    for p in range(k // 512):
        a[p, :8] = np.random.permutation(np.resize(levels, 8))
        for g in range(8):
            far = levels[np.abs(levels - a[p, g]) >= 10]
            a[p, g + 8] = far[np.random.randint(len(far))]
    return np.exp2(a.ravel()).repeat(32)


def f64(x):
    return np.asarray(x).astype(np.float64)


def striped(idx):
    return np.tile(idx.reshape(-1, 16).T, (8, 1)).astype(np.uint16)


def unstriped(offs):
    return offs[:16].T.reshape(-1).astype(np.int64)


E2M1 = np.array([0.0, 0.5, 1.0, 1.5, 2.0, 3.0, 4.0, 6.0, -0.0, -0.5, -1.0, -1.5, -2.0, -3.0, -4.0, -6.0])


def pack_weight(w, fmt):
    k, n = w.shape
    w = f64(np.asarray(w, np.float32).astype(ml_dtypes.bfloat16)).reshape(k // 32, 32, n)
    amax = np.abs(w).max(1)
    if fmt == "e4m3":
        byte = np.frexp(amax)[1] - 1 + 127 - 7
    else:
        mant, ex = np.frexp(amax / 6.0)
        byte = np.where(mant > 0.5, ex, ex - 1) + 127
    byte = np.clip(np.where(amax > 0, byte, 1), 1, 254)
    scaled = (w * np.exp2(127.0 - byte)[:, None, :]).reshape(k, n).astype(np.float32)
    by_word = np.ascontiguousarray(scaled.reshape(k // 512, 128, 4, n).transpose(0, 1, 3, 2))
    if fmt == "e4m3":
        words = by_word.astype(ml_dtypes.float8_e4m3fn).view(np.uint8)
    else:
        c = by_word.astype(ml_dtypes.float4_e2m1fn).view(np.uint8) & 0xF
        words = (c[..., 0::2] | (c[..., 1::2] << 4)).reshape(k // 512, 128, 2 * n)
    return np.ascontiguousarray(words), np.ascontiguousarray(byte.astype(np.uint8).reshape(k // 512, 16, n))


def unpack_weight(words, scales, fmt):
    g, _, n = scales.shape
    words = np.ascontiguousarray(words).reshape(g, 128, n, -1)
    if fmt == "e4m3":
        vals = words.view(ml_dtypes.float8_e4m3fn).astype(np.float64)
    else:
        nib = np.empty((g, 128, n, 4), np.uint8)
        nib[..., 0::2] = words & 0xF
        nib[..., 1::2] = words >> 4
        vals = E2M1[nib]
    vals = vals * np.repeat(np.exp2(scales.astype(np.float64) - 127.0), 8, axis=1)[..., None]
    return vals.transpose(0, 1, 3, 2).reshape(g * 512, n)


def gelu(v):
    return 0.5 * v * (1.0 + np.tanh(np.sqrt(2.0 / np.pi) * (v + 0.044715 * v**3)))


def striped8(idx):
    return np.concatenate([v.reshape(-1, 16).T for v in idx]).astype(np.uint16)


def unstriped8(offs):
    return np.stack([offs[16 * g:16 * g + 16].T.reshape(-1) for g in range(8)]).astype(np.int64)


def runs(v, idx8):
    k = np.arange(v.shape[0])
    return v[k[:, None], idx8[k % 512 // 64]]


K, K2, H, N, T, S = 1024, 512, 1024, 256, 2048, 1024

def setup_inputs():
    n = np.random.standard_normal
    s = mx_kscale(K)[:, None]
    s2 = mx_kscale(K2)[:, None]
    u = mx_kscale(H)[:, None]
    tab_words, tab_scales = pack_weight(n((K, T)) * s, "e4m3")
    tab2_words, tab2_scales = pack_weight(n((K2, T)) * s2, "e4m3")
    wp_words, wp_scales = pack_weight(n((K, H)) / np.sqrt(K) / s, "e2m1")
    wf_words, wf_scales = pack_weight(n((H, N)) / np.sqrt(H) / u, "e4m3")
    return {
        "tab_words": tab_words, "tab_scales": tab_scales,
        "offs": striped8(np.stack([np.random.permutation(T)[:S] for _ in range(8)])),
        "tab2_words": tab2_words, "tab2_scales": tab2_scales,
        "offs2": striped(np.random.permutation(T)[:S]),
        "wp_words": wp_words, "wp_scales": wp_scales,
        "wr": (n((K2, H)) / np.sqrt(K2) / s2).astype(np.float32),
        "gain": (np.exp(0.3 * n(H)) * u[:, 0]).astype(np.float32),
        "wf_words": wf_words, "wf_scales": wf_scales,
    }

def reference(tab_words, tab_scales, offs, tab2_words, tab2_scales, offs2,
              wp_words, wp_scales, wr, gain, wf_words, wf_scales):
    v = runs(unpack_weight(tab_words, tab_scales, "e4m3"), unstriped8(offs))
    v2 = unpack_weight(tab2_words, tab2_scales, "e4m3")[:, unstriped(offs2)]
    wp = unpack_weight(wp_words, wp_scales, "e2m1")
    a = wp.T @ v
    b = mxq(f64(wr), 0, "e4m3").T @ v2
    f = np.sqrt(np.square(a) + 0.1)
    h = np.square(f - b) * f64(gain)[:, None]
    wf = unpack_weight(wf_words, wf_scales, "e4m3")
    y = wf.T @ mxq(h, 0, "e4m3")
    return y

@@ -1,0 +1,287 @@
+from contextlib import ExitStack
+
+import concourse.mybir as mybir
+
+K, K2, H, N, T, S = 1024, 512, 1024, 256, 2048, 1024
+FLOPS = 2 * S * (K * H + K2 * H + H * N)
+
+F32 = mybir.dt.float32
+BF16 = mybir.dt.bfloat16
+I32 = mybir.dt.int32
+U32 = mybir.dt.uint32
+U16 = mybir.dt.uint16
+U8 = mybir.dt.uint8
+FP8X4 = mybir.dt.float8_e4m3fn_x4
+FP4X4 = mybir.dt.float4_e2m1fn_x4
+ALU = mybir.AluOpType
+ACT = mybir.ActivationFunctionType
+
+P = 128
+JW = 512
+RB = 512
+
+
+def tile_list_phase_match_families_kernel(
+    tc, tab_words, tab_scales, offs, tab2_words, tab2_scales, offs2,
+    wp_words, wp_scales, wr, gain, wf_words, wf_scales, out,
+):
+    nc = tc.nc
+    with ExitStack() as ctx:
+        keep = ctx.enter_context(tc.tile_pool(name="keep", bufs=1))
+        work = ctx.enter_context(tc.tile_pool(name="work", bufs=3))
+        stage = ctx.enter_context(tc.tile_pool(name="stage", bufs=4))
+        psa = ctx.enter_context(tc.psum_pool(name="psa", bufs=2))
+        psb = ctx.enter_context(tc.psum_pool(name="psb", bufs=2))
+        pso = ctx.enter_context(tc.psum_pool(name="pso", bufs=4))
+
+        lists = keep.tile([P, S // 16], U16, name="lists")
+        lists2 = keep.tile([P, S // 16], U16, name="lists2")
+        ts_raw = keep.tile([P, T], U8, name="ts_raw", align_bytes=64)
+        ts_got = keep.tile([P, S], U8, name="ts_got", align_bytes=64)
+        ts_plane = keep.tile([P, 2 * S], U8, name="ts_plane", align_bytes=64)
+        t2s_raw = keep.tile([P, T], U8, name="t2s_raw", align_bytes=64)
+        wps_raw = keep.tile([P, 2 * H], U8, name="wps_raw", align_bytes=64)
+        wfs = keep.tile([P, 2 * N], U8, name="wfs", align_bytes=64)
+
+        nc.vector.memset(ts_raw[:].bitcast(I32), 0)
+        nc.vector.memset(wps_raw[:].bitcast(I32), 0)
+        nc.vector.memset(ts_plane[:].bitcast(I32), 0)
+        nc.vector.memset(t2s_raw[:].bitcast(I32), 0)
+        nc.vector.memset(wfs[:].bitcast(I32), 0)
+
+        nc.sync.dma_start(lists[:], offs)
+        nc.sync.dma_start(ts_raw[0:P:4, :].bitcast(I32), tab_scales.rearrange("a q t -> q a t").bitcast(I32))
+        for d in range(4):
+            nc.sync.dma_start(
+                wps_raw[32 * d : 32 * d + 4, :].bitcast(I32).rearrange("p (a c) -> p a c", a=2),
+                wp_scales[:, 4 * d : 4 * d + 4, :].rearrange("a q c -> q a c").bitcast(I32),
+            )
+        wp_raw = [keep.tile([P, 2 * 2 * RB], U8, name="wp_raw%d" % b, align_bytes=64) for b in range(2)]
+        tw = [keep.tile([P, T], I32, name="tw%d" % a, align_bytes=64) for a in range(2)]
+        t2w = keep.tile([P, T], I32, name="t2w", align_bytes=64)
+        g_raw = keep.tile([P, 2, 4], F32, name="g_raw")
+        wr_raw = [keep.tile([P, 4, RB], F32, name="wr_raw%d" % b, align_bytes=64) for b in range(2)]
+        wfw = keep.tile([P, 2, N], I32, name="wfw", align_bytes=64)
+
+        def load_wp(b):
+            nc.sync.dma_start(
+                wp_raw[b][:].bitcast(I32).rearrange("p (a c) -> p a c", a=2),
+                wp_words[:, :, 2 * RB * b : 2 * RB * (b + 1)].rearrange("a p c -> p a c").bitcast(I32),
+            )
+
+        def load_wr(b):
+            nc.sync.dma_start(wr_raw[b][:], wr[:, RB * b : RB * (b + 1)].rearrange("(p j) c -> p j c", j=4))
+
+        nc.sync.dma_start(g_raw[:], gain.rearrange("(b p t) -> p b t", b=2, t=4))
+        load_wp(0)
+        for a in range(2):
+            nc.sync.dma_start(tw[a][:], tab_words[a].rearrange("p t i -> p (t i)").bitcast(I32))
+        nc.sync.dma_start(lists2[:], offs2)
+        for d in range(4):
+            nc.sync.dma_start(
+                t2s_raw[32 * d : 32 * d + 4, :].bitcast(I32), tab2_scales[0, 4 * d : 4 * d + 4, :].bitcast(I32)
+            )
+        load_wp(1)
+        nc.sync.dma_start(t2w[:], tab2_words[0].rearrange("p t i -> p (t i)").bitcast(I32))
+        load_wr(0)
+        load_wr(1)
+        for d in range(4):
+            nc.sync.dma_start(
+                wfs[32 * d : 32 * d + 4, :].bitcast(I32).rearrange("p (a c) -> p a c", a=2),
+                wf_scales[:, 4 * d : 4 * d + 4, :].rearrange("a q c -> q a c").bitcast(I32),
+            )
+        nc.sync.dma_start(wfw[:], wf_words.rearrange("a p c i -> p a (c i)").bitcast(I32))
+
+        g = g_raw[:].rearrange("p b t -> p (b t)")
+        half = keep.tile([P, 8], F32, name="half")
+        sgh = keep.tile([P, 8], F32, name="sgh")
+        sg = keep.tile([P, 8], F32, name="sg")
+        gabs = keep.tile([P, 8], F32, name="gabs")
+        groot = keep.tile([P, 8], F32, name="groot")
+        gsq = keep.tile([P, 8], F32, name="gsq")
+        gbias = keep.tile([P, 8], F32, name="gbias")
+        gneg = keep.tile([P, 8], F32, name="gneg")
+        signs = keep.tile([P, 2, 128, 4], BF16, name="signs", align_bytes=64)
+        nc.gpsimd.memset(half[:], 0.5)
+        nc.gpsimd.tensor_scalar(sgh[:], g, 0.0, 0.5, ALU.is_ge, ALU.subtract)
+        nc.gpsimd.tensor_scalar(sg[:], sgh[:], 2.0, 0.0, ALU.mult, ALU.add)
+        nc.gpsimd.tensor_tensor(gabs[:], g, sg[:], ALU.mult)
+        nc.gpsimd.tensor_tensor(groot[:], gabs[:], half[:], ALU.pow)
+        nc.gpsimd.tensor_tensor(gsq[:], groot[:], groot[:], ALU.mult)
+        nc.gpsimd.tensor_scalar(gbias[:], gsq[:], 0.1, 0.0, ALU.mult, ALU.add)
+        nc.gpsimd.tensor_scalar(gneg[:], groot[:], -1.0, 0.0, ALU.mult, ALU.add)
+        for b in range(2):
+            nc.gpsimd.tensor_scalar(
+                signs[:, b, :, :], sg[:, 4 * b : 4 * b + 4].unsqueeze(1).to_broadcast([P, 128, 4]),
+                1.0, 0.0, ALU.mult, ALU.add,
+            )
+
+        warm = keep.tile([P, 1], F32, name="warm")
+        nc.scalar.activation(warm[:], half[:, 0:1], ACT.Sqrt)
+
+        nc.vector.tensor_copy(ts_got[:], ts_raw[:].indirect(lists[:]))
+        for d in range(4):
+            nc.scalar.dma_start(
+                ts_plane[32 * d : 32 * d + 4, :].bitcast(I32),
+                ts_got[32 * d : 32 * d + 32 : 4, :].bitcast(I32),
+            )
+
+        wp_c = [keep.tile([P, 2 * 2 * RB], U8, name="wp_c%d" % b, align_bytes=64) for b in range(2)]
+        wp_s = [keep.tile([P, 2 * RB], U8, name="wp_s%d" % b, align_bytes=64) for b in range(2)]
+
+        def order_wp(b):
+            nc.vector.tensor_copy(
+                wp_s[b][:].rearrange("p (a t m) -> p a m t", a=2, t=4),
+                wps_raw[:].rearrange("p (a b m t) -> p a b m t", a=2, b=2, t=4)[:, :, b, :, :],
+            )
+            nc.vector.tensor_copy(
+                wp_c[b][:].bitcast(U16).rearrange("p (a t m) -> p a m t", a=2, t=4),
+                wp_raw[b][:].bitcast(U16).rearrange("p (a m t) -> p a m t", a=2, t=4),
+            )
+
+        v_c = [[keep.tile([P, JW], U32, name="v_c%d_%d" % (a, h), align_bytes=64) for h in range(2)] for a in range(2)]
+        v2_c = [keep.tile([P, JW], U32, name="v2_c%d" % h, align_bytes=64) for h in range(2)]
+        v2_s = [keep.tile([P, JW], U8, name="v2_s%d" % h, align_bytes=64) for h in range(2)]
+
+        def cols(h):
+            return slice(h * JW // 16, (h + 1) * JW // 16)
+
+        def gather_v(h):
+            for a in range(2):
+                nc.vector.tensor_copy(v_c[a][h][:], tw[a][:].bitcast(U32).indirect(lists[:, cols(h)]))
+
+        def gather_v2(h):
+            nc.vector.tensor_copy(v2_s[h][:], t2s_raw[:].indirect(lists2[:, cols(h)]))
+            nc.vector.tensor_copy(v2_c[h][:], t2w[:].bitcast(U32).indirect(lists2[:, cols(h)]))
+
+        wr_g = [keep.tile([P, 4 * RB], BF16, name="wr_g%d" % b, align_bytes=64) for b in range(2)]
+        wr_c = [keep.tile([P, RB], U32, name="wr_c%d" % b, align_bytes=64) for b in range(2)]
+        wr_s = [keep.tile([P, RB], U8, name="wr_s%d" % b, align_bytes=64) for b in range(2)]
+
+        def cast_wr(b):
+            nc.vector.tensor_copy(
+                wr_g[b][:].rearrange("p (t m j) -> p m j t", t=4, j=4),
+                wr_raw[b][:].rearrange("p j (m t) -> p m j t", t=4),
+            )
+
+        def quant_wr(b):
+            nc.vector.quantize_mx(out=wr_c[b][:].bitcast(FP8X4), scales=wr_s[b][:], in_=wr_g[b][:])
+
+        f_tiles = {}
+
+        def modulus(h, b):
+            sq = work.tile([P, 4, JW], F32, name="sq")
+            f = work.tile([P, 4, JW], F32, name="f")
+            f_tiles[h, b] = f
+            for t in range(4):
+                acc = psa.tile([P, JW], F32, name="acc_a")
+                for a in range(2):
+                    c0 = a * RB + t * 128
+                    nc.tensor.matmul_mx(
+                        out=acc[:],
+                        lhsT=wp_c[b][:, 2 * c0 : 2 * c0 + 256].bitcast(FP4X4),
+                        lhsT_scale=wp_s[b][:, c0 : c0 + 128],
+                        rhs=v_c[a][h][:].bitcast(FP8X4),
+                        rhs_scale=ts_plane[:, a * S + h * JW : a * S + (h + 1) * JW],
+                        start=(a == 0),
+                        stop=(a == 1),
+                    )
+                nc.scalar.activation(sq[:, t, :], acc[:], ACT.Square)
+                i = 4 * b + t
+                nc.scalar.activation(
+                    f[:, t, :], sq[:, t, :], ACT.Sqrt, bias=gbias[:, i : i + 1], scale=gsq[:, i : i + 1]
+                )
+
+        acc_o = {}
+
+        d_tiles = {}
+
+        def residual(h, b):
+            f = f_tiles[h, b]
+            dd = work.tile([P, 4, JW], F32, name="dd")
+            for t in range(4):
+                acc = psb.tile([P, JW], F32, name="acc_b")
+                nc.tensor.matmul_mx(
+                    out=acc[:],
+                    lhsT=wr_c[b][:, t * 128 : (t + 1) * 128].bitcast(FP8X4),
+                    lhsT_scale=wr_s[b][:, t * 128 : (t + 1) * 128],
+                    rhs=v2_c[h][:].bitcast(FP8X4),
+                    rhs_scale=v2_s[h][:],
+                    start=True,
+                    stop=True,
+                )
+                i = 4 * b + t
+                nc.vector.scalar_tensor_tensor(
+                    dd[:, t, :], acc[:], gneg[:, i : i + 1], f[:, t, :], ALU.mult, ALU.add
+                )
+            d_tiles[h, b] = dd
+
+        def field(h, b, parts):
+            dd = d_tiles[h, b]
+            w = JW // parts
+            ow = JW if h == 0 else JW // 2
+            for part in range(parts):
+                j0 = part * w
+                habs = work.tile([P, w, 4], BF16, name="habs", align_bytes=64)
+                nc.scalar.activation(
+                    habs[:].rearrange("p (c i) t -> p c t i", i=4),
+                    dd[:, :, j0 : j0 + w].rearrange("p t (c i) -> p c t i", i=4),
+                    ACT.Square,
+                )
+                hs = work.tile([P, w // 128, 512], BF16, name="hs", align_bytes=64)
+                nc.vector.tensor_tensor(
+                    hs[:],
+                    habs[:].rearrange("p (q j) t -> p q (j t)", j=128),
+                    signs[:, b, :, :].rearrange("p j t -> p (j t)").unsqueeze(1).to_broadcast([P, w // 128, 512]),
+                    ALU.mult,
+                )
+                h_c = work.tile([P, w], U32, name="h_c", align_bytes=64)
+                h_s = work.tile([P, w], U8, name="h_s", align_bytes=64)
+                nc.vector.quantize_mx(
+                    out=h_c[:].bitcast(FP8X4), scales=h_s[:], in_=hs[:].rearrange("p q x -> p (q x)")
+                )
+                for o0 in range(0, w, ow):
+                    for n in range(2):
+                        key = (h, n, j0 + o0)
+                        if b == 0:
+                            acc_o[key] = pso.tile([P, ow], F32, name="acc_o")
+                        nc.tensor.matmul_mx(
+                            out=acc_o[key][:],
+                            lhsT=wfw[:, b, n * 128 : (n + 1) * 128].bitcast(FP8X4),
+                            lhsT_scale=wfs[:, b * N + n * 128 : b * N + (n + 1) * 128],
+                            rhs=h_c[:, o0 : o0 + ow].bitcast(FP8X4),
+                            rhs_scale=h_s[:, o0 : o0 + ow],
+                            start=(b == 0),
+                            stop=(b == 1),
+                        )
+                        if b == 1:
+                            res = stage.tile([P, ow], F32, name="res")
+                            c0 = h * JW + j0 + o0
+                            if n == 0 or h == 0:
+                                nc.scalar.copy(res[:], acc_o[key][:])
+                            else:
+                                nc.vector.tensor_copy(res[:], acc_o[key][:])
+                            nc.sync.dma_start(out[n * 128 : (n + 1) * 128, c0 : c0 + ow], res[:])
+
+        order_wp(0)
+        gather_v(0)
+        modulus(0, 0)
+        order_wp(1)
+        gather_v2(0)
+        modulus(0, 1)
+        cast_wr(0)
+        quant_wr(0)
+        gather_v(1)
+        residual(0, 0)
+        cast_wr(1)
+        quant_wr(1)
+        modulus(1, 0)
+        field(0, 0, 1)
+        residual(0, 1)
+        gather_v2(1)
+        modulus(1, 1)
+        field(0, 1, 1)
+        residual(1, 0)
+        residual(1, 1)
+        field(1, 0, 1)
+        field(1, 1, 2)

@@ -18,6 +18,7 @@ ACT = mybir.ActivationFunctionType
 
 P = 128
 JW = 512
+RING = 6
 RB = 512
 
 
@@ -28,260 +29,268 @@ def tile_list_phase_match_families_kernel(
     nc = tc.nc
     with ExitStack() as ctx:
         keep = ctx.enter_context(tc.tile_pool(name="keep", bufs=1))
+        reuse = ctx.enter_context(tc.tile_pool(name="reuse", bufs=1))
         work = ctx.enter_context(tc.tile_pool(name="work", bufs=3))
+        sqp = ctx.enter_context(tc.tile_pool(name="sqp", bufs=3))
         stage = ctx.enter_context(tc.tile_pool(name="stage", bufs=4))
-        psa = ctx.enter_context(tc.psum_pool(name="psa", bufs=2))
-        psb = ctx.enter_context(tc.psum_pool(name="psb", bufs=2))
-        pso = ctx.enter_context(tc.psum_pool(name="pso", bufs=4))
+        psr = ctx.enter_context(tc.psum_pool(name="psr", bufs=1))
+        pso = ctx.enter_context(tc.psum_pool(name="pso", bufs=2))
+
+        def held(shape, dtype, name, tag=None):
+            return keep.tile(shape, dtype, name=name, tag=tag or name, align_bytes=64)
+
+        def placed(shape, dtype, name, offset):
+            return reuse.tile(shape, dtype, name=name, offset=offset, align_bytes=64)
 
         lists = keep.tile([P, S // 16], U16, name="lists")
         lists2 = keep.tile([P, S // 16], U16, name="lists2")
-        ts_raw = keep.tile([P, T], U8, name="ts_raw", align_bytes=64)
-        ts_got = keep.tile([P, S], U8, name="ts_got", align_bytes=64)
-        ts_plane = keep.tile([P, 2 * S], U8, name="ts_plane", align_bytes=64)
-        t2s_raw = keep.tile([P, T], U8, name="t2s_raw", align_bytes=64)
-        wps_raw = keep.tile([P, 2 * H], U8, name="wps_raw", align_bytes=64)
-        wfs = keep.tile([P, 2 * N], U8, name="wfs", align_bytes=64)
+        g_raw = keep.tile([P, 2, 4], F32, name="g_raw")
+        ts_raw = held([P, T], U8, "ts_raw", "slot_e")
+        wps_raw = held([P, H], U8, "wps_raw", "slot_a")
+        tw = [held([P, T], I32, "tw%d" % a) for a in range(2)]
 
         nc.vector.memset(ts_raw[:].bitcast(I32), 0)
         nc.vector.memset(wps_raw[:].bitcast(I32), 0)
-        nc.vector.memset(ts_plane[:].bitcast(I32), 0)
-        nc.vector.memset(t2s_raw[:].bitcast(I32), 0)
-        nc.vector.memset(wfs[:].bitcast(I32), 0)
 
-        nc.sync.dma_start(lists[:], offs)
-        nc.sync.dma_start(ts_raw[0:P:4, :].bitcast(I32), tab_scales.rearrange("a q t -> q a t").bitcast(I32))
-        for d in range(4):
+        def load_wp(b, raw):
             nc.sync.dma_start(
-                wps_raw[32 * d : 32 * d + 4, :].bitcast(I32).rearrange("p (a c) -> p a c", a=2),
-                wp_scales[:, 4 * d : 4 * d + 4, :].rearrange("a q c -> q a c").bitcast(I32),
-            )
-        wp_raw = [keep.tile([P, 2 * 2 * RB], U8, name="wp_raw%d" % b, align_bytes=64) for b in range(2)]
-        tw = [keep.tile([P, T], I32, name="tw%d" % a, align_bytes=64) for a in range(2)]
-        t2w = keep.tile([P, T], I32, name="t2w", align_bytes=64)
-        g_raw = keep.tile([P, 2, 4], F32, name="g_raw")
-        wr_raw = [keep.tile([P, 4, RB], F32, name="wr_raw%d" % b, align_bytes=64) for b in range(2)]
-        wfw = keep.tile([P, 2, N], I32, name="wfw", align_bytes=64)
-
-        def load_wp(b):
-            nc.sync.dma_start(
-                wp_raw[b][:].bitcast(I32).rearrange("p (a c) -> p a c", a=2),
+                raw.rearrange("p (a c) -> p a c", a=2),
                 wp_words[:, :, 2 * RB * b : 2 * RB * (b + 1)].rearrange("a p c -> p a c").bitcast(I32),
             )
 
-        def load_wr(b):
-            nc.sync.dma_start(wr_raw[b][:], wr[:, RB * b : RB * (b + 1)].rearrange("(p j) c -> p j c", j=4))
+        def load_wr(b, raw):
+            nc.sync.dma_start(raw, wr[:, RB * b : RB * (b + 1)].rearrange("(p j) c -> p j c", j=4))
 
+        nc.sync.dma_start(lists[:], offs)
         nc.sync.dma_start(g_raw[:], gain.rearrange("(b p t) -> p b t", b=2, t=4))
-        load_wp(0)
+        nc.sync.dma_start(lists2[:], offs2)
+        nc.sync.dma_start(ts_raw[0:P:4, :].bitcast(I32), tab_scales.rearrange("a q t -> q a t").bitcast(I32))
+        nc.sync.dma_start(wps_raw[0:P:4, :].bitcast(I32), wp_scales.rearrange("a q c -> q a c").bitcast(I32))
+        wp_raw0 = held([P, RB], I32, "wp_raw0", "slot_d")
+        load_wp(0, wp_raw0[:])
         for a in range(2):
             nc.sync.dma_start(tw[a][:], tab_words[a].rearrange("p t i -> p (t i)").bitcast(I32))
-        nc.sync.dma_start(lists2[:], offs2)
-        for d in range(4):
-            nc.sync.dma_start(
-                t2s_raw[32 * d : 32 * d + 4, :].bitcast(I32), tab2_scales[0, 4 * d : 4 * d + 4, :].bitcast(I32)
-            )
-        load_wp(1)
-        nc.sync.dma_start(t2w[:], tab2_words[0].rearrange("p t i -> p (t i)").bitcast(I32))
-        load_wr(0)
-        load_wr(1)
-        for d in range(4):
-            nc.sync.dma_start(
-                wfs[32 * d : 32 * d + 4, :].bitcast(I32).rearrange("p (a c) -> p a c", a=2),
-                wf_scales[:, 4 * d : 4 * d + 4, :].rearrange("a q c -> q a c").bitcast(I32),
-            )
-        nc.sync.dma_start(wfw[:], wf_words.rearrange("a p c i -> p a (c i)").bitcast(I32))
-
-        g = g_raw[:].rearrange("p b t -> p (b t)")
-        half = keep.tile([P, 8], F32, name="half")
-        sgh = keep.tile([P, 8], F32, name="sgh")
-        sg = keep.tile([P, 8], F32, name="sg")
-        gabs = keep.tile([P, 8], F32, name="gabs")
-        groot = keep.tile([P, 8], F32, name="groot")
-        gsq = keep.tile([P, 8], F32, name="gsq")
-        gbias = keep.tile([P, 8], F32, name="gbias")
-        gneg = keep.tile([P, 8], F32, name="gneg")
-        signs = keep.tile([P, 2, 128, 4], BF16, name="signs", align_bytes=64)
-        nc.gpsimd.memset(half[:], 0.5)
-        nc.gpsimd.tensor_scalar(sgh[:], g, 0.0, 0.5, ALU.is_ge, ALU.subtract)
-        nc.gpsimd.tensor_scalar(sg[:], sgh[:], 2.0, 0.0, ALU.mult, ALU.add)
-        nc.gpsimd.tensor_tensor(gabs[:], g, sg[:], ALU.mult)
-        nc.gpsimd.tensor_tensor(groot[:], gabs[:], half[:], ALU.pow)
-        nc.gpsimd.tensor_tensor(gsq[:], groot[:], groot[:], ALU.mult)
-        nc.gpsimd.tensor_scalar(gbias[:], gsq[:], 0.1, 0.0, ALU.mult, ALU.add)
-        nc.gpsimd.tensor_scalar(gneg[:], groot[:], -1.0, 0.0, ALU.mult, ALU.add)
-        for b in range(2):
-            nc.gpsimd.tensor_scalar(
-                signs[:, b, :, :], sg[:, 4 * b : 4 * b + 4].unsqueeze(1).to_broadcast([P, 128, 4]),
-                1.0, 0.0, ALU.mult, ALU.add,
-            )
-
-        warm = keep.tile([P, 1], F32, name="warm")
-        nc.scalar.activation(warm[:], half[:, 0:1], ACT.Sqrt)
-
-        nc.vector.tensor_copy(ts_got[:], ts_raw[:].indirect(lists[:]))
-        for d in range(4):
-            nc.scalar.dma_start(
-                ts_plane[32 * d : 32 * d + 4, :].bitcast(I32),
-                ts_got[32 * d : 32 * d + 32 : 4, :].bitcast(I32),
-            )
-
-        wp_c = [keep.tile([P, 2 * 2 * RB], U8, name="wp_c%d" % b, align_bytes=64) for b in range(2)]
-        wp_s = [keep.tile([P, 2 * RB], U8, name="wp_s%d" % b, align_bytes=64) for b in range(2)]
-
-        def order_wp(b):
-            nc.vector.tensor_copy(
-                wp_s[b][:].rearrange("p (a t m) -> p a m t", a=2, t=4),
-                wps_raw[:].rearrange("p (a b m t) -> p a b m t", a=2, b=2, t=4)[:, :, b, :, :],
-            )
-            nc.vector.tensor_copy(
-                wp_c[b][:].bitcast(U16).rearrange("p (a t m) -> p a m t", a=2, t=4),
-                wp_raw[b][:].bitcast(U16).rearrange("p (a m t) -> p a m t", a=2, t=4),
-            )
-
-        v_c = [[keep.tile([P, JW], U32, name="v_c%d_%d" % (a, h), align_bytes=64) for h in range(2)] for a in range(2)]
-        v2_c = [keep.tile([P, JW], U32, name="v2_c%d" % h, align_bytes=64) for h in range(2)]
-        v2_s = [keep.tile([P, JW], U8, name="v2_s%d" % h, align_bytes=64) for h in range(2)]
 
         def cols(h):
             return slice(h * JW // 16, (h + 1) * JW // 16)
 
-        def gather_v(h):
-            for a in range(2):
-                nc.vector.tensor_copy(v_c[a][h][:], tw[a][:].bitcast(U32).indirect(lists[:, cols(h)]))
+        ts_got = held([P, S], U8, "ts_got", "slot_b")
+        staged = placed([P, S + H], U8, "staged", 7168)
+        plane = held([P, 2, S + H], U8, "plane")
+        nc.vector.tensor_copy(ts_got[:], ts_raw[:].indirect(lists[:]))
+        nc.vector.tensor_copy(
+            staged[:, S:].rearrange("p (b t m) -> p b m t", b=2, t=4),
+            wps_raw[:].rearrange("p (b m t) -> p b m t", b=2, t=4),
+        )
+        nc.vector.tensor_copy(staged[:, :S].bitcast(I32), ts_got[:].bitcast(I32))
+        for d in range(4):
+            nc.sync.dma_start(
+                plane[32 * d : 32 * d + 4, :, :].rearrange("p a c -> p (a c)").bitcast(I32),
+                staged[32 * d : 32 * d + 32 : 4, :].bitcast(I32),
+            )
+
+        g = g_raw[:].rearrange("p b t -> p (b t)")
+        gabs = keep.tile([P, 8], F32, name="gabs")
+        groot = keep.tile([P, 8], F32, name="groot")
+        gbias = keep.tile([P, 8], F32, name="gbias")
+        signs = held([P, 2, 128, 4], BF16, "signs")
+        nc.vector.scalar_tensor_tensor(gabs[:], g, -1.0, g, ALU.mult, ALU.max)
+        nc.scalar.activation(groot[:], gabs[:], ACT.Sqrt)
+        nc.scalar.activation(gbias[:], gabs[:], ACT.Copy, scale=0.1)
+        for b in range(2):
+            nc.scalar.activation(signs[:, b, :, :], g_raw[:, b, :].unsqueeze(1).to_broadcast([P, 128, 4]), ACT.Sign)
+
+        wp_c = [held([P, 2 * 2 * RB], U8, "wp_c%d" % b) for b in range(2)]
+
+        def order_wp(b, raw):
+            nc.vector.tensor_copy(
+                wp_c[b][:].bitcast(U16).rearrange("p (a t m) -> p a m t", a=2, t=4),
+                raw.bitcast(U16).rearrange("p (a m t) -> p a m t", a=2, t=4),
+            )
+
+        v_c = {}
+        v2_c = [held([P, JW], U32, "v2_c%d" % h) for h in range(2)]
+        v2_s = [held([P, JW], U8, "v2_s%d" % h) for h in range(2)]
+
+        def gather_v(h, a):
+            if (h, a) == (1, 0):
+                v_c[a, h] = placed([P, JW], U32, "v_c_late", 8192)
+            else:
+                v_c[a, h] = held([P, JW], U32, "v_c%d_%d" % (a, h))
+            nc.vector.tensor_copy(v_c[a, h][:], tw[a][:].bitcast(U32).indirect(lists[:, cols(h)]))
+
+        order_wp(0, wp_raw0[:])
+        gather_v(0, 0)
+        gather_v(0, 1)
+
+        wp_raw1 = held([P, RB], I32, "wp_raw1", "slot_b")
+        load_wp(1, wp_raw1[:])
+        t2w = held([P, T], I32, "t2w", "slot_d")
+        nc.sync.dma_start(t2w[:], tab2_words[0].rearrange("p t i -> p (t i)").bitcast(I32))
+        t2s_raw = held([P, T], U8, "t2s_raw", "slot_a")
+        nc.gpsimd.memset(t2s_raw[:].bitcast(I32), 0)
+        for d in range(4):
+            nc.sync.dma_start(
+                t2s_raw[32 * d : 32 * d + 4, :].bitcast(I32), tab2_scales[0, 4 * d : 4 * d + 4, :].bitcast(I32)
+            )
+        wr_raw0 = placed([P, 4, RB], F32, "wr_raw0", 0)
+        load_wr(0, wr_raw0[:])
 
         def gather_v2(h):
             nc.vector.tensor_copy(v2_s[h][:], t2s_raw[:].indirect(lists2[:, cols(h)]))
             nc.vector.tensor_copy(v2_c[h][:], t2w[:].bitcast(U32).indirect(lists2[:, cols(h)]))
 
-        wr_g = [keep.tile([P, 4 * RB], BF16, name="wr_g%d" % b, align_bytes=64) for b in range(2)]
-        wr_c = [keep.tile([P, RB], U32, name="wr_c%d" % b, align_bytes=64) for b in range(2)]
-        wr_s = [keep.tile([P, RB], U8, name="wr_s%d" % b, align_bytes=64) for b in range(2)]
+        wr_g = [held([P, 4 * RB], BF16, "wr_g%d" % b) for b in range(2)]
+        wr_c = [held([P, RB], U32, "wr_c%d" % b) for b in range(2)]
+        wr_s = [held([P, RB], U8, "wr_s%d" % b) for b in range(2)]
 
-        def cast_wr(b):
+        def cast_wr(b, raw):
             nc.vector.tensor_copy(
                 wr_g[b][:].rearrange("p (t m j) -> p m j t", t=4, j=4),
-                wr_raw[b][:].rearrange("p j (m t) -> p m j t", t=4),
+                raw.rearrange("p j (m t) -> p m j t", t=4),
             )
 
         def quant_wr(b):
             nc.vector.quantize_mx(out=wr_c[b][:].bitcast(FP8X4), scales=wr_s[b][:], in_=wr_g[b][:])
 
         f_tiles = {}
-
-        def modulus(h, b):
-            sq = work.tile([P, 4, JW], F32, name="sq")
-            f = work.tile([P, 4, JW], F32, name="f")
-            f_tiles[h, b] = f
-            for t in range(4):
-                acc = psa.tile([P, JW], F32, name="acc_a")
-                for a in range(2):
-                    c0 = a * RB + t * 128
-                    nc.tensor.matmul_mx(
-                        out=acc[:],
-                        lhsT=wp_c[b][:, 2 * c0 : 2 * c0 + 256].bitcast(FP4X4),
-                        lhsT_scale=wp_s[b][:, c0 : c0 + 128],
-                        rhs=v_c[a][h][:].bitcast(FP8X4),
-                        rhs_scale=ts_plane[:, a * S + h * JW : a * S + (h + 1) * JW],
-                        start=(a == 0),
-                        stop=(a == 1),
-                    )
-                nc.scalar.activation(sq[:, t, :], acc[:], ACT.Square)
-                i = 4 * b + t
-                nc.scalar.activation(
-                    f[:, t, :], sq[:, t, :], ACT.Sqrt, bias=gbias[:, i : i + 1], scale=gsq[:, i : i + 1]
-                )
-
-        acc_o = {}
-
         d_tiles = {}
+        h_tiles = {}
+        banks = []
+        pending = []
 
-        def residual(h, b):
-            f = f_tiles[h, b]
-            dd = work.tile([P, 4, JW], F32, name="dd")
-            for t in range(4):
-                acc = psb.tile([P, JW], F32, name="acc_b")
+        def next_bank():
+            bank = psr.tile([P, JW], F32, name="bank", tag="bank%d" % (len(banks) % RING))
+            banks.append(bank)
+            return bank
+
+        def root():
+            h, b, t, sq = pending.pop()
+            i = 4 * b + t
+            nc.scalar.activation(
+                f_tiles[h, b][:, t, :], sq[:], ACT.Sqrt, bias=gbias[:, i : i + 1], scale=gabs[:, i : i + 1]
+            )
+
+        def modulus(h, b, t):
+            if t == 0:
+                f_tiles[h, b] = held([P, 4, JW], F32, "f%d_%d" % (h, b))
+            acc = next_bank()
+            for a in range(2):
+                c0 = a * RB + t * 128
+                s0 = S + b * RB + t * 128
                 nc.tensor.matmul_mx(
                     out=acc[:],
-                    lhsT=wr_c[b][:, t * 128 : (t + 1) * 128].bitcast(FP8X4),
-                    lhsT_scale=wr_s[b][:, t * 128 : (t + 1) * 128],
-                    rhs=v2_c[h][:].bitcast(FP8X4),
-                    rhs_scale=v2_s[h][:],
-                    start=True,
-                    stop=True,
+                    lhsT=wp_c[b][:, 2 * c0 : 2 * c0 + 256].bitcast(FP4X4),
+                    lhsT_scale=plane[:, a, s0 : s0 + 128],
+                    rhs=v_c[a, h][:].bitcast(FP8X4),
+                    rhs_scale=plane[:, a, h * JW : (h + 1) * JW],
+                    start=(a == 0),
+                    stop=(a == 1),
                 )
-                i = 4 * b + t
-                nc.vector.scalar_tensor_tensor(
-                    dd[:, t, :], acc[:], gneg[:, i : i + 1], f[:, t, :], ALU.mult, ALU.add
-                )
-            d_tiles[h, b] = dd
+            sq = sqp.tile([P, JW], F32, name="sq")
+            nc.scalar.activation(sq[:], acc[:], ACT.Square)
+            if pending:
+                root()
+            pending.append((h, b, t, sq))
 
-        def field(h, b, parts):
+        def residual(h, b, t):
+            if t == 0:
+                d_tiles[h, b] = held([P, 4, JW], F32, "dd%d_%d" % (h, b))
+            acc = next_bank()
+            nc.tensor.matmul_mx(
+                out=acc[:],
+                lhsT=wr_c[b][:, t * 128 : (t + 1) * 128].bitcast(FP8X4),
+                lhsT_scale=wr_s[b][:, t * 128 : (t + 1) * 128],
+                rhs=v2_c[h][:].bitcast(FP8X4),
+                rhs_scale=v2_s[h][:],
+                start=True,
+                stop=True,
+            )
+            i = 4 * b + t
+            nc.vector.scalar_tensor_tensor(
+                d_tiles[h, b][:, t, :], acc[:], groot[:, i : i + 1], f_tiles[h, b][:, t, :], ALU.mult, ALU.subtract
+            )
+
+        def field(h, b, j0, w):
             dd = d_tiles[h, b]
-            w = JW // parts
-            ow = JW if h == 0 else JW // 2
-            for part in range(parts):
-                j0 = part * w
-                habs = work.tile([P, w, 4], BF16, name="habs", align_bytes=64)
-                nc.scalar.activation(
-                    habs[:].rearrange("p (c i) t -> p c t i", i=4),
-                    dd[:, :, j0 : j0 + w].rearrange("p t (c i) -> p c t i", i=4),
-                    ACT.Square,
-                )
-                hs = work.tile([P, w // 128, 512], BF16, name="hs", align_bytes=64)
-                nc.vector.tensor_tensor(
-                    hs[:],
-                    habs[:].rearrange("p (q j) t -> p q (j t)", j=128),
-                    signs[:, b, :, :].rearrange("p j t -> p (j t)").unsqueeze(1).to_broadcast([P, w // 128, 512]),
-                    ALU.mult,
-                )
-                h_c = work.tile([P, w], U32, name="h_c", align_bytes=64)
-                h_s = work.tile([P, w], U8, name="h_s", align_bytes=64)
-                nc.vector.quantize_mx(
-                    out=h_c[:].bitcast(FP8X4), scales=h_s[:], in_=hs[:].rearrange("p q x -> p (q x)")
-                )
-                for o0 in range(0, w, ow):
-                    for n in range(2):
-                        key = (h, n, j0 + o0)
-                        if b == 0:
-                            acc_o[key] = pso.tile([P, ow], F32, name="acc_o")
-                        nc.tensor.matmul_mx(
-                            out=acc_o[key][:],
-                            lhsT=wfw[:, b, n * 128 : (n + 1) * 128].bitcast(FP8X4),
-                            lhsT_scale=wfs[:, b * N + n * 128 : b * N + (n + 1) * 128],
-                            rhs=h_c[:, o0 : o0 + ow].bitcast(FP8X4),
-                            rhs_scale=h_s[:, o0 : o0 + ow],
-                            start=(b == 0),
-                            stop=(b == 1),
-                        )
-                        if b == 1:
-                            res = stage.tile([P, ow], F32, name="res")
-                            c0 = h * JW + j0 + o0
-                            if n == 0 or h == 0:
-                                nc.scalar.copy(res[:], acc_o[key][:])
-                            else:
-                                nc.vector.tensor_copy(res[:], acc_o[key][:])
-                            nc.sync.dma_start(out[n * 128 : (n + 1) * 128, c0 : c0 + ow], res[:])
+            habs = work.tile([P, w, 4], BF16, name="habs", align_bytes=64)
+            woven = habs[:].rearrange("p (c i) t -> p c t i", i=4)
+            rows = dd[:, :, j0 : j0 + w].rearrange("p t (c i) -> p c t i", i=4)
+            if (h, b) == (0, 0):
+                nc.gpsimd.tensor_tensor(woven, rows, rows, ALU.mult)
+            else:
+                nc.scalar.activation(woven, rows, ACT.Square)
+            hs = work.tile([P, w // 128, 512], BF16, name="hs", align_bytes=64)
+            nc.vector.tensor_tensor(
+                hs[:],
+                habs[:].rearrange("p (q j) t -> p q (j t)", j=128),
+                signs[:, b, :, :].rearrange("p j t -> p (j t)").unsqueeze(1).to_broadcast([P, w // 128, 512]),
+                ALU.mult,
+            )
+            h_c = held([P, w], U32, "h_c%d_%d_%d" % (h, b, j0))
+            h_s = held([P, w], U8, "h_s%d_%d_%d" % (h, b, j0))
+            nc.vector.quantize_mx(out=h_c[:].bitcast(FP8X4), scales=h_s[:], in_=hs[:].rearrange("p q x -> p (q x)"))
+            h_tiles[h, b] = (h_c, h_s, j0)
 
-        order_wp(0)
-        gather_v(0)
-        modulus(0, 0)
-        order_wp(1)
+        def scores(h, j0, w):
+            acc = pso.tile([P, 2, w], F32, name="acc_o")
+            for n in range(2):
+                for b in range(2):
+                    h_c, h_s, first = h_tiles[h, b]
+                    nc.tensor.matmul_mx(
+                        out=acc[:, n, :],
+                        lhsT=wfw[:, b * N + n * 128 : b * N + (n + 1) * 128].bitcast(FP8X4),
+                        lhsT_scale=wfs[:, b * N + n * 128 : b * N + (n + 1) * 128],
+                        rhs=h_c[:, j0 - first : j0 - first + w].bitcast(FP8X4),
+                        rhs_scale=h_s[:, j0 - first : j0 - first + w],
+                        start=(b == 0),
+                        stop=(b == 1),
+                    )
+            res = stage.tile([P, 2, w], F32, name="res")
+            nc.scalar.copy(res[:], acc[:])
+            c0 = h * JW + j0
+            nc.sync.dma_start(out[:, c0 : c0 + w].rearrange("(n p) c -> p n c", n=2), res[:])
+
+        for t in range(4):
+            modulus(0, 0, t)
+        order_wp(1, wp_raw1[:])
+        wr_raw1 = held([P, 4, RB], F32, "wr_raw1", "slot_b")
+        load_wr(1, wr_raw1[:])
+        for t in range(4):
+            modulus(0, 1, t)
+        gather_v(1, 0)
+        gather_v(1, 1)
         gather_v2(0)
-        modulus(0, 1)
-        cast_wr(0)
+        cast_wr(0, wr_raw0[:])
+        wfw = placed([P, 2 * N], I32, "wfw", 0)
+        wfs = placed([P, 2 * N], U8, "wfs", 2048)
+        nc.sync.dma_start(
+            wfw[:].rearrange("p (a c) -> p a c", a=2), wf_words.rearrange("a p c i -> p a (c i)").bitcast(I32)
+        )
+        for d in range(4):
+            nc.sync.dma_start(
+                wfs[32 * d : 32 * d + 4, :].bitcast(I32).rearrange("p (a c) -> p a c", a=2),
+                wf_scales[:, 4 * d : 4 * d + 4, :].rearrange("a q c -> q a c").bitcast(I32),
+            )
+        for t in range(4):
+            modulus(1, 0, t)
+        cast_wr(1, wr_raw1[:])
         quant_wr(0)
-        gather_v(1)
-        residual(0, 0)
-        cast_wr(1)
-        quant_wr(1)
-        modulus(1, 0)
-        field(0, 0, 1)
-        residual(0, 1)
         gather_v2(1)
-        modulus(1, 1)
-        field(0, 1, 1)
-        residual(1, 0)
-        residual(1, 1)
-        field(1, 0, 1)
-        field(1, 1, 2)
+        quant_wr(1)
+        for t in range(4):
+            modulus(1, 1, t)
+            residual(0, t // 2, 2 * (t % 2))
+            residual(0, t // 2, 2 * (t % 2) + 1)
+        root()
+        for b in range(2):
+            for t in range(4):
+                residual(1, b, t)
+        field(0, 0, 0, JW)
+        field(0, 1, 0, JW)
+        scores(0, 0, 256)
+        scores(0, 256, 256)
+        field(1, 0, 0, JW)
+        for j0, w in ((0, 256), (256, 128), (384, 128)):
+            field(1, 1, j0, w)
+            scores(1, j0, w)

@@ -18,7 +18,6 @@ ACT = mybir.ActivationFunctionType
 
 P = 128
 JW = 512
-RING = 6
 RB = 512
 
 
@@ -30,11 +29,9 @@ def tile_list_phase_match_families_kernel(
     with ExitStack() as ctx:
         keep = ctx.enter_context(tc.tile_pool(name="keep", bufs=1))
         reuse = ctx.enter_context(tc.tile_pool(name="reuse", bufs=1))
-        work = ctx.enter_context(tc.tile_pool(name="work", bufs=3))
         sqp = ctx.enter_context(tc.tile_pool(name="sqp", bufs=3))
-        stage = ctx.enter_context(tc.tile_pool(name="stage", bufs=4))
+        stage = ctx.enter_context(tc.tile_pool(name="stage", bufs=5))
         psr = ctx.enter_context(tc.psum_pool(name="psr", bufs=1))
-        pso = ctx.enter_context(tc.psum_pool(name="pso", bufs=2))
 
         def held(shape, dtype, name, tag=None):
             return keep.tile(shape, dtype, name=name, tag=tag or name, align_bytes=64)
@@ -63,19 +60,21 @@ def tile_list_phase_match_families_kernel(
 
         nc.sync.dma_start(lists[:], offs)
         nc.sync.dma_start(g_raw[:], gain.rearrange("(b p t) -> p b t", b=2, t=4))
-        nc.sync.dma_start(lists2[:], offs2)
         nc.sync.dma_start(ts_raw[0:P:4, :].bitcast(I32), tab_scales.rearrange("a q t -> q a t").bitcast(I32))
         nc.sync.dma_start(wps_raw[0:P:4, :].bitcast(I32), wp_scales.rearrange("a q c -> q a c").bitcast(I32))
-        wp_raw0 = held([P, RB], I32, "wp_raw0", "slot_d")
+        wp_raw0 = placed([P, RB], I32, "wp_raw0", 7168)
         load_wp(0, wp_raw0[:])
         for a in range(2):
             nc.sync.dma_start(tw[a][:], tab_words[a].rearrange("p t i -> p (t i)").bitcast(I32))
+        wp_raw1 = held([P, RB], I32, "wp_raw1", "slot_d")
+        load_wp(1, wp_raw1[:])
+        nc.sync.dma_start(lists2[:], offs2)
 
         def cols(h):
             return slice(h * JW // 16, (h + 1) * JW // 16)
 
         ts_got = held([P, S], U8, "ts_got", "slot_b")
-        staged = placed([P, S + H], U8, "staged", 7168)
+        staged = placed([P, S + H], U8, "staged", 23552)
         plane = held([P, 2, S + H], U8, "plane")
         nc.vector.tensor_copy(ts_got[:], ts_raw[:].indirect(lists[:]))
         nc.vector.tensor_copy(
@@ -109,12 +108,12 @@ def tile_list_phase_match_families_kernel(
             )
 
         v_c = {}
-        v2_c = [held([P, JW], U32, "v2_c%d" % h) for h in range(2)]
-        v2_s = [held([P, JW], U8, "v2_s%d" % h) for h in range(2)]
+        v2_c = {}
+        v2_s = {}
 
         def gather_v(h, a):
             if (h, a) == (1, 0):
-                v_c[a, h] = placed([P, JW], U32, "v_c_late", 8192)
+                v_c[a, h] = placed([P, JW], U32, "v_c_late", 24576)
             else:
                 v_c[a, h] = held([P, JW], U32, "v_c%d_%d" % (a, h))
             nc.vector.tensor_copy(v_c[a, h][:], tw[a][:].bitcast(U32).indirect(lists[:, cols(h)]))
@@ -123,34 +122,38 @@ def tile_list_phase_match_families_kernel(
         gather_v(0, 0)
         gather_v(0, 1)
 
-        wp_raw1 = held([P, RB], I32, "wp_raw1", "slot_b")
-        load_wp(1, wp_raw1[:])
-        t2w = held([P, T], I32, "t2w", "slot_d")
+        wr_raw = [placed([P, 4, RB], F32, "wr_raw%d" % b, 8192 * (b + 1))[:] for b in range(2)]
+        t2w = placed([P, T], I32, "t2w", 0)
         nc.sync.dma_start(t2w[:], tab2_words[0].rearrange("p t i -> p (t i)").bitcast(I32))
-        t2s_raw = held([P, T], U8, "t2s_raw", "slot_a")
+        load_wr(0, wr_raw[0])
+        t2s_raw = held([P, T], U8, "t2s_raw", "slot_b")
         nc.gpsimd.memset(t2s_raw[:].bitcast(I32), 0)
         for d in range(4):
             nc.sync.dma_start(
                 t2s_raw[32 * d : 32 * d + 4, :].bitcast(I32), tab2_scales[0, 4 * d : 4 * d + 4, :].bitcast(I32)
             )
-        wr_raw0 = placed([P, 4, RB], F32, "wr_raw0", 0)
-        load_wr(0, wr_raw0[:])
+        load_wr(1, wr_raw[1])
 
         def gather_v2(h):
-            nc.vector.tensor_copy(v2_s[h][:], t2s_raw[:].indirect(lists2[:, cols(h)]))
+            v2_c[h] = held([P, JW], U32, "v2_c%d" % h)
+            v2_s[h] = held([P, JW], U8, "v2_s%d" % h)
             nc.vector.tensor_copy(v2_c[h][:], t2w[:].bitcast(U32).indirect(lists2[:, cols(h)]))
+            nc.vector.tensor_copy(v2_s[h][:], t2s_raw[:].indirect(lists2[:, cols(h)]))
 
-        wr_g = [held([P, 4 * RB], BF16, "wr_g%d" % b) for b in range(2)]
-        wr_c = [held([P, RB], U32, "wr_c%d" % b) for b in range(2)]
+        wr_g = {}
+        wr_c = {}
         wr_s = [held([P, RB], U8, "wr_s%d" % b) for b in range(2)]
 
         def cast_wr(b, raw):
-            nc.vector.tensor_copy(
-                wr_g[b][:].rearrange("p (t m j) -> p m j t", t=4, j=4),
-                raw.rearrange("p j (m t) -> p m j t", t=4),
+            wr_g[b] = held([P, 4 * RB], BF16, "wr_g%d" % b, "slot_g")
+            nc.gpsimd.tensor_scalar(
+                wr_g[b][:].rearrange("p (t m j) -> p t m j", t=4, j=4),
+                raw.rearrange("p j (m t) -> p t m j", t=4),
+                1.0, 0.0, ALU.mult, ALU.add,
             )
 
         def quant_wr(b):
+            wr_c[b] = held([P, RB], U32, "wr_c%d" % b, "f0_0" if b else None)
             nc.vector.quantize_mx(out=wr_c[b][:].bitcast(FP8X4), scales=wr_s[b][:], in_=wr_g[b][:])
 
         f_tiles = {}
@@ -158,9 +161,13 @@ def tile_list_phase_match_families_kernel(
         h_tiles = {}
         banks = []
         pending = []
+        signed = []
+        stores = {}
 
         def next_bank():
-            bank = psr.tile([P, JW], F32, name="bank", tag="bank%d" % (len(banks) % RING))
+            part, t = divmod(len(banks), 4)
+            pair = ((0, 1), (2, 3), (0, 1), (2, 0), (1, 3), (2, 1), (0, 3), (2, 1))[part][t // 2]
+            bank = psr.tile([P, JW], F32, name="bank", tag="bank%d" % (2 * pair + t % 2))
             banks.append(bank)
             return bank
 
@@ -213,14 +220,18 @@ def tile_list_phase_match_families_kernel(
 
         def field(h, b, j0, w):
             dd = d_tiles[h, b]
-            habs = work.tile([P, w, 4], BF16, name="habs", align_bytes=64)
+            first = (h, b) == (0, 0)
+            reused = {(0, 0, 0): "slot_g", (0, 1, 256): "v_c1_1", (1, 0, 0): "wp_c1"}
+            habs = held([P, w, 4], BF16, "habs%d_%d_%d" % (h, b, j0), reused.get((h, b, j0)))
             woven = habs[:].rearrange("p (c i) t -> p c t i", i=4)
             rows = dd[:, :, j0 : j0 + w].rearrange("p t (c i) -> p c t i", i=4)
-            if (h, b) == (0, 0):
-                nc.gpsimd.tensor_tensor(woven, rows, rows, ALU.mult)
+            if first or (h, j0) == (0, 0):
+                plain = dd[:, :, j0 : j0 + w].rearrange("p t j -> p j t")
+                nc.gpsimd.tensor_tensor(habs[:], plain, plain, ALU.mult)
             else:
                 nc.scalar.activation(woven, rows, ACT.Square)
-            hs = work.tile([P, w // 128, 512], BF16, name="hs", align_bytes=64)
+            hs = held([P, w // 128, 512], BF16, "hs", ("f1_1", "slot_g")[len(signed) % 2])
+            signed.append(hs)
             nc.vector.tensor_tensor(
                 hs[:],
                 habs[:].rearrange("p (q j) t -> p q (j t)", j=128),
@@ -232,65 +243,73 @@ def tile_list_phase_match_families_kernel(
             nc.vector.quantize_mx(out=h_c[:].bitcast(FP8X4), scales=h_s[:], in_=hs[:].rearrange("p q x -> p (q x)"))
             h_tiles[h, b] = (h_c, h_s, j0)
 
-        def scores(h, j0, w):
-            acc = pso.tile([P, 2, w], F32, name="acc_o")
+        def scores(h, b, j0, w):
+            if b == 0:
+                bank = psr.tile([P, JW], F32, name="bank", tag="bank%d" % len(stores))
+                stores[h, j0] = bank[:, : 2 * w].rearrange("p (n c) -> p n c", n=2)
+            acc = stores[h, j0]
+            h_c, h_s, first = h_tiles[h, b]
             for n in range(2):
-                for b in range(2):
-                    h_c, h_s, first = h_tiles[h, b]
-                    nc.tensor.matmul_mx(
-                        out=acc[:, n, :],
-                        lhsT=wfw[:, b * N + n * 128 : b * N + (n + 1) * 128].bitcast(FP8X4),
-                        lhsT_scale=wfs[:, b * N + n * 128 : b * N + (n + 1) * 128],
-                        rhs=h_c[:, j0 - first : j0 - first + w].bitcast(FP8X4),
-                        rhs_scale=h_s[:, j0 - first : j0 - first + w],
-                        start=(b == 0),
-                        stop=(b == 1),
-                    )
-            res = stage.tile([P, 2, w], F32, name="res")
-            nc.scalar.copy(res[:], acc[:])
-            c0 = h * JW + j0
-            nc.sync.dma_start(out[:, c0 : c0 + w].rearrange("(n p) c -> p n c", n=2), res[:])
+                nc.tensor.matmul_mx(
+                    out=acc[:, n, :],
+                    lhsT=wfw[:, b * N + n * 128 : b * N + (n + 1) * 128].bitcast(FP8X4),
+                    lhsT_scale=wfs.bitcast(U8)[:, b * N + n * 128 : b * N + (n + 1) * 128],
+                    rhs=h_c[:, j0 - first : j0 - first + w].bitcast(FP8X4),
+                    rhs_scale=h_s[:, j0 - first : j0 - first + w],
+                    start=(b, n) == (0, 0),
+                    stop=(b, n) == (1, 1),
+                )
+            if b == 1:
+                res = stage.tile([P, 2, w], F32, name="res")
+                if j0 + w == JW and h == 1:
+                    nc.vector.tensor_copy(res[:], acc)
+                else:
+                    nc.scalar.copy(res[:], acc)
+                c0 = h * JW + j0
+                nc.sync.dma_start(out[:, c0 : c0 + w].rearrange("(n p) c -> p n c", n=2), res[:])
 
         for t in range(4):
             modulus(0, 0, t)
         order_wp(1, wp_raw1[:])
-        wr_raw1 = held([P, 4, RB], F32, "wr_raw1", "slot_b")
-        load_wr(1, wr_raw1[:])
+        wf_all = held([P, 2 * N + N // 2], I32, "wf_all", "slot_d")
+        wfw = wf_all[:, : 2 * N]
+        wfs = wf_all[:, 2 * N :]
+        nc.sync.dma_start(
+            wfw.rearrange("p (a c) -> p a c", a=2), wf_words.rearrange("a p c i -> p a (c i)").bitcast(I32)
+        )
+        for d in range(4):
+            nc.sync.dma_start(
+                wfs[32 * d : 32 * d + 4, :].rearrange("p (a c) -> p a c", a=2),
+                wf_scales[:, 4 * d : 4 * d + 4, :].rearrange("a q c -> q a c").bitcast(I32),
+            )
         for t in range(4):
             modulus(0, 1, t)
         gather_v(1, 0)
         gather_v(1, 1)
+        cast_wr(0, wr_raw[0])
         gather_v2(0)
-        cast_wr(0, wr_raw0[:])
-        wfw = placed([P, 2 * N], I32, "wfw", 0)
-        wfs = placed([P, 2 * N], U8, "wfs", 2048)
-        nc.sync.dma_start(
-            wfw[:].rearrange("p (a c) -> p a c", a=2), wf_words.rearrange("a p c i -> p a (c i)").bitcast(I32)
-        )
-        for d in range(4):
-            nc.sync.dma_start(
-                wfs[32 * d : 32 * d + 4, :].bitcast(I32).rearrange("p (a c) -> p a c", a=2),
-                wf_scales[:, 4 * d : 4 * d + 4, :].rearrange("a q c -> q a c").bitcast(I32),
-            )
-        for t in range(4):
-            modulus(1, 0, t)
-        cast_wr(1, wr_raw1[:])
-        quant_wr(0)
         gather_v2(1)
+        quant_wr(0)
+        cast_wr(1, wr_raw[1])
+        root()
+        for t in range(4):
+            residual(0, 0, t)
         quant_wr(1)
         for t in range(4):
+            modulus(1, 0, t)
+        for t in range(4):
+            residual(0, 1, t)
+        for t in range(4):
             modulus(1, 1, t)
-            residual(0, t // 2, 2 * (t % 2))
-            residual(0, t // 2, 2 * (t % 2) + 1)
         root()
         for b in range(2):
             for t in range(4):
                 residual(1, b, t)
-        field(0, 0, 0, JW)
-        field(0, 1, 0, JW)
-        scores(0, 0, 256)
-        scores(0, 256, 256)
-        field(1, 0, 0, JW)
-        for j0, w in ((0, 256), (256, 128), (384, 128)):
-            field(1, 1, j0, w)
-            scores(1, j0, w)
+        pieces = (((0, 256), (256, 256)), ((0, 256), (256, 128), (384, 128)))
+        for h in range(2):
+            field(h, 0, 0, JW)
+            for j0, w in pieces[h]:
+                scores(h, 0, j0, w)
+            for j0, w in pieces[h]:
+                field(h, 1, j0, w)
+                scores(h, 1, j0, w)

@@ -73,20 +73,24 @@ def tile_list_phase_match_families_kernel(
         def cols(h):
             return slice(h * JW // 16, (h + 1) * JW // 16)
 
-        ts_got = held([P, S], U8, "ts_got", "slot_b")
-        staged = placed([P, S + H], U8, "staged", 23552)
-        plane = held([P, 2, S + H], U8, "plane")
-        nc.vector.tensor_copy(ts_got[:], ts_raw[:].indirect(lists[:]))
+        ts_got0 = held([P, JW], U8, "ts_got0", "slot_b")
+        staged = placed([P, JW + H], U8, "staged", 23552)
+        plane0 = held([P, 2, JW + H], U8, "plane0")
+        nc.vector.tensor_copy(ts_got0[:], ts_raw[:].indirect(lists[:, cols(0)]))
         nc.vector.tensor_copy(
-            staged[:, S:].rearrange("p (b t m) -> p b m t", b=2, t=4),
+            staged[:, JW:].rearrange("p (b t m) -> p b m t", b=2, t=4),
             wps_raw[:].rearrange("p (b m t) -> p b m t", b=2, t=4),
         )
-        nc.vector.tensor_copy(staged[:, :S].bitcast(I32), ts_got[:].bitcast(I32))
-        for d in range(4):
-            nc.sync.dma_start(
-                plane[32 * d : 32 * d + 4, :, :].rearrange("p a c -> p (a c)").bitcast(I32),
-                staged[32 * d : 32 * d + 32 : 4, :].bitcast(I32),
-            )
+        nc.vector.tensor_copy(staged[:, :JW].bitcast(I32), ts_got0[:].bitcast(I32))
+
+        def move_rows(plane, rows):
+            for d in range(4):
+                nc.scalar.dma_start(
+                    plane[32 * d : 32 * d + 4, :, :].rearrange("p a c -> p (a c)").bitcast(I32),
+                    rows[32 * d : 32 * d + 32 : 4, :].bitcast(I32),
+                )
+
+        move_rows(plane0, staged)
 
         g = g_raw[:].rearrange("p b t -> p (b t)")
         gabs = keep.tile([P, 8], F32, name="gabs")
@@ -108,8 +112,6 @@ def tile_list_phase_match_families_kernel(
             )
 
         v_c = {}
-        v2_c = {}
-        v2_s = {}
 
         def gather_v(h, a):
             if (h, a) == (1, 0):
@@ -120,6 +122,10 @@ def tile_list_phase_match_families_kernel(
 
         order_wp(0, wp_raw0[:])
         gather_v(0, 0)
+        ts_got1 = held([P, JW], U8, "ts_got1", "slot_a")
+        plane1 = held([P, 2, JW], U8, "plane1")
+        nc.vector.tensor_copy(ts_got1[:], ts_raw[:].indirect(lists[:, cols(1)]))
+        move_rows(plane1, ts_got1)
         gather_v(0, 1)
 
         wr_raw = [placed([P, 4, RB], F32, "wr_raw%d" % b, 8192 * (b + 1))[:] for b in range(2)]
@@ -134,26 +140,26 @@ def tile_list_phase_match_families_kernel(
             )
         load_wr(1, wr_raw[1])
 
-        def gather_v2(h):
-            v2_c[h] = held([P, JW], U32, "v2_c%d" % h)
-            v2_s[h] = held([P, JW], U8, "v2_s%d" % h)
-            nc.vector.tensor_copy(v2_c[h][:], t2w[:].bitcast(U32).indirect(lists2[:, cols(h)]))
-            nc.vector.tensor_copy(v2_s[h][:], t2s_raw[:].indirect(lists2[:, cols(h)]))
+        v2_c = held([P, S], U32, "v2_c")
+        v2_s = held([P, S], U8, "v2_s")
+
+        def gather_v2():
+            nc.vector.tensor_copy(v2_c[:], t2w[:].bitcast(U32).indirect(lists2[:]))
+            nc.vector.tensor_copy(v2_s[:], t2s_raw[:].indirect(lists2[:]))
 
         wr_g = {}
         wr_c = {}
         wr_s = [held([P, RB], U8, "wr_s%d" % b) for b in range(2)]
 
         def cast_wr(b, raw):
-            wr_g[b] = held([P, 4 * RB], BF16, "wr_g%d" % b, "slot_g")
-            nc.gpsimd.tensor_scalar(
-                wr_g[b][:].rearrange("p (t m j) -> p t m j", t=4, j=4),
-                raw.rearrange("p j (m t) -> p t m j", t=4),
-                1.0, 0.0, ALU.mult, ALU.add,
+            wr_g[b] = held([P, 4 * RB], BF16, "wr_g%d" % b, "slot_g" if b else None)
+            nc.vector.tensor_copy(
+                wr_g[b][:].rearrange("p (t m j) -> p m j t", t=4, j=4),
+                raw.rearrange("p j (m t) -> p m j t", t=4),
             )
 
         def quant_wr(b):
-            wr_c[b] = held([P, RB], U32, "wr_c%d" % b, "f0_0" if b else None)
+            wr_c[b] = held([P, RB], U32, "wr_c%d" % b)
             nc.vector.quantize_mx(out=wr_c[b][:].bitcast(FP8X4), scales=wr_s[b][:], in_=wr_g[b][:])
 
         f_tiles = {}
@@ -184,13 +190,13 @@ def tile_list_phase_match_families_kernel(
             acc = next_bank()
             for a in range(2):
                 c0 = a * RB + t * 128
-                s0 = S + b * RB + t * 128
+                s0 = JW + b * RB + t * 128
                 nc.tensor.matmul_mx(
                     out=acc[:],
                     lhsT=wp_c[b][:, 2 * c0 : 2 * c0 + 256].bitcast(FP4X4),
-                    lhsT_scale=plane[:, a, s0 : s0 + 128],
+                    lhsT_scale=plane0[:, a, s0 : s0 + 128],
                     rhs=v_c[a, h][:].bitcast(FP8X4),
-                    rhs_scale=plane[:, a, h * JW : (h + 1) * JW],
+                    rhs_scale=(plane0, plane1)[h][:, a, :JW],
                     start=(a == 0),
                     stop=(a == 1),
                 )
@@ -208,8 +214,8 @@ def tile_list_phase_match_families_kernel(
                 out=acc[:],
                 lhsT=wr_c[b][:, t * 128 : (t + 1) * 128].bitcast(FP8X4),
                 lhsT_scale=wr_s[b][:, t * 128 : (t + 1) * 128],
-                rhs=v2_c[h][:].bitcast(FP8X4),
-                rhs_scale=v2_s[h][:],
+                rhs=v2_c[:, h * JW : (h + 1) * JW].bitcast(FP8X4),
+                rhs_scale=v2_s[:, h * JW : (h + 1) * JW],
                 start=True,
                 stop=True,
             )
@@ -221,13 +227,12 @@ def tile_list_phase_match_families_kernel(
         def field(h, b, j0, w):
             dd = d_tiles[h, b]
             first = (h, b) == (0, 0)
-            reused = {(0, 0, 0): "slot_g", (0, 1, 256): "v_c1_1", (1, 0, 0): "wp_c1"}
+            reused = {(0, 0, 0): "slot_g", (0, 1, 0): "v_c1_1", (1, 0, 0): "wp_c1"}
             habs = held([P, w, 4], BF16, "habs%d_%d_%d" % (h, b, j0), reused.get((h, b, j0)))
             woven = habs[:].rearrange("p (c i) t -> p c t i", i=4)
             rows = dd[:, :, j0 : j0 + w].rearrange("p t (c i) -> p c t i", i=4)
-            if first or (h, j0) == (0, 0):
-                plain = dd[:, :, j0 : j0 + w].rearrange("p t j -> p j t")
-                nc.gpsimd.tensor_tensor(habs[:], plain, plain, ALU.mult)
+            if first:
+                nc.gpsimd.tensor_tensor(woven, rows, rows, ALU.mult)
             else:
                 nc.scalar.activation(woven, rows, ACT.Square)
             hs = held([P, w // 128, 512], BF16, "hs", ("f1_1", "slot_g")[len(signed) % 2])
@@ -286,15 +291,14 @@ def tile_list_phase_match_families_kernel(
             modulus(0, 1, t)
         gather_v(1, 0)
         gather_v(1, 1)
+        gather_v2()
         cast_wr(0, wr_raw[0])
-        gather_v2(0)
-        gather_v2(1)
-        quant_wr(0)
         cast_wr(1, wr_raw[1])
+        quant_wr(0)
+        quant_wr(1)
         root()
         for t in range(4):
             residual(0, 0, t)
-        quant_wr(1)
         for t in range(4):
             modulus(1, 0, t)
         for t in range(4):

@@ -167,6 +167,7 @@ def tile_list_phase_match_families_kernel(
         h_tiles = {}
         banks = []
         pending = []
+        habs_from = {}
         signed = []
         stores = {}
 
@@ -206,35 +207,51 @@ def tile_list_phase_match_families_kernel(
                 root()
             pending.append((h, b, t, sq))
 
-        def residual(h, b, t):
-            if t == 0:
+        def residual(h, b, ts, j0, w):
+            if (h, b) not in d_tiles:
                 d_tiles[h, b] = held([P, 4, JW], F32, "dd%d_%d" % (h, b))
-            acc = next_bank()
-            nc.tensor.matmul_mx(
-                out=acc[:],
-                lhsT=wr_c[b][:, t * 128 : (t + 1) * 128].bitcast(FP8X4),
-                lhsT_scale=wr_s[b][:, t * 128 : (t + 1) * 128],
-                rhs=v2_c[:, h * JW : (h + 1) * JW].bitcast(FP8X4),
-                rhs_scale=v2_s[:, h * JW : (h + 1) * JW],
-                start=True,
-                stop=True,
-            )
-            i = 4 * b + t
-            nc.vector.scalar_tensor_tensor(
-                d_tiles[h, b][:, t, :], acc[:], groot[:, i : i + 1], f_tiles[h, b][:, t, :], ALU.mult, ALU.subtract
-            )
+            bank = next_bank()
+            for k, t in enumerate(ts):
+                nc.tensor.matmul_mx(
+                    out=bank[:, k * w : (k + 1) * w],
+                    lhsT=wr_c[b][:, t * 128 : (t + 1) * 128].bitcast(FP8X4),
+                    lhsT_scale=wr_s[b][:, t * 128 : (t + 1) * 128],
+                    rhs=v2_c[:, h * JW + j0 : h * JW + j0 + w].bitcast(FP8X4),
+                    rhs_scale=v2_s[:, h * JW + j0 : h * JW + j0 + w],
+                    start=True,
+                    stop=True,
+                )
+            for k, t in enumerate(ts):
+                i = 4 * b + t
+                nc.vector.scalar_tensor_tensor(
+                    d_tiles[h, b][:, t, j0 : j0 + w], bank[:, k * w : (k + 1) * w], groot[:, i : i + 1],
+                    f_tiles[h, b][:, t, j0 : j0 + w], ALU.mult, ALU.subtract,
+                )
+
+        def square(h, b, habs, j0, w, on_gpsimd):
+            first = habs_from[h, b]
+            cut = habs[:, j0 - first : j0 - first + w, :]
+            rows = d_tiles[h, b][:, :, j0 : j0 + w]
+            if on_gpsimd:
+                plain = rows.rearrange("p t j -> p j t")
+                nc.gpsimd.tensor_tensor(cut, plain, plain, ALU.mult)
+            else:
+                nc.scalar.activation(
+                    cut.rearrange("p (c i) t -> p c t i", i=4), rows.rearrange("p t (c i) -> p c t i", i=4), ACT.Square
+                )
 
         def field(h, b, j0, w):
-            dd = d_tiles[h, b]
-            first = (h, b) == (0, 0)
             reused = {(0, 0, 0): "slot_g", (0, 1, 0): "v_c1_1", (1, 0, 0): "wp_c1"}
             habs = held([P, w, 4], BF16, "habs%d_%d_%d" % (h, b, j0), reused.get((h, b, j0)))
-            woven = habs[:].rearrange("p (c i) t -> p c t i", i=4)
-            rows = dd[:, :, j0 : j0 + w].rearrange("p t (c i) -> p c t i", i=4)
-            if first:
-                nc.gpsimd.tensor_tensor(woven, rows, rows, ALU.mult)
+            habs_from[h, b] = j0
+            if (h, b) == (0, 0):
+                square(h, b, habs, 0, 256, True)
+                square(h, b, habs, 256, 256, True)
+            elif (h, b, j0) == (0, 1, 256):
+                square(h, b, habs, 256, 128, False)
+                square(h, b, habs, 384, 128, True)
             else:
-                nc.scalar.activation(woven, rows, ACT.Square)
+                square(h, b, habs, j0, w, False)
             hs = held([P, w // 128, 512], BF16, "hs", ("f1_1", "slot_g")[len(signed) % 2])
             signed.append(hs)
             nc.vector.tensor_tensor(
@@ -297,18 +314,19 @@ def tile_list_phase_match_families_kernel(
         quant_wr(0)
         quant_wr(1)
         root()
-        for t in range(4):
-            residual(0, 0, t)
+        for j0 in (0, 256):
+            for ts in ((0, 1), (2, 3)):
+                residual(0, 0, ts, j0, 256)
         for t in range(4):
             modulus(1, 0, t)
         for t in range(4):
-            residual(0, 1, t)
+            residual(0, 1, (t,), 0, JW)
         for t in range(4):
             modulus(1, 1, t)
         root()
         for b in range(2):
             for t in range(4):
-                residual(1, b, t)
+                residual(1, b, (t,), 0, JW)
         pieces = (((0, 256), (256, 256)), ((0, 256), (256, 128), (384, 128)))
         for h in range(2):
             field(h, 0, 0, JW)

@@ -46,8 +46,9 @@ def tile_list_phase_match_families_kernel(
         wps_raw = held([P, H], U8, "wps_raw", "slot_a")
         tw = [held([P, T], I32, "tw%d" % a) for a in range(2)]
 
-        nc.vector.memset(ts_raw[:].bitcast(I32), 0)
-        nc.vector.memset(wps_raw[:].bitcast(I32), 0)
+        nc.vector.memset(ts_raw[:, : 3 * T // 4].bitcast(I32), 0)
+        nc.gpsimd.memset(ts_raw[:, 3 * T // 4 :].bitcast(I32), 0)
+        nc.gpsimd.memset(wps_raw[:].bitcast(I32), 0)
 
         def load_wp(b, raw):
             nc.sync.dma_start(
@@ -60,37 +61,31 @@ def tile_list_phase_match_families_kernel(
 
         nc.sync.dma_start(lists[:], offs)
         nc.sync.dma_start(g_raw[:], gain.rearrange("(b p t) -> p b t", b=2, t=4))
+        nc.sync.dma_start(lists2[:], offs2)
         nc.sync.dma_start(ts_raw[0:P:4, :].bitcast(I32), tab_scales.rearrange("a q t -> q a t").bitcast(I32))
         nc.sync.dma_start(wps_raw[0:P:4, :].bitcast(I32), wp_scales.rearrange("a q c -> q a c").bitcast(I32))
         wp_raw0 = placed([P, RB], I32, "wp_raw0", 7168)
         load_wp(0, wp_raw0[:])
         for a in range(2):
             nc.sync.dma_start(tw[a][:], tab_words[a].rearrange("p t i -> p (t i)").bitcast(I32))
-        wp_raw1 = held([P, RB], I32, "wp_raw1", "slot_d")
-        load_wp(1, wp_raw1[:])
-        nc.sync.dma_start(lists2[:], offs2)
 
         def cols(h):
             return slice(h * JW // 16, (h + 1) * JW // 16)
 
-        ts_got0 = held([P, JW], U8, "ts_got0", "slot_b")
-        staged = placed([P, JW + H], U8, "staged", 23552)
-        plane0 = held([P, 2, JW + H], U8, "plane0")
-        nc.vector.tensor_copy(ts_got0[:], ts_raw[:].indirect(lists[:, cols(0)]))
+        ts_got = placed([P, S], U8, "ts_got", 28160)
+        staged = placed([P, S + H], U8, "staged", 23552)
+        plane = held([P, 2, S + H], U8, "plane")
+        nc.vector.tensor_copy(ts_got[:], ts_raw[:].indirect(lists[:]))
         nc.vector.tensor_copy(
-            staged[:, JW:].rearrange("p (b t m) -> p b m t", b=2, t=4),
-            wps_raw[:].rearrange("p (b m t) -> p b m t", b=2, t=4),
+            staged[:, S:].rearrange("p (b t m) -> p b t m", b=2, t=4),
+            wps_raw[:].rearrange("p (b m t) -> p b t m", b=2, t=4),
         )
-        nc.vector.tensor_copy(staged[:, :JW].bitcast(I32), ts_got0[:].bitcast(I32))
-
-        def move_rows(plane, rows):
-            for d in range(4):
-                nc.scalar.dma_start(
-                    plane[32 * d : 32 * d + 4, :, :].rearrange("p a c -> p (a c)").bitcast(I32),
-                    rows[32 * d : 32 * d + 32 : 4, :].bitcast(I32),
-                )
-
-        move_rows(plane0, staged)
+        nc.vector.tensor_copy(staged[:, :S].bitcast(I32), ts_got[:].bitcast(I32))
+        for d in range(4):
+            nc.sync.dma_start(
+                plane[32 * d : 32 * d + 4, :, :].rearrange("p a c -> p (a c)").bitcast(I32),
+                staged[32 * d : 32 * d + 32 : 4, :].bitcast(I32),
+            )
 
         g = g_raw[:].rearrange("p b t -> p (b t)")
         gabs = keep.tile([P, 8], F32, name="gabs")
@@ -107,8 +102,8 @@ def tile_list_phase_match_families_kernel(
 
         def order_wp(b, raw):
             nc.vector.tensor_copy(
-                wp_c[b][:].bitcast(U16).rearrange("p (a t m) -> p a m t", a=2, t=4),
-                raw.bitcast(U16).rearrange("p (a m t) -> p a m t", a=2, t=4),
+                wp_c[b][:].bitcast(U16).rearrange("p (a t m) -> p a t m", a=2, t=4),
+                raw.bitcast(U16).rearrange("p (a m t) -> p a t m", a=2, t=4),
             )
 
         v_c = {}
@@ -122,17 +117,15 @@ def tile_list_phase_match_families_kernel(
 
         order_wp(0, wp_raw0[:])
         gather_v(0, 0)
-        ts_got1 = held([P, JW], U8, "ts_got1", "slot_a")
-        plane1 = held([P, 2, JW], U8, "plane1")
-        nc.vector.tensor_copy(ts_got1[:], ts_raw[:].indirect(lists[:, cols(1)]))
-        move_rows(plane1, ts_got1)
         gather_v(0, 1)
 
+        wp_raw1 = placed([P, RB], I32, "wp_raw1", 28672)
+        load_wp(1, wp_raw1[:])
         wr_raw = [placed([P, 4, RB], F32, "wr_raw%d" % b, 8192 * (b + 1))[:] for b in range(2)]
         t2w = placed([P, T], I32, "t2w", 0)
         nc.sync.dma_start(t2w[:], tab2_words[0].rearrange("p t i -> p (t i)").bitcast(I32))
         load_wr(0, wr_raw[0])
-        t2s_raw = held([P, T], U8, "t2s_raw", "slot_b")
+        t2s_raw = placed([P, T], U8, "t2s_raw", 26624)
         nc.gpsimd.memset(t2s_raw[:].bitcast(I32), 0)
         for d in range(4):
             nc.sync.dma_start(
@@ -191,13 +184,13 @@ def tile_list_phase_match_families_kernel(
             acc = next_bank()
             for a in range(2):
                 c0 = a * RB + t * 128
-                s0 = JW + b * RB + t * 128
+                s0 = S + b * RB + t * 128
                 nc.tensor.matmul_mx(
                     out=acc[:],
                     lhsT=wp_c[b][:, 2 * c0 : 2 * c0 + 256].bitcast(FP4X4),
-                    lhsT_scale=plane0[:, a, s0 : s0 + 128],
+                    lhsT_scale=plane[:, a, s0 : s0 + 128],
                     rhs=v_c[a, h][:].bitcast(FP8X4),
-                    rhs_scale=(plane0, plane1)[h][:, a, :JW],
+                    rhs_scale=plane[:, a, h * JW : (h + 1) * JW],
                     start=(a == 0),
                     stop=(a == 1),
                 )
@@ -247,12 +240,9 @@ def tile_list_phase_match_families_kernel(
             if (h, b) == (0, 0):
                 square(h, b, habs, 0, 256, True)
                 square(h, b, habs, 256, 256, True)
-            elif (h, b, j0) == (0, 1, 256):
-                square(h, b, habs, 256, 128, False)
-                square(h, b, habs, 384, 128, True)
             else:
                 square(h, b, habs, j0, w, False)
-            hs = held([P, w // 128, 512], BF16, "hs", ("f1_1", "slot_g")[len(signed) % 2])
+            hs = held([P, w // 128, 512], BF16, "hs", ("f1_0", "f1_1")[len(signed) % 2])
             signed.append(hs)
             nc.vector.tensor_tensor(
                 hs[:],
@@ -293,7 +283,7 @@ def tile_list_phase_match_families_kernel(
         for t in range(4):
             modulus(0, 0, t)
         order_wp(1, wp_raw1[:])
-        wf_all = held([P, 2 * N + N // 2], I32, "wf_all", "slot_d")
+        wf_all = placed([P, 2 * N + N // 2], I32, "wf_all", 28672)
         wfw = wf_all[:, : 2 * N]
         wfs = wf_all[:, 2 * N :]
         nc.sync.dma_start(
@@ -327,11 +317,15 @@ def tile_list_phase_match_families_kernel(
         for b in range(2):
             for t in range(4):
                 residual(1, b, (t,), 0, JW)
-        pieces = (((0, 256), (256, 256)), ((0, 256), (256, 128), (384, 128)))
-        for h in range(2):
-            field(h, 0, 0, JW)
-            for j0, w in pieces[h]:
-                scores(h, 0, j0, w)
-            for j0, w in pieces[h]:
-                field(h, 1, j0, w)
-                scores(h, 1, j0, w)
+        halves = ((0, 256), (256, 256))
+        for b in range(2):
+            field(0, b, 0, JW)
+            for j0, w in halves:
+                scores(0, b, j0, w)
+        pieces = ((0, 256), (256, 128), (384, 128))
+        field(1, 0, 0, JW)
+        for j0, w in pieces:
+            scores(1, 0, j0, w)
+        for j0, w in pieces:
+            field(1, 1, j0, w)
+            scores(1, 1, j0, w)

@@ -19,6 +19,14 @@ ACT = mybir.ActivationFunctionType
 P = 128
 JW = 512
 RB = 512
+PIECE = 256
+VECTOR_CLEARS = 3 * T // 4
+
+TAB2_WORDS_AT = 0
+WR_AT = TAB2_WORDS_AT + 4 * T
+LATE_PICKS_AT = WR_AT + 2 * 16 * RB
+TAB2_SCALES_AT = LATE_PICKS_AT + 4 * JW
+WP_SECOND_AT = TAB2_SCALES_AT + T
 
 
 def tile_list_phase_match_families_kernel(
@@ -33,299 +41,280 @@ def tile_list_phase_match_families_kernel(
         stage = ctx.enter_context(tc.tile_pool(name="stage", bufs=5))
         psr = ctx.enter_context(tc.psum_pool(name="psr", bufs=1))
 
-        def held(shape, dtype, name, tag=None):
-            return keep.tile(shape, dtype, name=name, tag=tag or name, align_bytes=64)
+        def held(shape, dtype, name, buffer=None):
+            return keep.tile(shape, dtype, name=name, tag=buffer or name, align_bytes=64)
 
         def placed(shape, dtype, name, offset):
             return reuse.tile(shape, dtype, name=name, offset=offset, align_bytes=64)
 
+        def psum_bank(number):
+            return psr.tile([P, JW], F32, name="bank", tag="bank%d" % number)
+
         lists = keep.tile([P, S // 16], U16, name="lists")
         lists2 = keep.tile([P, S // 16], U16, name="lists2")
         g_raw = keep.tile([P, 2, 4], F32, name="g_raw")
-        ts_raw = held([P, T], U8, "ts_raw", "slot_e")
-        wps_raw = held([P, H], U8, "wps_raw", "slot_a")
-        tw = [held([P, T], I32, "tw%d" % a) for a in range(2)]
+        ts_raw = held([P, T], U8, "ts_raw")
+        wps_raw = held([P, H], U8, "wps_raw")
+        tw = [held([P, T], I32, "tw%d" % kp) for kp in range(2)]
 
-        nc.vector.memset(ts_raw[:, : 3 * T // 4].bitcast(I32), 0)
-        nc.gpsimd.memset(ts_raw[:, 3 * T // 4 :].bitcast(I32), 0)
+        nc.vector.memset(ts_raw[:, :VECTOR_CLEARS].bitcast(I32), 0)
+        nc.gpsimd.memset(ts_raw[:, VECTOR_CLEARS:].bitcast(I32), 0)
         nc.gpsimd.memset(wps_raw[:].bitcast(I32), 0)
 
-        def load_wp(b, raw):
+        def load_wp(blk, raw):
             nc.sync.dma_start(
-                raw.rearrange("p (a c) -> p a c", a=2),
-                wp_words[:, :, 2 * RB * b : 2 * RB * (b + 1)].rearrange("a p c -> p a c").bitcast(I32),
+                raw[:].rearrange("p (kp c) -> p kp c", kp=2),
+                wp_words[:, :, 2 * RB * blk : 2 * RB * (blk + 1)].rearrange("kp p c -> p kp c").bitcast(I32),
             )
 
-        def load_wr(b, raw):
-            nc.sync.dma_start(raw, wr[:, RB * b : RB * (b + 1)].rearrange("(p j) c -> p j c", j=4))
+        def load_wr(blk):
+            nc.sync.dma_start(
+                wr_raw[blk][:], wr[:, RB * blk : RB * (blk + 1)].rearrange("(p i) c -> p i c", i=4)
+            )
 
         nc.sync.dma_start(lists[:], offs)
-        nc.sync.dma_start(g_raw[:], gain.rearrange("(b p t) -> p b t", b=2, t=4))
+        nc.sync.dma_start(g_raw[:], gain.rearrange("(blk p t) -> p blk t", blk=2, t=4))
         nc.sync.dma_start(lists2[:], offs2)
-        nc.sync.dma_start(ts_raw[0:P:4, :].bitcast(I32), tab_scales.rearrange("a q t -> q a t").bitcast(I32))
-        nc.sync.dma_start(wps_raw[0:P:4, :].bitcast(I32), wp_scales.rearrange("a q c -> q a c").bitcast(I32))
-        wp_raw0 = placed([P, RB], I32, "wp_raw0", 7168)
-        load_wp(0, wp_raw0[:])
-        for a in range(2):
-            nc.sync.dma_start(tw[a][:], tab_words[a].rearrange("p t i -> p (t i)").bitcast(I32))
+        nc.sync.dma_start(ts_raw[0:P:4, :].bitcast(I32), tab_scales.rearrange("kp q c -> q kp c").bitcast(I32))
+        nc.sync.dma_start(wps_raw[0:P:4, :].bitcast(I32), wp_scales.rearrange("kp q c -> q kp c").bitcast(I32))
+        wp_raw0 = placed([P, RB], I32, "wp_raw0", WR_AT - 2 * RB)
+        load_wp(0, wp_raw0)
+        for kp in range(2):
+            nc.sync.dma_start(tw[kp][:], tab_words[kp].rearrange("p c i -> p (c i)").bitcast(I32))
 
-        def cols(h):
-            return slice(h * JW // 16, (h + 1) * JW // 16)
-
-        ts_got = placed([P, S], U8, "ts_got", 28160)
-        staged = placed([P, S + H], U8, "staged", 23552)
+        ts_got = placed([P, S], U8, "ts_got", WP_SECOND_AT - S // 2)
+        staged = placed([P, S + H], U8, "staged", LATE_PICKS_AT - (S + H) // 2)
         plane = held([P, 2, S + H], U8, "plane")
         nc.vector.tensor_copy(ts_got[:], ts_raw[:].indirect(lists[:]))
         nc.vector.tensor_copy(
-            staged[:, S:].rearrange("p (b t m) -> p b t m", b=2, t=4),
-            wps_raw[:].rearrange("p (b m t) -> p b t m", b=2, t=4),
+            staged[:, S:].rearrange("p (blk t c) -> p blk t c", blk=2, t=4),
+            wps_raw[:].rearrange("p (blk c t) -> p blk t c", blk=2, t=4),
         )
         nc.vector.tensor_copy(staged[:, :S].bitcast(I32), ts_got[:].bitcast(I32))
-        for d in range(4):
+        for quad in range(4):
             nc.sync.dma_start(
-                plane[32 * d : 32 * d + 4, :, :].rearrange("p a c -> p (a c)").bitcast(I32),
-                staged[32 * d : 32 * d + 32 : 4, :].bitcast(I32),
+                plane[32 * quad : 32 * quad + 4, :, :].rearrange("p kp c -> p (kp c)").bitcast(I32),
+                staged[32 * quad : 32 * quad + 32 : 4, :].bitcast(I32),
             )
 
-        g = g_raw[:].rearrange("p b t -> p (b t)")
+        gains = g_raw[:].rearrange("p blk t -> p (blk t)")
         gabs = keep.tile([P, 8], F32, name="gabs")
         groot = keep.tile([P, 8], F32, name="groot")
         gbias = keep.tile([P, 8], F32, name="gbias")
         signs = held([P, 2, 128, 4], BF16, "signs")
-        nc.vector.scalar_tensor_tensor(gabs[:], g, -1.0, g, ALU.mult, ALU.max)
+        nc.vector.scalar_tensor_tensor(gabs[:], gains, -1.0, gains, ALU.mult, ALU.max)
         nc.scalar.activation(groot[:], gabs[:], ACT.Sqrt)
         nc.scalar.activation(gbias[:], gabs[:], ACT.Copy, scale=0.1)
-        for b in range(2):
-            nc.scalar.activation(signs[:, b, :, :], g_raw[:, b, :].unsqueeze(1).to_broadcast([P, 128, 4]), ACT.Sign)
+        for blk in range(2):
+            nc.scalar.activation(
+                signs[:, blk, :, :], g_raw[:, blk, :].unsqueeze(1).to_broadcast([P, 128, 4]), ACT.Sign
+            )
 
-        wp_c = [held([P, 2 * 2 * RB], U8, "wp_c%d" % b) for b in range(2)]
+        wp_c = [held([P, 2 * 2 * RB], U8, "wp_c%d" % blk) for blk in range(2)]
 
-        def order_wp(b, raw):
+        def order_wp(blk, raw):
             nc.vector.tensor_copy(
-                wp_c[b][:].bitcast(U16).rearrange("p (a t m) -> p a t m", a=2, t=4),
-                raw.bitcast(U16).rearrange("p (a m t) -> p a t m", a=2, t=4),
+                wp_c[blk][:].bitcast(U16).rearrange("p (kp t c) -> p kp t c", kp=2, t=4),
+                raw[:].bitcast(U16).rearrange("p (kp c t) -> p kp t c", kp=2, t=4),
             )
 
         v_c = {}
 
-        def gather_v(h, a):
-            if (h, a) == (1, 0):
-                v_c[a, h] = placed([P, JW], U32, "v_c_late", 24576)
-            else:
-                v_c[a, h] = held([P, JW], U32, "v_c%d_%d" % (a, h))
-            nc.vector.tensor_copy(v_c[a, h][:], tw[a][:].bitcast(U32).indirect(lists[:, cols(h)]))
+        def gather_v(half, kp, picks):
+            v_c[half, kp] = picks
+            entries = lists[:, half * JW // 16 : (half + 1) * JW // 16]
+            nc.vector.tensor_copy(picks[:], tw[kp][:].bitcast(U32).indirect(entries))
 
-        order_wp(0, wp_raw0[:])
-        gather_v(0, 0)
-        gather_v(0, 1)
+        order_wp(0, wp_raw0)
+        gather_v(0, 0, held([P, JW], U32, "v_c0_0"))
+        gather_v(0, 1, held([P, JW], U32, "v_c1_0"))
 
-        wp_raw1 = placed([P, RB], I32, "wp_raw1", 28672)
-        load_wp(1, wp_raw1[:])
-        wr_raw = [placed([P, 4, RB], F32, "wr_raw%d" % b, 8192 * (b + 1))[:] for b in range(2)]
-        t2w = placed([P, T], I32, "t2w", 0)
-        nc.sync.dma_start(t2w[:], tab2_words[0].rearrange("p t i -> p (t i)").bitcast(I32))
-        load_wr(0, wr_raw[0])
-        t2s_raw = placed([P, T], U8, "t2s_raw", 26624)
+        wp_raw1 = placed([P, RB], I32, "wp_raw1", WP_SECOND_AT)
+        load_wp(1, wp_raw1)
+        wr_raw = [placed([P, 4, RB], F32, "wr_raw%d" % blk, WR_AT + 16 * RB * blk) for blk in range(2)]
+        t2w = placed([P, T], I32, "t2w", TAB2_WORDS_AT)
+        nc.sync.dma_start(t2w[:], tab2_words[0].rearrange("p c i -> p (c i)").bitcast(I32))
+        load_wr(0)
+        t2s_raw = placed([P, T], U8, "t2s_raw", TAB2_SCALES_AT)
         nc.gpsimd.memset(t2s_raw[:].bitcast(I32), 0)
-        for d in range(4):
+        for quad in range(4):
             nc.sync.dma_start(
-                t2s_raw[32 * d : 32 * d + 4, :].bitcast(I32), tab2_scales[0, 4 * d : 4 * d + 4, :].bitcast(I32)
+                t2s_raw[32 * quad : 32 * quad + 4, :].bitcast(I32),
+                tab2_scales[0, 4 * quad : 4 * quad + 4, :].bitcast(I32),
             )
-        load_wr(1, wr_raw[1])
+        load_wr(1)
 
         v2_c = held([P, S], U32, "v2_c")
         v2_s = held([P, S], U8, "v2_s")
-
-        def gather_v2():
-            nc.vector.tensor_copy(v2_c[:], t2w[:].bitcast(U32).indirect(lists2[:]))
-            nc.vector.tensor_copy(v2_s[:], t2s_raw[:].indirect(lists2[:]))
-
         wr_g = {}
         wr_c = {}
-        wr_s = [held([P, RB], U8, "wr_s%d" % b) for b in range(2)]
+        wr_s = [held([P, RB], U8, "wr_s%d" % blk) for blk in range(2)]
 
-        def cast_wr(b, raw):
-            wr_g[b] = held([P, 4 * RB], BF16, "wr_g%d" % b, "slot_g" if b else None)
+        def round_wr(blk, rounded):
+            wr_g[blk] = rounded
             nc.vector.tensor_copy(
-                wr_g[b][:].rearrange("p (t m j) -> p m j t", t=4, j=4),
-                raw.rearrange("p j (m t) -> p m j t", t=4),
+                rounded[:].rearrange("p (t c i) -> p c i t", t=4, i=4),
+                wr_raw[blk][:].rearrange("p i (c t) -> p c i t", t=4),
             )
 
-        def quant_wr(b):
-            wr_c[b] = held([P, RB], U32, "wr_c%d" % b)
-            nc.vector.quantize_mx(out=wr_c[b][:].bitcast(FP8X4), scales=wr_s[b][:], in_=wr_g[b][:])
+        def quantise_wr(blk):
+            wr_c[blk] = held([P, RB], U32, "wr_c%d" % blk)
+            nc.vector.quantize_mx(out=wr_c[blk][:].bitcast(FP8X4), scales=wr_s[blk][:], in_=wr_g[blk][:])
 
-        f_tiles = {}
-        d_tiles = {}
-        h_tiles = {}
-        banks = []
-        pending = []
-        habs_from = {}
-        signed = []
-        stores = {}
+        moduli = {}
+        diffs = {}
+        fields = {}
+        sums = {}
+        waiting_root = []
+        signed_tiles = []
 
-        def next_bank():
-            part, t = divmod(len(banks), 4)
-            pair = ((0, 1), (2, 3), (0, 1), (2, 0), (1, 3), (2, 1), (0, 3), (2, 1))[part][t // 2]
-            bank = psr.tile([P, JW], F32, name="bank", tag="bank%d" % (2 * pair + t % 2))
-            banks.append(bank)
-            return bank
-
-        def root():
-            h, b, t, sq = pending.pop()
-            i = 4 * b + t
+        def take_root():
+            half, blk, t, sq = waiting_root.pop()
+            col = 4 * blk + t
             nc.scalar.activation(
-                f_tiles[h, b][:, t, :], sq[:], ACT.Sqrt, bias=gbias[:, i : i + 1], scale=gabs[:, i : i + 1]
+                moduli[half, blk][:, t, :], sq[:], ACT.Sqrt, bias=gbias[:, col : col + 1], scale=gabs[:, col : col + 1]
             )
 
-        def modulus(h, b, t):
-            if t == 0:
-                f_tiles[h, b] = held([P, 4, JW], F32, "f%d_%d" % (h, b))
-            acc = next_bank()
-            for a in range(2):
-                c0 = a * RB + t * 128
-                s0 = S + b * RB + t * 128
-                nc.tensor.matmul_mx(
-                    out=acc[:],
-                    lhsT=wp_c[b][:, 2 * c0 : 2 * c0 + 256].bitcast(FP4X4),
-                    lhsT_scale=plane[:, a, s0 : s0 + 128],
-                    rhs=v_c[a, h][:].bitcast(FP8X4),
-                    rhs_scale=plane[:, a, h * JW : (h + 1) * JW],
-                    start=(a == 0),
-                    stop=(a == 1),
-                )
-            sq = sqp.tile([P, JW], F32, name="sq")
-            nc.scalar.activation(sq[:], acc[:], ACT.Square)
-            if pending:
-                root()
-            pending.append((h, b, t, sq))
+        def modulus(half, blk, banks):
+            moduli[half, blk] = held([P, 4, JW], F32, "f%d_%d" % (half, blk))
+            for t in range(4):
+                acc = psum_bank(banks[t])
+                for kp in range(2):
+                    word0 = kp * RB + t * P
+                    scale0 = S + blk * RB + t * P
+                    nc.tensor.matmul_mx(
+                        out=acc[:],
+                        lhsT=wp_c[blk][:, 2 * word0 : 2 * (word0 + P)].bitcast(FP4X4),
+                        lhsT_scale=plane[:, kp, scale0 : scale0 + P],
+                        rhs=v_c[half, kp][:].bitcast(FP8X4),
+                        rhs_scale=plane[:, kp, half * JW : (half + 1) * JW],
+                        start=(kp == 0),
+                        stop=(kp == 1),
+                    )
+                sq = sqp.tile([P, JW], F32, name="sq")
+                nc.scalar.activation(sq[:], acc[:], ACT.Square)
+                if waiting_root:
+                    take_root()
+                waiting_root.append((half, blk, t, sq))
 
-        def residual(h, b, ts, j0, w):
-            if (h, b) not in d_tiles:
-                d_tiles[h, b] = held([P, 4, JW], F32, "dd%d_%d" % (h, b))
-            bank = next_bank()
-            for k, t in enumerate(ts):
-                nc.tensor.matmul_mx(
-                    out=bank[:, k * w : (k + 1) * w],
-                    lhsT=wr_c[b][:, t * 128 : (t + 1) * 128].bitcast(FP8X4),
-                    lhsT_scale=wr_s[b][:, t * 128 : (t + 1) * 128],
-                    rhs=v2_c[:, h * JW + j0 : h * JW + j0 + w].bitcast(FP8X4),
-                    rhs_scale=v2_s[:, h * JW + j0 : h * JW + j0 + w],
-                    start=True,
-                    stop=True,
-                )
-            for k, t in enumerate(ts):
-                i = 4 * b + t
-                nc.vector.scalar_tensor_tensor(
-                    d_tiles[h, b][:, t, j0 : j0 + w], bank[:, k * w : (k + 1) * w], groot[:, i : i + 1],
-                    f_tiles[h, b][:, t, j0 : j0 + w], ALU.mult, ALU.subtract,
-                )
+        def residual(half, blk, banks, width):
+            diffs[half, blk] = held([P, 4, JW], F32, "dd%d_%d" % (half, blk))
+            in_bank = JW // width
+            for step in range(4):
+                run, first_t = divmod(step * in_bank, 4)
+                j0 = run * width
+                entries = slice(half * JW + j0, half * JW + j0 + width)
+                acc = psum_bank(banks[step])
+                for place in range(in_bank):
+                    t = first_t + place
+                    nc.tensor.matmul_mx(
+                        out=acc[:, place * width : (place + 1) * width],
+                        lhsT=wr_c[blk][:, t * P : (t + 1) * P].bitcast(FP8X4),
+                        lhsT_scale=wr_s[blk][:, t * P : (t + 1) * P],
+                        rhs=v2_c[:, entries].bitcast(FP8X4),
+                        rhs_scale=v2_s[:, entries],
+                        start=True,
+                        stop=True,
+                    )
+                for place in range(in_bank):
+                    t = first_t + place
+                    col = 4 * blk + t
+                    nc.vector.scalar_tensor_tensor(
+                        diffs[half, blk][:, t, j0 : j0 + width], acc[:, place * width : (place + 1) * width],
+                        groot[:, col : col + 1], moduli[half, blk][:, t, j0 : j0 + width], ALU.mult, ALU.subtract,
+                    )
 
-        def square(h, b, habs, j0, w, on_gpsimd):
-            first = habs_from[h, b]
-            cut = habs[:, j0 - first : j0 - first + w, :]
-            rows = d_tiles[h, b][:, :, j0 : j0 + w]
-            if on_gpsimd:
-                plain = rows.rearrange("p t j -> p j t")
-                nc.gpsimd.tensor_tensor(cut, plain, plain, ALU.mult)
-            else:
-                nc.scalar.activation(
-                    cut.rearrange("p (c i) t -> p c t i", i=4), rows.rearrange("p t (c i) -> p c t i", i=4), ACT.Square
-                )
+        def square_on_gpsimd(habs, rows):
+            for j0 in range(0, JW, PIECE):
+                woven = rows[:, :, j0 : j0 + PIECE].rearrange("p t j -> p j t")
+                nc.gpsimd.tensor_tensor(habs[:, j0 : j0 + PIECE, :], woven, woven, ALU.mult)
 
-        def field(h, b, j0, w):
-            reused = {(0, 0, 0): "slot_g", (0, 1, 0): "v_c1_1", (1, 0, 0): "wp_c1"}
-            habs = held([P, w, 4], BF16, "habs%d_%d_%d" % (h, b, j0), reused.get((h, b, j0)))
-            habs_from[h, b] = j0
-            if (h, b) == (0, 0):
-                square(h, b, habs, 0, 256, True)
-                square(h, b, habs, 256, 256, True)
-            else:
-                square(h, b, habs, j0, w, False)
-            hs = held([P, w // 128, 512], BF16, "hs", ("f1_0", "f1_1")[len(signed) % 2])
-            signed.append(hs)
+        def square_on_scalar(habs, rows):
+            nc.scalar.activation(
+                habs[:].rearrange("p (c j) t -> p c t j", j=2), rows.rearrange("p t (c j) -> p c t j", j=2), ACT.Square
+            )
+
+        def field(half, blk, j0, width, square, buffer=None):
+            habs = held([P, width, 4], BF16, "habs%d_%d_%d" % (half, blk, j0), buffer)
+            square(habs, diffs[half, blk][:, :, j0 : j0 + width])
+            hs = held([P, width // 128, 512], BF16, "hs", ("f1_0", "f1_1")[len(signed_tiles) % 2])
+            signed_tiles.append(hs)
             nc.vector.tensor_tensor(
                 hs[:],
-                habs[:].rearrange("p (q j) t -> p q (j t)", j=128),
-                signs[:, b, :, :].rearrange("p j t -> p (j t)").unsqueeze(1).to_broadcast([P, w // 128, 512]),
+                habs[:].rearrange("p (c j) t -> p c (j t)", j=128),
+                signs[:, blk, :, :].rearrange("p j t -> p (j t)").unsqueeze(1).to_broadcast([P, width // 128, 512]),
                 ALU.mult,
             )
-            h_c = held([P, w], U32, "h_c%d_%d_%d" % (h, b, j0))
-            h_s = held([P, w], U8, "h_s%d_%d_%d" % (h, b, j0))
-            nc.vector.quantize_mx(out=h_c[:].bitcast(FP8X4), scales=h_s[:], in_=hs[:].rearrange("p q x -> p (q x)"))
-            h_tiles[h, b] = (h_c, h_s, j0)
+            h_c = held([P, width], U32, "h_c%d_%d_%d" % (half, blk, j0))
+            h_s = held([P, width], U8, "h_s%d_%d_%d" % (half, blk, j0))
+            nc.vector.quantize_mx(out=h_c[:].bitcast(FP8X4), scales=h_s[:], in_=hs[:].rearrange("p c x -> p (c x)"))
+            fields[half, blk] = (h_c, h_s, j0)
 
-        def scores(h, b, j0, w):
-            if b == 0:
-                bank = psr.tile([P, JW], F32, name="bank", tag="bank%d" % len(stores))
-                stores[h, j0] = bank[:, : 2 * w].rearrange("p (n c) -> p n c", n=2)
-            acc = stores[h, j0]
-            h_c, h_s, first = h_tiles[h, b]
+        def scores(half, blk, j0, width, copy=nc.scalar.copy):
+            if blk == 0:
+                sums[half, j0] = psum_bank(len(sums))[:, : 2 * width].rearrange("p (n c) -> p n c", n=2)
+            acc = sums[half, j0]
+            h_c, h_s, h_first = fields[half, blk]
+            entries = slice(j0 - h_first, j0 - h_first + width)
             for n in range(2):
+                columns = slice(blk * N + n * P, blk * N + (n + 1) * P)
                 nc.tensor.matmul_mx(
                     out=acc[:, n, :],
-                    lhsT=wfw[:, b * N + n * 128 : b * N + (n + 1) * 128].bitcast(FP8X4),
-                    lhsT_scale=wfs.bitcast(U8)[:, b * N + n * 128 : b * N + (n + 1) * 128],
-                    rhs=h_c[:, j0 - first : j0 - first + w].bitcast(FP8X4),
-                    rhs_scale=h_s[:, j0 - first : j0 - first + w],
-                    start=(b, n) == (0, 0),
-                    stop=(b, n) == (1, 1),
+                    lhsT=wf_c[:, columns].bitcast(FP8X4),
+                    lhsT_scale=wf_s.bitcast(U8)[:, columns],
+                    rhs=h_c[:, entries].bitcast(FP8X4),
+                    rhs_scale=h_s[:, entries],
+                    start=(blk, n) == (0, 0),
+                    stop=(blk, n) == (1, 1),
                 )
-            if b == 1:
-                res = stage.tile([P, 2, w], F32, name="res")
-                if j0 + w == JW and h == 1:
-                    nc.vector.tensor_copy(res[:], acc)
-                else:
-                    nc.scalar.copy(res[:], acc)
-                c0 = h * JW + j0
-                nc.sync.dma_start(out[:, c0 : c0 + w].rearrange("(n p) c -> p n c", n=2), res[:])
+            if blk == 1:
+                res = stage.tile([P, 2, width], F32, name="res")
+                copy(res[:], acc)
+                c0 = half * JW + j0
+                nc.sync.dma_start(out[:, c0 : c0 + width].rearrange("(n p) c -> p n c", n=2), res[:])
 
-        for t in range(4):
-            modulus(0, 0, t)
-        order_wp(1, wp_raw1[:])
-        wf_all = placed([P, 2 * N + N // 2], I32, "wf_all", 28672)
-        wfw = wf_all[:, : 2 * N]
-        wfs = wf_all[:, 2 * N :]
+        modulus(0, 0, (0, 1, 2, 3))
+        order_wp(1, wp_raw1)
+        wf_all = placed([P, 2 * N + N // 2], I32, "wf_all", WP_SECOND_AT)
+        wf_c = wf_all[:, : 2 * N]
+        wf_s = wf_all[:, 2 * N :]
         nc.sync.dma_start(
-            wfw.rearrange("p (a c) -> p a c", a=2), wf_words.rearrange("a p c i -> p a (c i)").bitcast(I32)
+            wf_c.rearrange("p (kp c) -> p kp c", kp=2), wf_words.rearrange("kp p c i -> p kp (c i)").bitcast(I32)
         )
-        for d in range(4):
+        for quad in range(4):
             nc.sync.dma_start(
-                wfs[32 * d : 32 * d + 4, :].rearrange("p (a c) -> p a c", a=2),
-                wf_scales[:, 4 * d : 4 * d + 4, :].rearrange("a q c -> q a c").bitcast(I32),
+                wf_s[32 * quad : 32 * quad + 4, :].rearrange("p (kp c) -> p kp c", kp=2),
+                wf_scales[:, 4 * quad : 4 * quad + 4, :].rearrange("kp q c -> q kp c").bitcast(I32),
             )
-        for t in range(4):
-            modulus(0, 1, t)
-        gather_v(1, 0)
-        gather_v(1, 1)
-        gather_v2()
-        cast_wr(0, wr_raw[0])
-        cast_wr(1, wr_raw[1])
-        quant_wr(0)
-        quant_wr(1)
-        root()
-        for j0 in (0, 256):
-            for ts in ((0, 1), (2, 3)):
-                residual(0, 0, ts, j0, 256)
-        for t in range(4):
-            modulus(1, 0, t)
-        for t in range(4):
-            residual(0, 1, (t,), 0, JW)
-        for t in range(4):
-            modulus(1, 1, t)
-        root()
-        for b in range(2):
-            for t in range(4):
-                residual(1, b, (t,), 0, JW)
-        halves = ((0, 256), (256, 256))
-        for b in range(2):
-            field(0, b, 0, JW)
-            for j0, w in halves:
-                scores(0, b, j0, w)
-        pieces = ((0, 256), (256, 128), (384, 128))
-        field(1, 0, 0, JW)
-        for j0, w in pieces:
-            scores(1, 0, j0, w)
-        for j0, w in pieces:
-            field(1, 1, j0, w)
-            scores(1, 1, j0, w)
+        modulus(0, 1, (4, 5, 6, 7))
+        gather_v(1, 0, placed([P, JW], U32, "v_c_late", LATE_PICKS_AT))
+        gather_v(1, 1, held([P, JW], U32, "v_c1_1"))
+        nc.vector.tensor_copy(v2_c[:], t2w[:].bitcast(U32).indirect(lists2[:]))
+        nc.vector.tensor_copy(v2_s[:], t2s_raw[:].indirect(lists2[:]))
+        round_wr(0, held([P, 4 * RB], BF16, "wr_g0"))
+        round_wr(1, held([P, 4 * RB], BF16, "wr_g1"))
+        quantise_wr(0)
+        quantise_wr(1)
+        take_root()
+        residual(0, 0, (0, 1, 2, 3), PIECE)
+        modulus(1, 0, (4, 5, 0, 1))
+        residual(0, 1, (2, 3, 6, 7), JW)
+        modulus(1, 1, (4, 5, 2, 3))
+        take_root()
+        residual(1, 0, (0, 1, 6, 7), JW)
+        residual(1, 1, (4, 5, 2, 3), JW)
+
+        halves = ((0, PIECE), (PIECE, PIECE))
+        field(0, 0, 0, JW, square_on_gpsimd, "wr_g1")
+        for j0, width in halves:
+            scores(0, 0, j0, width)
+        field(0, 1, 0, JW, square_on_scalar, "v_c1_1")
+        for j0, width in halves:
+            scores(0, 1, j0, width)
+        pieces = ((0, PIECE), (PIECE, PIECE // 2), (PIECE + PIECE // 2, PIECE // 2))
+        field(1, 0, 0, JW, square_on_scalar, "wp_c1")
+        for j0, width in pieces:
+            scores(1, 0, j0, width)
+        for j0, width in pieces:
+            field(1, 1, j0, width, square_on_scalar)
+            scores(1, 1, j0, width, nc.vector.tensor_copy if j0 + width == JW else nc.scalar.copy)

@@ -26,7 +26,10 @@ TAB2_WORDS_AT = 0
 WR_AT = TAB2_WORDS_AT + 4 * T
 LATE_PICKS_AT = WR_AT + 2 * 16 * RB
 TAB2_SCALES_AT = LATE_PICKS_AT + 4 * JW
-WP_SECOND_AT = TAB2_SCALES_AT + T
+FIRST_MODULUS_AT = TAB2_SCALES_AT + T
+LAST_MODULUS_AT = FIRST_MODULUS_AT + 16 * JW
+ROUNDED_AT = LAST_MODULUS_AT + 16 * JW + 4 * T + 8 * PIECE
+FIRST_TABLE_AT = LAST_MODULUS_AT + 16 * JW
 
 
 def tile_list_phase_match_families_kernel(
@@ -55,7 +58,7 @@ def tile_list_phase_match_families_kernel(
         g_raw = keep.tile([P, 2, 4], F32, name="g_raw")
         ts_raw = held([P, T], U8, "ts_raw")
         wps_raw = held([P, H], U8, "wps_raw")
-        tw = [held([P, T], I32, "tw%d" % kp) for kp in range(2)]
+        tw = [placed([P, T], I32, "tw0", FIRST_TABLE_AT), held([P, T], I32, "tw1")]
 
         nc.vector.memset(ts_raw[:, :VECTOR_CLEARS].bitcast(I32), 0)
         nc.gpsimd.memset(ts_raw[:, VECTOR_CLEARS:].bitcast(I32), 0)
@@ -82,8 +85,8 @@ def tile_list_phase_match_families_kernel(
         for kp in range(2):
             nc.sync.dma_start(tw[kp][:], tab_words[kp].rearrange("p c i -> p (c i)").bitcast(I32))
 
-        ts_got = placed([P, S], U8, "ts_got", WP_SECOND_AT - S // 2)
-        staged = placed([P, S + H], U8, "staged", LATE_PICKS_AT - (S + H) // 2)
+        ts_got = placed([P, S], U8, "ts_got", TAB2_SCALES_AT - S // 2)
+        staged = held([P, S + H], U8, "staged")
         plane = held([P, 2, S + H], U8, "plane")
         nc.vector.tensor_copy(ts_got[:], ts_raw[:].indirect(lists[:]))
         nc.vector.tensor_copy(
@@ -129,7 +132,7 @@ def tile_list_phase_match_families_kernel(
         gather_v(0, 0, held([P, JW], U32, "v_c0_0"))
         gather_v(0, 1, held([P, JW], U32, "v_c1_0"))
 
-        wp_raw1 = placed([P, RB], I32, "wp_raw1", WP_SECOND_AT)
+        wp_raw1 = placed([P, RB], I32, "wp_raw1", LATE_PICKS_AT - 64)
         load_wp(1, wp_raw1)
         wr_raw = [placed([P, 4, RB], F32, "wr_raw%d" % blk, WR_AT + 16 * RB * blk) for blk in range(2)]
         t2w = placed([P, T], I32, "t2w", TAB2_WORDS_AT)
@@ -142,23 +145,24 @@ def tile_list_phase_match_families_kernel(
                 t2s_raw[32 * quad : 32 * quad + 4, :].bitcast(I32),
                 tab2_scales[0, 4 * quad : 4 * quad + 4, :].bitcast(I32),
             )
-        load_wr(1)
 
-        v2_c = held([P, S], U32, "v2_c")
-        v2_s = held([P, S], U8, "v2_s")
+        v2_c = {}
+        v2_s = {}
+
         wr_g = {}
         wr_c = {}
         wr_s = [held([P, RB], U8, "wr_s%d" % blk) for blk in range(2)]
 
         def round_wr(blk, rounded):
             wr_g[blk] = rounded
-            nc.vector.tensor_copy(
-                rounded[:].rearrange("p (t c i) -> p c i t", t=4, i=4),
-                wr_raw[blk][:].rearrange("p i (c t) -> p c i t", t=4),
+            nc.gpsimd.tensor_scalar(
+                rounded[:].rearrange("p (t c i) -> p c t i", t=4, i=4),
+                wr_raw[blk][:].rearrange("p i (c t) -> p c t i", t=4),
+                1.0, 0.0, ALU.mult, ALU.add,
             )
 
-        def quantise_wr(blk):
-            wr_c[blk] = held([P, RB], U32, "wr_c%d" % blk)
+        def quantise_wr(blk, codes):
+            wr_c[blk] = codes
             nc.vector.quantize_mx(out=wr_c[blk][:].bitcast(FP8X4), scales=wr_s[blk][:], in_=wr_g[blk][:])
 
         moduli = {}
@@ -176,7 +180,10 @@ def tile_list_phase_match_families_kernel(
             )
 
         def modulus(half, blk, banks):
-            moduli[half, blk] = held([P, 4, JW], F32, "f%d_%d" % (half, blk))
+            if (half, blk) == (0, 0):
+                moduli[half, blk] = placed([P, 4, JW], F32, "f0_0", FIRST_MODULUS_AT)
+            else:
+                moduli[half, blk] = held([P, 4, JW], F32, "f%d_%d" % (half, blk))
             for t in range(4):
                 acc = psum_bank(banks[t])
                 for kp in range(2):
@@ -197,46 +204,42 @@ def tile_list_phase_match_families_kernel(
                     take_root()
                 waiting_root.append((half, blk, t, sq))
 
-        def residual(half, blk, banks, width):
-            diffs[half, blk] = held([P, 4, JW], F32, "dd%d_%d" % (half, blk))
+        def residual(half, blk, banks, j0, width, tile):
+            diffs[half, blk, j0] = tile
             in_bank = JW // width
-            for step in range(4):
-                run, first_t = divmod(step * in_bank, 4)
-                j0 = run * width
-                entries = slice(half * JW + j0, half * JW + j0 + width)
-                acc = psum_bank(banks[step])
+            entries = slice(j0, j0 + width)
+            for step, bank in enumerate(banks):
+                acc = psum_bank(bank)
                 for place in range(in_bank):
-                    t = first_t + place
+                    t = step * in_bank + place
                     nc.tensor.matmul_mx(
                         out=acc[:, place * width : (place + 1) * width],
                         lhsT=wr_c[blk][:, t * P : (t + 1) * P].bitcast(FP8X4),
                         lhsT_scale=wr_s[blk][:, t * P : (t + 1) * P],
-                        rhs=v2_c[:, entries].bitcast(FP8X4),
-                        rhs_scale=v2_s[:, entries],
+                        rhs=v2_c[half][:, entries].bitcast(FP8X4),
+                        rhs_scale=v2_s[half][:, entries],
                         start=True,
                         stop=True,
                     )
                 for place in range(in_bank):
-                    t = first_t + place
+                    t = step * in_bank + place
                     col = 4 * blk + t
                     nc.vector.scalar_tensor_tensor(
-                        diffs[half, blk][:, t, j0 : j0 + width], acc[:, place * width : (place + 1) * width],
-                        groot[:, col : col + 1], moduli[half, blk][:, t, j0 : j0 + width], ALU.mult, ALU.subtract,
+                        tile[:, t, :], acc[:, place * width : (place + 1) * width],
+                        groot[:, col : col + 1], moduli[half, blk][:, t, entries], ALU.mult, ALU.subtract,
                     )
 
         def square_on_gpsimd(habs, rows):
-            for j0 in range(0, JW, PIECE):
-                woven = rows[:, :, j0 : j0 + PIECE].rearrange("p t j -> p j t")
-                nc.gpsimd.tensor_tensor(habs[:, j0 : j0 + PIECE, :], woven, woven, ALU.mult)
+            woven = rows.rearrange("p t j -> p j t")
+            nc.gpsimd.tensor_tensor(habs, woven, woven, ALU.mult)
 
         def square_on_scalar(habs, rows):
             nc.scalar.activation(
-                habs[:].rearrange("p (c j) t -> p c t j", j=2), rows.rearrange("p t (c j) -> p c t j", j=2), ACT.Square
+                habs.rearrange("p (c j) t -> p c t j", j=2), rows.rearrange("p t (c j) -> p c t j", j=2), ACT.Square
             )
 
-        def field(half, blk, j0, width, square, buffer=None):
-            habs = held([P, width, 4], BF16, "habs%d_%d_%d" % (half, blk, j0), buffer)
-            square(habs, diffs[half, blk][:, :, j0 : j0 + width])
+        def field(half, blk, j0, habs):
+            width = habs.shape[1]
             hs = held([P, width // 128, 512], BF16, "hs", ("f1_0", "f1_1")[len(signed_tiles) % 2])
             signed_tiles.append(hs)
             nc.vector.tensor_tensor(
@@ -252,7 +255,7 @@ def tile_list_phase_match_families_kernel(
 
         def scores(half, blk, j0, width, copy=nc.scalar.copy):
             if blk == 0:
-                sums[half, j0] = psum_bank(len(sums))[:, : 2 * width].rearrange("p (n c) -> p n c", n=2)
+                sums[half, j0] = psum_bank((4, 5, 2, 3, 0)[len(sums)])[:, : 2 * width].rearrange("p (n c) -> p n c", n=2)
             acc = sums[half, j0]
             h_c, h_s, h_first = fields[half, blk]
             entries = slice(j0 - h_first, j0 - h_first + width)
@@ -275,7 +278,19 @@ def tile_list_phase_match_families_kernel(
 
         modulus(0, 0, (0, 1, 2, 3))
         order_wp(1, wp_raw1)
-        wf_all = placed([P, 2 * N + N // 2], I32, "wf_all", WP_SECOND_AT)
+        load_wr(1)
+        modulus(0, 1, (4, 5, 6, 7))
+        gather_v(1, 0, placed([P, JW], U32, "v_c_late", LATE_PICKS_AT))
+        gather_v(1, 1, held([P, JW], U32, "v_c1_1"))
+        picks2 = held([P, S], U32, "v2_c")
+        bytes2 = held([P, S], U8, "v2_s")
+        nc.vector.tensor_copy(picks2[:], t2w[:].bitcast(U32).indirect(lists2[:]))
+        nc.vector.tensor_copy(bytes2[:], t2s_raw[:].indirect(lists2[:]))
+        for half in range(2):
+            v2_c[half] = picks2[:, half * JW : (half + 1) * JW]
+            v2_s[half] = bytes2[:, half * JW : (half + 1) * JW]
+        round_wr(0, held([P, 4 * RB], BF16, "wr_g0"))
+        wf_all = placed([P, 2 * N + N // 2], I32, "wf_all", WR_AT)
         wf_c = wf_all[:, : 2 * N]
         wf_s = wf_all[:, 2 * N :]
         nc.sync.dma_start(
@@ -286,35 +301,41 @@ def tile_list_phase_match_families_kernel(
                 wf_s[32 * quad : 32 * quad + 4, :].rearrange("p (kp c) -> p kp c", kp=2),
                 wf_scales[:, 4 * quad : 4 * quad + 4, :].rearrange("kp q c -> q kp c").bitcast(I32),
             )
-        modulus(0, 1, (4, 5, 6, 7))
-        gather_v(1, 0, placed([P, JW], U32, "v_c_late", LATE_PICKS_AT))
-        gather_v(1, 1, held([P, JW], U32, "v_c1_1"))
-        nc.vector.tensor_copy(v2_c[:], t2w[:].bitcast(U32).indirect(lists2[:]))
-        nc.vector.tensor_copy(v2_s[:], t2s_raw[:].indirect(lists2[:]))
-        round_wr(0, held([P, 4 * RB], BF16, "wr_g0"))
-        round_wr(1, held([P, 4 * RB], BF16, "wr_g1"))
-        quantise_wr(0)
-        quantise_wr(1)
+        round_wr(1, placed([P, 4 * RB], BF16, "wr_g1", ROUNDED_AT))
+        quantise_wr(0, placed([P, RB], U32, "wr_c0", TAB2_SCALES_AT))
         take_root()
-        residual(0, 0, (0, 1, 2, 3), PIECE)
+        residual(0, 0, (0, 1), 0, PIECE, held([P, 4, PIECE], F32, "dd0_0_0")[:])
+        quantise_wr(1, held([P, RB], U32, "wr_c1"))
+        residual(0, 0, (2, 3), PIECE, PIECE, placed([P, 4, PIECE], F32, "dd0_0_1", ROUNDED_AT - 8 * PIECE)[:])
         modulus(1, 0, (4, 5, 0, 1))
-        residual(0, 1, (2, 3, 6, 7), JW)
+        residual(0, 1, (2, 3, 6, 7), 0, JW, held([P, 4, JW], F32, "dd0_1"))
         modulus(1, 1, (4, 5, 2, 3))
         take_root()
-        residual(1, 0, (0, 1, 6, 7), JW)
-        residual(1, 1, (4, 5, 2, 3), JW)
+        residual(1, 0, (0, 1, 6, 7), 0, JW, held([P, 4, JW], F32, "dd1_0", "f0_1"))
+        residual(1, 1, (0, 1, 6, 7), 0, JW, held([P, 4, JW], F32, "dd1_1"))
 
         halves = ((0, PIECE), (PIECE, PIECE))
-        field(0, 0, 0, JW, square_on_gpsimd, "wr_g1")
+        habs = placed([P, JW, 4], BF16, "habs0_0", ROUNDED_AT + 8 * PIECE)
+        for j0, width in halves:
+            square_on_gpsimd(habs[:, j0 : j0 + width, :], diffs[0, 0, j0])
+        field(0, 0, 0, habs)
         for j0, width in halves:
             scores(0, 0, j0, width)
-        field(0, 1, 0, JW, square_on_scalar, "v_c1_1")
+        second = held([P, JW, 4], BF16, "habs0_1", "v_c1_1")
+        square_on_scalar(second[:], diffs[0, 1, 0][:])
+        pieces = ((0, PIECE), (PIECE, PIECE // 2), (PIECE + PIECE // 2, PIECE // 2))
+        third = held([P, JW, 4], BF16, "habs1_0", "wp_c1")
+        square_on_scalar(third[:], diffs[1, 0, 0][:])
+        last = {}
+        for j0, width in pieces:
+            last[j0] = held([P, width, 4], BF16, "habs1_1_%d" % j0)
+            square_on_scalar(last[j0][:], diffs[1, 1, 0][:, :, j0 : j0 + width])
+        field(0, 1, 0, second)
         for j0, width in halves:
             scores(0, 1, j0, width)
-        pieces = ((0, PIECE), (PIECE, PIECE // 2), (PIECE + PIECE // 2, PIECE // 2))
-        field(1, 0, 0, JW, square_on_scalar, "wp_c1")
+        field(1, 0, 0, third)
         for j0, width in pieces:
             scores(1, 0, j0, width)
         for j0, width in pieces:
-            field(1, 1, j0, width, square_on_scalar)
+            field(1, 1, j0, last[j0])
             scores(1, 1, j0, width, nc.vector.tensor_copy if j0 + width == JW else nc.scalar.copy)

@@ -1,6 +1,7 @@
 from contextlib import ExitStack
 
 import concourse.mybir as mybir
+from concourse.masks import make_identity
 
 K, K2, H, N, T, S = 1024, 512, 1024, 256, 2048, 1024
 FLOPS = 2 * S * (K * H + K2 * H + H * N)
@@ -24,12 +25,12 @@ VECTOR_CLEARS = 3 * T // 4
 
 TAB2_WORDS_AT = 0
 WR_AT = TAB2_WORDS_AT + 4 * T
-LATE_PICKS_AT = WR_AT + 2 * 16 * RB
-TAB2_SCALES_AT = LATE_PICKS_AT + 4 * JW
-FIRST_MODULUS_AT = TAB2_SCALES_AT + T
-LAST_MODULUS_AT = FIRST_MODULUS_AT + 16 * JW
-ROUNDED_AT = LAST_MODULUS_AT + 16 * JW + 4 * T + 8 * PIECE
-FIRST_TABLE_AT = LAST_MODULUS_AT + 16 * JW
+TAB2_SCALES_AT = WR_AT + 2 * 16 * RB
+SECOND_ROUNDING_AT = TAB2_SCALES_AT + T - 64
+FIRST_SQUARES_AT = TAB2_SCALES_AT - 64
+SECOND_DIFFS_AT = FIRST_SQUARES_AT + 8 * JW
+LATE_PICKS_AT = SECOND_DIFFS_AT + 16 * JW
+SIGN_BANK = 7
 
 
 def tile_list_phase_match_families_kernel(
@@ -58,7 +59,7 @@ def tile_list_phase_match_families_kernel(
         g_raw = keep.tile([P, 2, 4], F32, name="g_raw")
         ts_raw = held([P, T], U8, "ts_raw")
         wps_raw = held([P, H], U8, "wps_raw")
-        tw = [placed([P, T], I32, "tw0", FIRST_TABLE_AT), held([P, T], I32, "tw1")]
+        tw = [held([P, T], I32, "tw%d" % kp) for kp in range(2)]
 
         nc.vector.memset(ts_raw[:, :VECTOR_CLEARS].bitcast(I32), 0)
         nc.gpsimd.memset(ts_raw[:, VECTOR_CLEARS:].bitcast(I32), 0)
@@ -85,8 +86,8 @@ def tile_list_phase_match_families_kernel(
         for kp in range(2):
             nc.sync.dma_start(tw[kp][:], tab_words[kp].rearrange("p c i -> p (c i)").bitcast(I32))
 
-        ts_got = placed([P, S], U8, "ts_got", TAB2_SCALES_AT - S // 2)
-        staged = held([P, S + H], U8, "staged")
+        ts_got = placed([P, S], U8, "ts_got", TAB2_SCALES_AT)
+        staged = placed([P, S + H], U8, "staged", LATE_PICKS_AT)
         plane = held([P, 2, S + H], U8, "plane")
         nc.vector.tensor_copy(ts_got[:], ts_raw[:].indirect(lists[:]))
         nc.vector.tensor_copy(
@@ -104,14 +105,21 @@ def tile_list_phase_match_families_kernel(
         gabs = keep.tile([P, 8], F32, name="gabs")
         groot = keep.tile([P, 8], F32, name="groot")
         gbias = keep.tile([P, 8], F32, name="gbias")
-        signs = held([P, 2, 128, 4], BF16, "signs")
         nc.vector.scalar_tensor_tensor(gabs[:], gains, -1.0, gains, ALU.mult, ALU.max)
         nc.scalar.activation(groot[:], gabs[:], ACT.Sqrt)
         nc.scalar.activation(gbias[:], gabs[:], ACT.Copy, scale=0.1)
+        ident = keep.tile([P, P], BF16, name="ident")
+        make_identity(nc, ident[:])
+        woven_signs = keep.tile([P, 2, P // 4, 4], BF16, name="woven_signs")
+        nc.scalar.activation(woven_signs[:], g_raw[:].unsqueeze(2).to_broadcast([P, 2, P // 4, 4]), ACT.Sign)
+        turned = psr.tile([P, 2, P], BF16, name="turned", tag="bank%d" % SIGN_BANK)
         for blk in range(2):
-            nc.scalar.activation(
-                signs[:, blk, :, :], g_raw[:, blk, :].unsqueeze(1).to_broadcast([P, 128, 4]), ACT.Sign
-            )
+            nc.tensor.transpose(turned[:, blk, :], woven_signs[:, blk, :, :].rearrange("p j t -> p (j t)"), ident[:])
+        turned_signs = keep.tile([P, 2, P], BF16, name="turned_signs")
+        nc.scalar.copy(turned_signs[:], turned[:])
+        signs = psr.tile([P, 2, P], BF16, name="signs", tag="bank%d" % SIGN_BANK)
+        for blk in range(2):
+            nc.tensor.transpose(signs[:, blk, :], turned_signs[:, blk, :], ident[:])
 
         wp_c = [held([P, 2 * 2 * RB], U8, "wp_c%d" % blk) for blk in range(2)]
 
@@ -132,19 +140,12 @@ def tile_list_phase_match_families_kernel(
         gather_v(0, 0, held([P, JW], U32, "v_c0_0"))
         gather_v(0, 1, held([P, JW], U32, "v_c1_0"))
 
-        wp_raw1 = placed([P, RB], I32, "wp_raw1", LATE_PICKS_AT - 64)
+        wp_raw1 = placed([P, RB], I32, "wp_raw1", TAB2_SCALES_AT - 2 * RB)
         load_wp(1, wp_raw1)
         wr_raw = [placed([P, 4, RB], F32, "wr_raw%d" % blk, WR_AT + 16 * RB * blk) for blk in range(2)]
         t2w = placed([P, T], I32, "t2w", TAB2_WORDS_AT)
         nc.sync.dma_start(t2w[:], tab2_words[0].rearrange("p c i -> p (c i)").bitcast(I32))
         load_wr(0)
-        t2s_raw = placed([P, T], U8, "t2s_raw", TAB2_SCALES_AT)
-        nc.gpsimd.memset(t2s_raw[:].bitcast(I32), 0)
-        for quad in range(4):
-            nc.sync.dma_start(
-                t2s_raw[32 * quad : 32 * quad + 4, :].bitcast(I32),
-                tab2_scales[0, 4 * quad : 4 * quad + 4, :].bitcast(I32),
-            )
 
         v2_c = {}
         v2_s = {}
@@ -153,13 +154,19 @@ def tile_list_phase_match_families_kernel(
         wr_c = {}
         wr_s = [held([P, RB], U8, "wr_s%d" % blk) for blk in range(2)]
 
-        def round_wr(blk, rounded):
+        def round_wr(blk, rounded, on_gpsimd):
             wr_g[blk] = rounded
-            nc.gpsimd.tensor_scalar(
-                rounded[:].rearrange("p (t c i) -> p c t i", t=4, i=4),
-                wr_raw[blk][:].rearrange("p i (c t) -> p c t i", t=4),
-                1.0, 0.0, ALU.mult, ALU.add,
-            )
+            if on_gpsimd:
+                nc.gpsimd.tensor_scalar(
+                    rounded[:].rearrange("p (t c i) -> p c t i", t=4, i=4),
+                    wr_raw[blk][:].rearrange("p i (c t) -> p c t i", t=4),
+                    1.0, 0.0, ALU.mult, ALU.add,
+                )
+            else:
+                nc.vector.tensor_copy(
+                    rounded[:].rearrange("p (t c i) -> p c i t", t=4, i=4),
+                    wr_raw[blk][:].rearrange("p i (c t) -> p c i t", t=4),
+                )
 
         def quantise_wr(blk, codes):
             wr_c[blk] = codes
@@ -179,12 +186,10 @@ def tile_list_phase_match_families_kernel(
                 moduli[half, blk][:, t, :], sq[:], ACT.Sqrt, bias=gbias[:, col : col + 1], scale=gabs[:, col : col + 1]
             )
 
-        def modulus(half, blk, banks):
-            if (half, blk) == (0, 0):
-                moduli[half, blk] = placed([P, 4, JW], F32, "f0_0", FIRST_MODULUS_AT)
-            else:
+        def modulus(half, blk, banks, tiles=range(4)):
+            if 0 in tiles:
                 moduli[half, blk] = held([P, 4, JW], F32, "f%d_%d" % (half, blk))
-            for t in range(4):
+            for t in tiles:
                 acc = psum_bank(banks[t])
                 for kp in range(2):
                     word0 = kp * RB + t * P
@@ -238,24 +243,28 @@ def tile_list_phase_match_families_kernel(
                 habs.rearrange("p (c j) t -> p c t j", j=2), rows.rearrange("p t (c j) -> p c t j", j=2), ACT.Square
             )
 
-        def field(half, blk, j0, habs):
-            width = habs.shape[1]
-            hs = held([P, width // 128, 512], BF16, "hs", ("f1_0", "f1_1")[len(signed_tiles) % 2])
+        def sign(blk, habs, buffer=None):
+            runs = habs.shape[1] * 4 // P
+            hs = held([P, runs, P], BF16, "hs%d" % len(signed_tiles), buffer)
             signed_tiles.append(hs)
             nc.vector.tensor_tensor(
                 hs[:],
-                habs[:].rearrange("p (c j) t -> p c (j t)", j=128),
-                signs[:, blk, :, :].rearrange("p j t -> p (j t)").unsqueeze(1).to_broadcast([P, width // 128, 512]),
+                habs.rearrange("p (c j) t -> p c (j t)", c=runs),
+                signs[:, blk, :].unsqueeze(1).to_broadcast([P, runs, P]),
                 ALU.mult,
             )
-            h_c = held([P, width], U32, "h_c%d_%d_%d" % (half, blk, j0))
+            return hs
+
+        def quantise_h(half, blk, j0, hs, buffer=None):
+            width = hs.shape[1] * P // 4
+            h_c = held([P, width], U32, "h_c%d_%d_%d" % (half, blk, j0), buffer)
             h_s = held([P, width], U8, "h_s%d_%d_%d" % (half, blk, j0))
             nc.vector.quantize_mx(out=h_c[:].bitcast(FP8X4), scales=h_s[:], in_=hs[:].rearrange("p c x -> p (c x)"))
             fields[half, blk] = (h_c, h_s, j0)
 
         def scores(half, blk, j0, width, copy=nc.scalar.copy):
             if blk == 0:
-                sums[half, j0] = psum_bank((4, 5, 2, 3, 0)[len(sums)])[:, : 2 * width].rearrange("p (n c) -> p n c", n=2)
+                sums[half, j0] = psum_bank((3, 4, 2, 5, 6)[len(sums)])[:, : 2 * width].rearrange("p (n c) -> p n c", n=2)
             acc = sums[half, j0]
             h_c, h_s, h_first = fields[half, blk]
             entries = slice(j0 - h_first, j0 - h_first + width)
@@ -277,19 +286,30 @@ def tile_list_phase_match_families_kernel(
                 nc.sync.dma_start(out[:, c0 : c0 + width].rearrange("(n p) c -> p n c", n=2), res[:])
 
         modulus(0, 0, (0, 1, 2, 3))
-        order_wp(1, wp_raw1)
-        load_wr(1)
-        modulus(0, 1, (4, 5, 6, 7))
-        gather_v(1, 0, placed([P, JW], U32, "v_c_late", LATE_PICKS_AT))
         gather_v(1, 1, held([P, JW], U32, "v_c1_1"))
+        gather_v(1, 0, placed([P, JW], U32, "v_c_late", LATE_PICKS_AT))
+        order_wp(1, wp_raw1)
+        t2s_raw = placed([P, T], U8, "t2s_raw", TAB2_SCALES_AT)
+        for quad in range(4):
+            nc.sync.dma_start(
+                t2s_raw[32 * quad : 32 * quad + 32, :].bitcast(I32),
+                tab2_scales[0, 4 * quad : 4 * quad + 4, :].bitcast(I32).partition_broadcast(8),
+            )
+        load_wr(1)
+        modulus(1, 0, (4, 5, 6, 0))
         picks2 = held([P, S], U32, "v2_c")
-        bytes2 = held([P, S], U8, "v2_s")
         nc.vector.tensor_copy(picks2[:], t2w[:].bitcast(U32).indirect(lists2[:]))
-        nc.vector.tensor_copy(bytes2[:], t2s_raw[:].indirect(lists2[:]))
-        for half in range(2):
+        round_wr(0, held([P, 4 * RB], BF16, "wr_g0"), False)
+
+        def gather_bytes2(half):
             v2_c[half] = picks2[:, half * JW : (half + 1) * JW]
-            v2_s[half] = bytes2[:, half * JW : (half + 1) * JW]
-        round_wr(0, held([P, 4 * RB], BF16, "wr_g0"))
+            v2_s[half] = held([P, JW], U8, "v2_s%d" % half)
+            entries = lists2[:, half * JW // 16 : (half + 1) * JW // 16]
+            nc.vector.tensor_copy(v2_s[half][:], t2s_raw[:].indirect(entries))
+
+        gather_bytes2(0)
+        quantise_wr(0, held([P, RB], U32, "wr_c0"))
+        gather_bytes2(1)
         wf_all = placed([P, 2 * N + N // 2], I32, "wf_all", WR_AT)
         wf_c = wf_all[:, : 2 * N]
         wf_s = wf_all[:, 2 * N :]
@@ -301,41 +321,49 @@ def tile_list_phase_match_families_kernel(
                 wf_s[32 * quad : 32 * quad + 4, :].rearrange("p (kp c) -> p kp c", kp=2),
                 wf_scales[:, 4 * quad : 4 * quad + 4, :].rearrange("kp q c -> q kp c").bitcast(I32),
             )
-        round_wr(1, placed([P, 4 * RB], BF16, "wr_g1", ROUNDED_AT))
-        quantise_wr(0, placed([P, RB], U32, "wr_c0", TAB2_SCALES_AT))
+        round_wr(1, placed([P, 4 * RB], BF16, "wr_g1", SECOND_ROUNDING_AT), True)
         take_root()
-        residual(0, 0, (0, 1), 0, PIECE, held([P, 4, PIECE], F32, "dd0_0_0")[:])
+        modulus(0, 1, (1, 2, 3, 4), (0, 1, 2))
+        residual(0, 0, (4, 5, 6, 0), 0, JW, held([P, 4, JW], F32, "dd0_0")[:])
         quantise_wr(1, held([P, RB], U32, "wr_c1"))
-        residual(0, 0, (2, 3), PIECE, PIECE, placed([P, 4, PIECE], F32, "dd0_0_1", ROUNDED_AT - 8 * PIECE)[:])
-        modulus(1, 0, (4, 5, 0, 1))
-        residual(0, 1, (2, 3, 6, 7), 0, JW, held([P, 4, JW], F32, "dd0_1"))
-        modulus(1, 1, (4, 5, 2, 3))
+        modulus(0, 1, (1, 2, 3, 4), (3,))
+        residual(1, 0, (5, 6, 0, 1), 0, JW, placed([P, 4, JW], F32, "dd1_0", SECOND_DIFFS_AT)[:])
+        modulus(1, 1, (2, 3, 4, 2), (0, 1, 2))
+        residual(0, 1, (5, 6, 0, 1), 0, JW, held([P, 4, JW], F32, "dd0_1")[:])
+        modulus(1, 1, (2, 3, 4, 2), (3,))
         take_root()
-        residual(1, 0, (0, 1, 6, 7), 0, JW, held([P, 4, JW], F32, "dd1_0", "f0_1"))
-        residual(1, 1, (0, 1, 6, 7), 0, JW, held([P, 4, JW], F32, "dd1_1"))
+        residual(1, 1, (5, 6, 0, 1), 0, JW, held([P, 4, JW], F32, "dd1_1")[:])
 
         halves = ((0, PIECE), (PIECE, PIECE))
-        habs = placed([P, JW, 4], BF16, "habs0_0", ROUNDED_AT + 8 * PIECE)
-        for j0, width in halves:
-            square_on_gpsimd(habs[:, j0 : j0 + width, :], diffs[0, 0, j0])
-        field(0, 0, 0, habs)
-        for j0, width in halves:
-            scores(0, 0, j0, width)
-        second = held([P, JW, 4], BF16, "habs0_1", "v_c1_1")
-        square_on_scalar(second[:], diffs[0, 1, 0][:])
         pieces = ((0, PIECE), (PIECE, PIECE // 2), (PIECE + PIECE // 2, PIECE // 2))
-        third = held([P, JW, 4], BF16, "habs1_0", "wp_c1")
-        square_on_scalar(third[:], diffs[1, 0, 0][:])
+        first = placed([P, JW, 4], BF16, "habs0_0", FIRST_SQUARES_AT)
+        for j0, width in halves:
+            square_on_gpsimd(first[:, j0 : j0 + width, :], diffs[0, 0, 0][:, :, j0 : j0 + width])
+        second = [held([P, PIECE, 4], BF16, "habs1_0_0"), held([P, PIECE, 4], BF16, "habs1_0_1", "v_c1_1")]
+        square_on_gpsimd(second[0][:], diffs[1, 0, 0][:, :, :PIECE])
+        third = held([P, JW, 4], BF16, "habs0_1", "wp_c1")
+        square_on_scalar(third[:], diffs[0, 1, 0])
+        square_on_scalar(second[1][:], diffs[1, 0, 0][:, :, PIECE:])
         last = {}
         for j0, width in pieces:
             last[j0] = held([P, width, 4], BF16, "habs1_1_%d" % j0)
             square_on_scalar(last[j0][:], diffs[1, 1, 0][:, :, j0 : j0 + width])
-        field(0, 1, 0, second)
+
+        signed_first = sign(0, first[:], "f0_1")
+        signed_second = sign(0, second[0][:], "f1_1")
+        quantise_h(0, 0, 0, signed_first, "habs1_0_0")
+        for j0, width in halves:
+            scores(0, 0, j0, width)
+        quantise_h(1, 0, 0, signed_second)
+        scores(1, 0, 0, PIECE)
+        signed_third = sign(1, third[:])
+        signed_rest = sign(0, second[1][:])
+        quantise_h(0, 1, 0, signed_third)
         for j0, width in halves:
             scores(0, 1, j0, width)
-        field(1, 0, 0, third)
-        for j0, width in pieces:
+        quantise_h(1, 0, PIECE, signed_rest)
+        for j0, width in pieces[1:]:
             scores(1, 0, j0, width)
         for j0, width in pieces:
-            field(1, 1, j0, last[j0])
+            quantise_h(1, 1, j0, sign(1, last[j0][:]))
             scores(1, 1, j0, width, nc.vector.tensor_copy if j0 + width == JW else nc.scalar.copy)

@@ -21,16 +21,18 @@ P = 128
 JW = 512
 RB = 512
 PIECE = 256
-VECTOR_CLEARS = 3 * T // 4
+VECTOR_CLEARS = T // 4
 
 TAB2_WORDS_AT = 0
 WR_AT = TAB2_WORDS_AT + 4 * T
 TAB2_SCALES_AT = WR_AT + 2 * 16 * RB
 SECOND_ROUNDING_AT = TAB2_SCALES_AT + T - 64
-FIRST_SQUARES_AT = TAB2_SCALES_AT - 64
+FIRST_SQUARES_AT = TAB2_SCALES_AT
 SECOND_DIFFS_AT = FIRST_SQUARES_AT + 8 * JW
 LATE_PICKS_AT = SECOND_DIFFS_AT + 16 * JW
+LAST_DIFFS_AT = FIRST_SQUARES_AT + 8 * PIECE - 16 * JW
 SIGN_BANK = 7
+GPSIMD_EXTRA = 128
 
 
 def tile_list_phase_match_families_kernel(
@@ -63,7 +65,7 @@ def tile_list_phase_match_families_kernel(
 
         nc.vector.memset(ts_raw[:, :VECTOR_CLEARS].bitcast(I32), 0)
         nc.gpsimd.memset(ts_raw[:, VECTOR_CLEARS:].bitcast(I32), 0)
-        nc.gpsimd.memset(wps_raw[:].bitcast(I32), 0)
+        nc.vector.memset(wps_raw[:].bitcast(I32), 0)
 
         def load_wp(blk, raw):
             nc.sync.dma_start(
@@ -105,7 +107,7 @@ def tile_list_phase_match_families_kernel(
         gabs = keep.tile([P, 8], F32, name="gabs")
         groot = keep.tile([P, 8], F32, name="groot")
         gbias = keep.tile([P, 8], F32, name="gbias")
-        nc.vector.scalar_tensor_tensor(gabs[:], gains, -1.0, gains, ALU.mult, ALU.max)
+        nc.scalar.activation(gabs[:], gains, ACT.Abs)
         nc.scalar.activation(groot[:], gabs[:], ACT.Sqrt)
         nc.scalar.activation(gbias[:], gabs[:], ACT.Copy, scale=0.1)
         ident = keep.tile([P, P], BF16, name="ident")
@@ -243,10 +245,11 @@ def tile_list_phase_match_families_kernel(
                 habs.rearrange("p (c j) t -> p c t j", j=2), rows.rearrange("p t (c j) -> p c t j", j=2), ACT.Square
             )
 
-        def sign(blk, habs, buffer=None):
+        def sign(blk, habs, hs=None):
             runs = habs.shape[1] * 4 // P
-            hs = held([P, runs, P], BF16, "hs%d" % len(signed_tiles), buffer)
-            signed_tiles.append(hs)
+            if hs is None:
+                hs = held([P, runs, P], BF16, "hs%d" % len(signed_tiles))
+                signed_tiles.append(hs)
             nc.vector.tensor_tensor(
                 hs[:],
                 habs.rearrange("p (c j) t -> p c (j t)", c=runs),
@@ -332,15 +335,19 @@ def tile_list_phase_match_families_kernel(
         residual(0, 1, (5, 6, 0, 1), 0, JW, held([P, 4, JW], F32, "dd0_1")[:])
         modulus(1, 1, (2, 3, 4, 2), (3,))
         take_root()
-        residual(1, 1, (5, 6, 0, 1), 0, JW, held([P, 4, JW], F32, "dd1_1")[:])
 
         halves = ((0, PIECE), (PIECE, PIECE))
         pieces = ((0, PIECE), (PIECE, PIECE // 2), (PIECE + PIECE // 2, PIECE // 2))
-        first = placed([P, JW, 4], BF16, "habs0_0", FIRST_SQUARES_AT)
-        for j0, width in halves:
-            square_on_gpsimd(first[:, j0 : j0 + width, :], diffs[0, 0, 0][:, :, j0 : j0 + width])
-        second = [held([P, PIECE, 4], BF16, "habs1_0_0"), held([P, PIECE, 4], BF16, "habs1_0_1", "v_c1_1")]
-        square_on_gpsimd(second[0][:], diffs[1, 0, 0][:, :, :PIECE])
+        first = [placed([P, PIECE, 4], BF16, "habs0_0_%d" % j0, FIRST_SQUARES_AT + 8 * j0) for j0, width in halves]
+        for piece, (j0, width) in enumerate(halves):
+            square_on_gpsimd(first[piece][:], diffs[0, 0, 0][:, :, j0 : j0 + width])
+        signed_first = held([P, 16, P], BF16, "hs_first", "f0_1")
+        sign(0, first[0][:], signed_first[:, :8, :])
+        residual(1, 1, (5, 6, 0, 1), 0, JW, placed([P, 4, JW], F32, "dd1_1", LAST_DIFFS_AT)[:])
+        sign(0, first[1][:], signed_first[:, 8:, :])
+        second = [held([P, PIECE, 4], BF16, "habs1_0_0", "v_c1_0"), held([P, PIECE, 4], BF16, "habs1_0_1", "v_c1_1")]
+        square_on_gpsimd(second[0][:, :GPSIMD_EXTRA, :], diffs[1, 0, 0][:, :, :GPSIMD_EXTRA])
+        square_on_scalar(second[0][:, GPSIMD_EXTRA:, :], diffs[1, 0, 0][:, :, GPSIMD_EXTRA:PIECE])
         third = held([P, JW, 4], BF16, "habs0_1", "wp_c1")
         square_on_scalar(third[:], diffs[0, 1, 0])
         square_on_scalar(second[1][:], diffs[1, 0, 0][:, :, PIECE:])
@@ -349,9 +356,8 @@ def tile_list_phase_match_families_kernel(
             last[j0] = held([P, width, 4], BF16, "habs1_1_%d" % j0)
             square_on_scalar(last[j0][:], diffs[1, 1, 0][:, :, j0 : j0 + width])
 
-        signed_first = sign(0, first[:], "f0_1")
-        signed_second = sign(0, second[0][:], "f1_1")
-        quantise_h(0, 0, 0, signed_first, "habs1_0_0")
+        signed_second = sign(0, second[0][:], None)
+        quantise_h(0, 0, 0, signed_first, "f1_1")
         for j0, width in halves:
             scores(0, 0, j0, width)
         quantise_h(1, 0, 0, signed_second)

@@ -1,7 +1,6 @@
 from contextlib import ExitStack
 
 import concourse.mybir as mybir
-from concourse.masks import make_identity
 
 K, K2, H, N, T, S = 1024, 512, 1024, 256, 2048, 1024
 FLOPS = 2 * S * (K * H + K2 * H + H * N)
@@ -30,8 +29,6 @@ SECOND_ROUNDING_AT = TAB2_SCALES_AT + T - 64
 FIRST_SQUARES_AT = TAB2_SCALES_AT
 SECOND_DIFFS_AT = FIRST_SQUARES_AT + 8 * JW
 LATE_PICKS_AT = SECOND_DIFFS_AT + 16 * JW
-LAST_DIFFS_AT = FIRST_SQUARES_AT + 8 * PIECE - 16 * JW
-SIGN_BANK = 7
 GPSIMD_EXTRA = 128
 
 
@@ -88,7 +85,7 @@ def tile_list_phase_match_families_kernel(
         for kp in range(2):
             nc.sync.dma_start(tw[kp][:], tab_words[kp].rearrange("p c i -> p (c i)").bitcast(I32))
 
-        ts_got = placed([P, S], U8, "ts_got", TAB2_SCALES_AT)
+        ts_got = placed([P, S], U8, "ts_got", TAB2_SCALES_AT - S // 2)
         staged = placed([P, S + H], U8, "staged", LATE_PICKS_AT)
         plane = held([P, 2, S + H], U8, "plane")
         nc.vector.tensor_copy(ts_got[:], ts_raw[:].indirect(lists[:]))
@@ -110,18 +107,8 @@ def tile_list_phase_match_families_kernel(
         nc.scalar.activation(gabs[:], gains, ACT.Abs)
         nc.scalar.activation(groot[:], gabs[:], ACT.Sqrt)
         nc.scalar.activation(gbias[:], gabs[:], ACT.Copy, scale=0.1)
-        ident = keep.tile([P, P], BF16, name="ident")
-        make_identity(nc, ident[:])
-        woven_signs = keep.tile([P, 2, P // 4, 4], BF16, name="woven_signs")
-        nc.scalar.activation(woven_signs[:], g_raw[:].unsqueeze(2).to_broadcast([P, 2, P // 4, 4]), ACT.Sign)
-        turned = psr.tile([P, 2, P], BF16, name="turned", tag="bank%d" % SIGN_BANK)
-        for blk in range(2):
-            nc.tensor.transpose(turned[:, blk, :], woven_signs[:, blk, :, :].rearrange("p j t -> p (j t)"), ident[:])
-        turned_signs = keep.tile([P, 2, P], BF16, name="turned_signs")
-        nc.scalar.copy(turned_signs[:], turned[:])
-        signs = psr.tile([P, 2, P], BF16, name="signs", tag="bank%d" % SIGN_BANK)
-        for blk in range(2):
-            nc.tensor.transpose(signs[:, blk, :], turned_signs[:, blk, :], ident[:])
+        signs = held([P, 2, P // 4, 4], BF16, "signs")
+        nc.scalar.activation(signs[:], g_raw[:].unsqueeze(2).to_broadcast([P, 2, P // 4, 4]), ACT.Sign)
 
         wp_c = [held([P, 2 * 2 * RB], U8, "wp_c%d" % blk) for blk in range(2)]
 
@@ -142,12 +129,19 @@ def tile_list_phase_match_families_kernel(
         gather_v(0, 0, held([P, JW], U32, "v_c0_0"))
         gather_v(0, 1, held([P, JW], U32, "v_c1_0"))
 
-        wp_raw1 = placed([P, RB], I32, "wp_raw1", TAB2_SCALES_AT - 2 * RB)
+        wp_raw1 = placed([P, RB], I32, "wp_raw1", TAB2_SCALES_AT - 4 * RB)
         load_wp(1, wp_raw1)
         wr_raw = [placed([P, 4, RB], F32, "wr_raw%d" % blk, WR_AT + 16 * RB * blk) for blk in range(2)]
         t2w = placed([P, T], I32, "t2w", TAB2_WORDS_AT)
         nc.sync.dma_start(t2w[:], tab2_words[0].rearrange("p c i -> p (c i)").bitcast(I32))
         load_wr(0)
+        t2s_raw = placed([P, T], U8, "t2s_raw", TAB2_SCALES_AT)
+        nc.gpsimd.memset(t2s_raw[:].bitcast(I32), 0)
+        for quad in range(4):
+            nc.sync.dma_start(
+                t2s_raw[32 * quad : 32 * quad + 4, :].bitcast(I32),
+                tab2_scales[0, 4 * quad : 4 * quad + 4, :].bitcast(I32),
+            )
 
         v2_c = {}
         v2_s = {}
@@ -253,7 +247,7 @@ def tile_list_phase_match_families_kernel(
             nc.vector.tensor_tensor(
                 hs[:],
                 habs.rearrange("p (c j) t -> p c (j t)", c=runs),
-                signs[:, blk, :].unsqueeze(1).to_broadcast([P, runs, P]),
+                signs[:, blk, :, :].rearrange("p j t -> p (j t)").unsqueeze(1).to_broadcast([P, runs, P]),
                 ALU.mult,
             )
             return hs
@@ -267,7 +261,7 @@ def tile_list_phase_match_families_kernel(
 
         def scores(half, blk, j0, width, copy=nc.scalar.copy):
             if blk == 0:
-                sums[half, j0] = psum_bank((3, 4, 2, 5, 6)[len(sums)])[:, : 2 * width].rearrange("p (n c) -> p n c", n=2)
+                sums[half, j0] = psum_bank((0, 1, 2, 3, 7)[len(sums)])[:, : 2 * width].rearrange("p (n c) -> p n c", n=2)
             acc = sums[half, j0]
             h_c, h_s, h_first = fields[half, blk]
             entries = slice(j0 - h_first, j0 - h_first + width)
@@ -292,14 +286,8 @@ def tile_list_phase_match_families_kernel(
         gather_v(1, 1, held([P, JW], U32, "v_c1_1"))
         gather_v(1, 0, placed([P, JW], U32, "v_c_late", LATE_PICKS_AT))
         order_wp(1, wp_raw1)
-        t2s_raw = placed([P, T], U8, "t2s_raw", TAB2_SCALES_AT)
-        for quad in range(4):
-            nc.sync.dma_start(
-                t2s_raw[32 * quad : 32 * quad + 32, :].bitcast(I32),
-                tab2_scales[0, 4 * quad : 4 * quad + 4, :].bitcast(I32).partition_broadcast(8),
-            )
         load_wr(1)
-        modulus(1, 0, (4, 5, 6, 0))
+        modulus(1, 0, (4, 5, 6, 7))
         picks2 = held([P, S], U32, "v2_c")
         nc.vector.tensor_copy(picks2[:], t2w[:].bitcast(U32).indirect(lists2[:]))
         round_wr(0, held([P, 4 * RB], BF16, "wr_g0"), False)
@@ -326,25 +314,21 @@ def tile_list_phase_match_families_kernel(
             )
         round_wr(1, placed([P, 4 * RB], BF16, "wr_g1", SECOND_ROUNDING_AT), True)
         take_root()
-        modulus(0, 1, (1, 2, 3, 4), (0, 1, 2))
-        residual(0, 0, (4, 5, 6, 0), 0, JW, held([P, 4, JW], F32, "dd0_0")[:])
+        modulus(0, 1, (0, 1, 2, 3), (0, 1, 2))
+        residual(0, 0, (3, 4, 5, 6), 0, JW, held([P, 4, JW], F32, "dd0_0")[:])
         quantise_wr(1, held([P, RB], U32, "wr_c1"))
-        modulus(0, 1, (1, 2, 3, 4), (3,))
-        residual(1, 0, (5, 6, 0, 1), 0, JW, placed([P, 4, JW], F32, "dd1_0", SECOND_DIFFS_AT)[:])
-        modulus(1, 1, (2, 3, 4, 2), (0, 1, 2))
-        residual(0, 1, (5, 6, 0, 1), 0, JW, held([P, 4, JW], F32, "dd0_1")[:])
-        modulus(1, 1, (2, 3, 4, 2), (3,))
+        modulus(0, 1, (0, 1, 2, 3), (3,))
+        residual(1, 0, (7, 4, 5, 6), 0, JW, placed([P, 4, JW], F32, "dd1_0", SECOND_DIFFS_AT)[:])
+        modulus(1, 1, (0, 1, 2, 3))
         take_root()
+        residual(0, 1, (7, 4, 5, 6), 0, JW, held([P, 4, JW], F32, "dd0_1")[:])
 
         halves = ((0, PIECE), (PIECE, PIECE))
         pieces = ((0, PIECE), (PIECE, PIECE // 2), (PIECE + PIECE // 2, PIECE // 2))
-        first = [placed([P, PIECE, 4], BF16, "habs0_0_%d" % j0, FIRST_SQUARES_AT + 8 * j0) for j0, width in halves]
-        for piece, (j0, width) in enumerate(halves):
-            square_on_gpsimd(first[piece][:], diffs[0, 0, 0][:, :, j0 : j0 + width])
-        signed_first = held([P, 16, P], BF16, "hs_first", "f0_1")
-        sign(0, first[0][:], signed_first[:, :8, :])
-        residual(1, 1, (5, 6, 0, 1), 0, JW, placed([P, 4, JW], F32, "dd1_1", LAST_DIFFS_AT)[:])
-        sign(0, first[1][:], signed_first[:, 8:, :])
+        first = placed([P, JW, 4], BF16, "habs0_0", FIRST_SQUARES_AT)
+        for j0, width in halves:
+            square_on_gpsimd(first[:, j0 : j0 + width, :], diffs[0, 0, 0][:, :, j0 : j0 + width])
+        residual(1, 1, (7, 4, 5, 6), 0, JW, held([P, 4, JW], F32, "dd1_1")[:])
         second = [held([P, PIECE, 4], BF16, "habs1_0_0", "v_c1_0"), held([P, PIECE, 4], BF16, "habs1_0_1", "v_c1_1")]
         square_on_gpsimd(second[0][:, :GPSIMD_EXTRA, :], diffs[1, 0, 0][:, :, :GPSIMD_EXTRA])
         square_on_scalar(second[0][:, GPSIMD_EXTRA:, :], diffs[1, 0, 0][:, :, GPSIMD_EXTRA:PIECE])
@@ -356,8 +340,9 @@ def tile_list_phase_match_families_kernel(
             last[j0] = held([P, width, 4], BF16, "habs1_1_%d" % j0)
             square_on_scalar(last[j0][:], diffs[1, 1, 0][:, :, j0 : j0 + width])
 
-        signed_second = sign(0, second[0][:], None)
-        quantise_h(0, 0, 0, signed_first, "f1_1")
+        signed_first = sign(0, first[:], held([P, 16, P], BF16, "hs_first", "f1_1"))
+        signed_second = sign(0, second[0][:])
+        quantise_h(0, 0, 0, signed_first)
         for j0, width in halves:
             scores(0, 0, j0, width)
         quantise_h(1, 0, 0, signed_second)

@@ -29,7 +29,7 @@ SECOND_ROUNDING_AT = TAB2_SCALES_AT + T - 64
 FIRST_SQUARES_AT = TAB2_SCALES_AT
 SECOND_DIFFS_AT = FIRST_SQUARES_AT + 8 * JW
 LATE_PICKS_AT = SECOND_DIFFS_AT + 16 * JW
-GPSIMD_EXTRA = 128
+FIRST_DIFFS_AT = LATE_PICKS_AT + 4 * JW
 
 
 def tile_list_phase_match_families_kernel(
@@ -315,7 +315,7 @@ def tile_list_phase_match_families_kernel(
         round_wr(1, placed([P, 4 * RB], BF16, "wr_g1", SECOND_ROUNDING_AT), True)
         take_root()
         modulus(0, 1, (0, 1, 2, 3), (0, 1, 2))
-        residual(0, 0, (3, 4, 5, 6), 0, JW, held([P, 4, JW], F32, "dd0_0")[:])
+        residual(0, 0, (3, 4, 5, 6), 0, JW, placed([P, 4, JW], F32, "dd0_0", FIRST_DIFFS_AT)[:])
         quantise_wr(1, held([P, RB], U32, "wr_c1"))
         modulus(0, 1, (0, 1, 2, 3), (3,))
         residual(1, 0, (7, 4, 5, 6), 0, JW, placed([P, 4, JW], F32, "dd1_0", SECOND_DIFFS_AT)[:])
@@ -326,12 +326,10 @@ def tile_list_phase_match_families_kernel(
         halves = ((0, PIECE), (PIECE, PIECE))
         pieces = ((0, PIECE), (PIECE, PIECE // 2), (PIECE + PIECE // 2, PIECE // 2))
         first = placed([P, JW, 4], BF16, "habs0_0", FIRST_SQUARES_AT)
-        for j0, width in halves:
-            square_on_gpsimd(first[:, j0 : j0 + width, :], diffs[0, 0, 0][:, :, j0 : j0 + width])
+        square_on_gpsimd(first[:], diffs[0, 0, 0])
         residual(1, 1, (7, 4, 5, 6), 0, JW, held([P, 4, JW], F32, "dd1_1")[:])
         second = [held([P, PIECE, 4], BF16, "habs1_0_0", "v_c1_0"), held([P, PIECE, 4], BF16, "habs1_0_1", "v_c1_1")]
-        square_on_gpsimd(second[0][:, :GPSIMD_EXTRA, :], diffs[1, 0, 0][:, :, :GPSIMD_EXTRA])
-        square_on_scalar(second[0][:, GPSIMD_EXTRA:, :], diffs[1, 0, 0][:, :, GPSIMD_EXTRA:PIECE])
+        square_on_scalar(second[0][:], diffs[1, 0, 0][:, :, :PIECE])
         third = held([P, JW, 4], BF16, "habs0_1", "wp_c1")
         square_on_scalar(third[:], diffs[0, 1, 0])
         square_on_scalar(second[1][:], diffs[1, 0, 0][:, :, PIECE:])
@@ -340,15 +338,15 @@ def tile_list_phase_match_families_kernel(
             last[j0] = held([P, width, 4], BF16, "habs1_1_%d" % j0)
             square_on_scalar(last[j0][:], diffs[1, 1, 0][:, :, j0 : j0 + width])
 
-        signed_first = sign(0, first[:], held([P, 16, P], BF16, "hs_first", "f1_1"))
-        signed_second = sign(0, second[0][:])
+        signed_first = sign(0, first[:], None)
+        signed_second = sign(0, second[0][:], placed([P, 8, P], BF16, "hs_second", FIRST_DIFFS_AT))
         quantise_h(0, 0, 0, signed_first)
         for j0, width in halves:
             scores(0, 0, j0, width)
         quantise_h(1, 0, 0, signed_second)
         scores(1, 0, 0, PIECE)
-        signed_third = sign(1, third[:])
-        signed_rest = sign(0, second[1][:])
+        signed_third = sign(1, third[:], placed([P, 16, P], BF16, "hs_third", FIRST_DIFFS_AT + 8 * JW))
+        signed_rest = sign(0, second[1][:], placed([P, 8, P], BF16, "hs_rest", FIRST_DIFFS_AT + 8 * PIECE))
         quantise_h(0, 1, 0, signed_third)
         for j0, width in halves:
             scores(0, 1, j0, width)

@@ -261,7 +261,7 @@ def tile_list_phase_match_families_kernel(
 
         def scores(half, blk, j0, width, copy=nc.scalar.copy):
             if blk == 0:
-                sums[half, j0] = psum_bank((0, 1, 2, 3, 7)[len(sums)])[:, : 2 * width].rearrange("p (n c) -> p n c", n=2)
+                sums[half, j0] = psum_bank((4, 5, 6, 3, 7)[len(sums)])[:, : 2 * width].rearrange("p (n c) -> p n c", n=2)
             acc = sums[half, j0]
             h_c, h_s, h_first = fields[half, blk]
             entries = slice(j0 - h_first, j0 - h_first + width)
@@ -318,16 +318,16 @@ def tile_list_phase_match_families_kernel(
         residual(0, 0, (3, 4, 5, 6), 0, JW, placed([P, 4, JW], F32, "dd0_0", FIRST_DIFFS_AT)[:])
         quantise_wr(1, held([P, RB], U32, "wr_c1"))
         modulus(0, 1, (0, 1, 2, 3), (3,))
-        residual(1, 0, (7, 4, 5, 6), 0, JW, placed([P, 4, JW], F32, "dd1_0", SECOND_DIFFS_AT)[:])
-        modulus(1, 1, (0, 1, 2, 3))
+        residual(1, 0, (7, 0, 1, 2), 0, JW, placed([P, 4, JW], F32, "dd1_0", SECOND_DIFFS_AT)[:])
+        modulus(1, 1, (4, 5, 6, 3))
         take_root()
-        residual(0, 1, (7, 4, 5, 6), 0, JW, held([P, 4, JW], F32, "dd0_1")[:])
+        residual(0, 1, (7, 0, 1, 2), 0, JW, held([P, 4, JW], F32, "dd0_1")[:])
 
         halves = ((0, PIECE), (PIECE, PIECE))
         pieces = ((0, PIECE), (PIECE, PIECE // 2), (PIECE + PIECE // 2, PIECE // 2))
         first = placed([P, JW, 4], BF16, "habs0_0", FIRST_SQUARES_AT)
         square_on_gpsimd(first[:], diffs[0, 0, 0])
-        residual(1, 1, (7, 4, 5, 6), 0, JW, held([P, 4, JW], F32, "dd1_1")[:])
+        residual(1, 1, (7, 0, 1, 2), 0, JW, held([P, 4, JW], F32, "dd1_1")[:])
         second = [held([P, PIECE, 4], BF16, "habs1_0_0", "v_c1_0"), held([P, PIECE, 4], BF16, "habs1_0_1", "v_c1_1")]
         square_on_scalar(second[0][:], diffs[1, 0, 0][:, :, :PIECE])
         third = held([P, JW, 4], BF16, "habs0_1", "wp_c1")

@@ -22,9 +22,10 @@ RB = 512
 PIECE = 256
 VECTOR_CLEARS = T // 4
 
-TAB2_WORDS_AT = 0
-WR_AT = TAB2_WORDS_AT + 4 * T
-TAB2_SCALES_AT = WR_AT + 2 * 16 * RB
+WR_AT = 0
+WP_SECOND_AT = WR_AT + 16 * RB
+TAB2_WORDS_AT = WP_SECOND_AT + 4 * RB
+TAB2_SCALES_AT = TAB2_WORDS_AT + 4 * T
 SECOND_ROUNDING_AT = TAB2_SCALES_AT + T - 64
 FIRST_SQUARES_AT = TAB2_SCALES_AT
 SECOND_DIFFS_AT = FIRST_SQUARES_AT + 8 * JW
@@ -80,7 +81,7 @@ def tile_list_phase_match_families_kernel(
         nc.sync.dma_start(lists2[:], offs2)
         nc.sync.dma_start(ts_raw[0:P:4, :].bitcast(I32), tab_scales.rearrange("kp q c -> q kp c").bitcast(I32))
         nc.sync.dma_start(wps_raw[0:P:4, :].bitcast(I32), wp_scales.rearrange("kp q c -> q kp c").bitcast(I32))
-        wp_raw0 = placed([P, RB], I32, "wp_raw0", WR_AT - 2 * RB)
+        wp_raw0 = placed([P, RB], I32, "wp_raw0", WP_SECOND_AT - 2 * RB)
         load_wp(0, wp_raw0)
         for kp in range(2):
             nc.sync.dma_start(tw[kp][:], tab_words[kp].rearrange("p c i -> p (c i)").bitcast(I32))
@@ -129,11 +130,11 @@ def tile_list_phase_match_families_kernel(
         gather_v(0, 0, held([P, JW], U32, "v_c0_0"))
         gather_v(0, 1, held([P, JW], U32, "v_c1_0"))
 
-        wp_raw1 = placed([P, RB], I32, "wp_raw1", TAB2_SCALES_AT - 4 * RB)
-        load_wp(1, wp_raw1)
-        wr_raw = [placed([P, 4, RB], F32, "wr_raw%d" % blk, WR_AT + 16 * RB * blk) for blk in range(2)]
         t2w = placed([P, T], I32, "t2w", TAB2_WORDS_AT)
         nc.sync.dma_start(t2w[:], tab2_words[0].rearrange("p c i -> p (c i)").bitcast(I32))
+        wp_raw1 = placed([P, RB], I32, "wp_raw1", WP_SECOND_AT)
+        load_wp(1, wp_raw1)
+        wr_raw = {0: placed([P, 4, RB], F32, "wr_raw0", WR_AT)}
         load_wr(0)
         t2s_raw = placed([P, T], U8, "t2s_raw", TAB2_SCALES_AT)
         nc.gpsimd.memset(t2s_raw[:].bitcast(I32), 0)
@@ -285,11 +286,12 @@ def tile_list_phase_match_families_kernel(
         modulus(0, 0, (0, 1, 2, 3))
         gather_v(1, 1, held([P, JW], U32, "v_c1_1"))
         gather_v(1, 0, placed([P, JW], U32, "v_c_late", LATE_PICKS_AT))
-        order_wp(1, wp_raw1)
+        wr_raw[1] = held([P, 4, RB], F32, "wr_raw1", "tw0")
         load_wr(1)
         modulus(1, 0, (4, 5, 6, 7))
         picks2 = held([P, S], U32, "v2_c")
         nc.vector.tensor_copy(picks2[:], t2w[:].bitcast(U32).indirect(lists2[:]))
+        order_wp(1, wp_raw1)
         round_wr(0, held([P, 4 * RB], BF16, "wr_g0"), False)
 
         def gather_bytes2(half):

@@ -22,14 +22,16 @@ RB = 512
 PIECE = 256
 VECTOR_CLEARS = T // 4
 
-WR_AT = 0
-WP_SECOND_AT = WR_AT + 16 * RB
-TAB2_WORDS_AT = WP_SECOND_AT + 4 * RB
-TAB2_SCALES_AT = TAB2_WORDS_AT + 4 * T
-SECOND_ROUNDING_AT = TAB2_SCALES_AT + T - 64
-FIRST_SQUARES_AT = TAB2_SCALES_AT
-SECOND_DIFFS_AT = FIRST_SQUARES_AT + 8 * JW
-LATE_PICKS_AT = SECOND_DIFFS_AT + 16 * JW
+TAB2_WORDS_AT = 0
+WP_SECOND_AT = TAB2_WORDS_AT + 4 * T
+WP_ORDERED_AT = WP_SECOND_AT + 4 * RB
+WR_SECOND_AT = WP_ORDERED_AT + 4 * RB
+SECOND_PICKS_AT = WR_SECOND_AT - JW // 2
+FIRST_PICKS_END = SECOND_PICKS_AT + 64
+WR_AT = WR_SECOND_AT + 16 * RB
+TAB2_SCALES_AT = WR_AT + 16 * RB
+SHARED_AT = TAB2_SCALES_AT + T - 64
+LATE_PICKS_AT = SHARED_AT + 24 * JW
 FIRST_DIFFS_AT = LATE_PICKS_AT + 4 * JW
 
 
@@ -57,7 +59,7 @@ def tile_list_phase_match_families_kernel(
         lists = keep.tile([P, S // 16], U16, name="lists")
         lists2 = keep.tile([P, S // 16], U16, name="lists2")
         g_raw = keep.tile([P, 2, 4], F32, name="g_raw")
-        ts_raw = held([P, T], U8, "ts_raw")
+        ts_raw = placed([P, T], U8, "ts_raw", TAB2_SCALES_AT - T // 2)
         wps_raw = held([P, H], U8, "wps_raw")
         tw = [held([P, T], I32, "tw%d" % kp) for kp in range(2)]
 
@@ -76,30 +78,36 @@ def tile_list_phase_match_families_kernel(
                 wr_raw[blk][:], wr[:, RB * blk : RB * (blk + 1)].rearrange("(p i) c -> p i c", i=4)
             )
 
+        wp_raw0 = held([P, RB], I32, "wp_raw0")
         nc.sync.dma_start(lists[:], offs)
+        load_wp(0, wp_raw0)
         nc.sync.dma_start(g_raw[:], gain.rearrange("(blk p t) -> p blk t", blk=2, t=4))
         nc.sync.dma_start(lists2[:], offs2)
         nc.sync.dma_start(ts_raw[0:P:4, :].bitcast(I32), tab_scales.rearrange("kp q c -> q kp c").bitcast(I32))
         nc.sync.dma_start(wps_raw[0:P:4, :].bitcast(I32), wp_scales.rearrange("kp q c -> q kp c").bitcast(I32))
-        wp_raw0 = placed([P, RB], I32, "wp_raw0", WP_SECOND_AT - 2 * RB)
-        load_wp(0, wp_raw0)
         for kp in range(2):
             nc.sync.dma_start(tw[kp][:], tab_words[kp].rearrange("p c i -> p (c i)").bitcast(I32))
 
-        ts_got = placed([P, S], U8, "ts_got", TAB2_SCALES_AT - S // 2)
-        staged = placed([P, S + H], U8, "staged", LATE_PICKS_AT)
-        plane = held([P, 2, S + H], U8, "plane")
-        nc.vector.tensor_copy(ts_got[:], ts_raw[:].indirect(lists[:]))
+        def gather_bytes(half, picks):
+            nc.vector.tensor_copy(picks, ts_raw[:].indirect(lists[:, half * JW // 16 : (half + 1) * JW // 16]))
+
+        def move_rows(planes, rows):
+            for quad in (0, 2, 1, 3):
+                nc.sync.dma_start(
+                    planes[32 * quad : 32 * quad + 4, :, :].rearrange("p kp c -> p (kp c)").bitcast(I32),
+                    rows[32 * quad : 32 * quad + 32 : 4, :].bitcast(I32),
+                )
+
+        first_got = placed([P, FIRST_PICKS_END], U8, "first_got", 0)[:, :JW]
+        staged = placed([P, JW + H], U8, "staged", LATE_PICKS_AT)
+        plane = held([P, 2, JW + H], U8, "plane")
+        gather_bytes(0, first_got)
         nc.vector.tensor_copy(
-            staged[:, S:].rearrange("p (blk t c) -> p blk t c", blk=2, t=4),
+            staged[:, JW:].rearrange("p (blk t c) -> p blk t c", blk=2, t=4),
             wps_raw[:].rearrange("p (blk c t) -> p blk t c", blk=2, t=4),
         )
-        nc.vector.tensor_copy(staged[:, :S].bitcast(I32), ts_got[:].bitcast(I32))
-        for quad in range(4):
-            nc.sync.dma_start(
-                plane[32 * quad : 32 * quad + 4, :, :].rearrange("p kp c -> p (kp c)").bitcast(I32),
-                staged[32 * quad : 32 * quad + 32 : 4, :].bitcast(I32),
-            )
+        nc.vector.tensor_copy(staged[:, :JW].bitcast(I32), first_got.bitcast(I32))
+        move_rows(plane, staged)
 
         gains = g_raw[:].rearrange("p blk t -> p (blk t)")
         gabs = keep.tile([P, 8], F32, name="gabs")
@@ -111,7 +119,7 @@ def tile_list_phase_match_families_kernel(
         signs = held([P, 2, P // 4, 4], BF16, "signs")
         nc.scalar.activation(signs[:], g_raw[:].unsqueeze(2).to_broadcast([P, 2, P // 4, 4]), ACT.Sign)
 
-        wp_c = [held([P, 2 * 2 * RB], U8, "wp_c%d" % blk) for blk in range(2)]
+        wp_c = {0: held([P, 2 * 2 * RB], U8, "wp_c0")}
 
         def order_wp(blk, raw):
             nc.vector.tensor_copy(
@@ -128,12 +136,17 @@ def tile_list_phase_match_families_kernel(
 
         order_wp(0, wp_raw0)
         gather_v(0, 0, held([P, JW], U32, "v_c0_0"))
+        second_got = placed([P, JW], U8, "second_got", SECOND_PICKS_AT)
+        gather_bytes(1, second_got[:])
         gather_v(0, 1, held([P, JW], U32, "v_c1_0"))
 
         t2w = placed([P, T], I32, "t2w", TAB2_WORDS_AT)
         nc.sync.dma_start(t2w[:], tab2_words[0].rearrange("p c i -> p (c i)").bitcast(I32))
         wp_raw1 = placed([P, RB], I32, "wp_raw1", WP_SECOND_AT)
         load_wp(1, wp_raw1)
+        late_plane = held([P, 2, JW], U8, "late_plane")
+        move_rows(late_plane, second_got)
+        v_s = (plane, late_plane)
         wr_raw = {0: placed([P, 4, RB], F32, "wr_raw0", WR_AT)}
         load_wr(0)
         t2s_raw = placed([P, T], U8, "t2s_raw", TAB2_SCALES_AT)
@@ -155,19 +168,19 @@ def tile_list_phase_match_families_kernel(
             wr_g[blk] = rounded
             if on_gpsimd:
                 nc.gpsimd.tensor_scalar(
-                    rounded[:].rearrange("p (t c i) -> p c t i", t=4, i=4),
+                    rounded.rearrange("p (t c i) -> p c t i", t=4, i=4),
                     wr_raw[blk][:].rearrange("p i (c t) -> p c t i", t=4),
                     1.0, 0.0, ALU.mult, ALU.add,
                 )
             else:
                 nc.vector.tensor_copy(
-                    rounded[:].rearrange("p (t c i) -> p c i t", t=4, i=4),
+                    rounded.rearrange("p (t c i) -> p c i t", t=4, i=4),
                     wr_raw[blk][:].rearrange("p i (c t) -> p c i t", t=4),
                 )
 
         def quantise_wr(blk, codes):
             wr_c[blk] = codes
-            nc.vector.quantize_mx(out=wr_c[blk][:].bitcast(FP8X4), scales=wr_s[blk][:], in_=wr_g[blk][:])
+            nc.vector.quantize_mx(out=wr_c[blk][:].bitcast(FP8X4), scales=wr_s[blk][:], in_=wr_g[blk])
 
         moduli = {}
         diffs = {}
@@ -190,13 +203,13 @@ def tile_list_phase_match_families_kernel(
                 acc = psum_bank(banks[t])
                 for kp in range(2):
                     word0 = kp * RB + t * P
-                    scale0 = S + blk * RB + t * P
+                    scale0 = JW + blk * RB + t * P
                     nc.tensor.matmul_mx(
                         out=acc[:],
                         lhsT=wp_c[blk][:, 2 * word0 : 2 * (word0 + P)].bitcast(FP4X4),
                         lhsT_scale=plane[:, kp, scale0 : scale0 + P],
                         rhs=v_c[half, kp][:].bitcast(FP8X4),
-                        rhs_scale=plane[:, kp, half * JW : (half + 1) * JW],
+                        rhs_scale=v_s[half][:, kp, :JW],
                         start=(kp == 0),
                         stop=(kp == 1),
                     )
@@ -206,12 +219,12 @@ def tile_list_phase_match_families_kernel(
                     take_root()
                 waiting_root.append((half, blk, t, sq))
 
-        def residual(half, blk, banks, j0, width, tile):
+        def residual(half, blk, banks, j0, width, tile, steps=range(4)):
             diffs[half, blk, j0] = tile
             in_bank = JW // width
             entries = slice(j0, j0 + width)
-            for step, bank in enumerate(banks):
-                acc = psum_bank(bank)
+            for step in steps:
+                acc = psum_bank(banks[step])
                 for place in range(in_bank):
                     t = step * in_bank + place
                     nc.tensor.matmul_mx(
@@ -286,13 +299,14 @@ def tile_list_phase_match_families_kernel(
         modulus(0, 0, (0, 1, 2, 3))
         gather_v(1, 1, held([P, JW], U32, "v_c1_1"))
         gather_v(1, 0, placed([P, JW], U32, "v_c_late", LATE_PICKS_AT))
-        wr_raw[1] = held([P, 4, RB], F32, "wr_raw1", "tw0")
+        wr_raw[1] = placed([P, 4, RB], F32, "wr_raw1", WR_SECOND_AT)
         load_wr(1)
         modulus(1, 0, (4, 5, 6, 7))
         picks2 = held([P, S], U32, "v2_c")
         nc.vector.tensor_copy(picks2[:], t2w[:].bitcast(U32).indirect(lists2[:]))
+        wp_c[1] = placed([P, 2 * 2 * RB], U8, "wp_c1", WP_ORDERED_AT)
         order_wp(1, wp_raw1)
-        round_wr(0, held([P, 4 * RB], BF16, "wr_g0"), False)
+        round_wr(0, held([P, 4 * RB], BF16, "wr_g0")[:], False)
 
         def gather_bytes2(half):
             v2_c[half] = picks2[:, half * JW : (half + 1) * JW]
@@ -314,25 +328,28 @@ def tile_list_phase_match_families_kernel(
                 wf_s[32 * quad : 32 * quad + 4, :].rearrange("p (kp c) -> p kp c", kp=2),
                 wf_scales[:, 4 * quad : 4 * quad + 4, :].rearrange("kp q c -> q kp c").bitcast(I32),
             )
-        round_wr(1, placed([P, 4 * RB], BF16, "wr_g1", SECOND_ROUNDING_AT), True)
+        shared = placed([P, 6 * JW], F32, "shared", SHARED_AT)
+        round_wr(1, shared[:, 3 * JW - 16 : 5 * JW - 16].bitcast(BF16), True)
         take_root()
         modulus(0, 1, (0, 1, 2, 3), (0, 1, 2))
         residual(0, 0, (3, 4, 5, 6), 0, JW, placed([P, 4, JW], F32, "dd0_0", FIRST_DIFFS_AT)[:])
+        second_diffs = shared[:, : 4 * JW].rearrange("p (t j) -> p t j", t=4)
+        residual(1, 0, (7, 0, 1, 2), 0, JW, second_diffs, (0, 1))
         quantise_wr(1, held([P, RB], U32, "wr_c1"))
         modulus(0, 1, (0, 1, 2, 3), (3,))
-        residual(1, 0, (7, 0, 1, 2), 0, JW, placed([P, 4, JW], F32, "dd1_0", SECOND_DIFFS_AT)[:])
+        residual(1, 0, (7, 0, 1, 2), 0, JW, second_diffs, (2, 3))
         modulus(1, 1, (4, 5, 6, 3))
         take_root()
         residual(0, 1, (7, 0, 1, 2), 0, JW, held([P, 4, JW], F32, "dd0_1")[:])
 
         halves = ((0, PIECE), (PIECE, PIECE))
         pieces = ((0, PIECE), (PIECE, PIECE // 2), (PIECE + PIECE // 2, PIECE // 2))
-        first = placed([P, JW, 4], BF16, "habs0_0", FIRST_SQUARES_AT)
-        square_on_gpsimd(first[:], diffs[0, 0, 0])
+        first = shared[:, 4 * JW :].bitcast(BF16).rearrange("p (j t) -> p j t", t=4)
+        square_on_gpsimd(first, diffs[0, 0, 0])
         residual(1, 1, (7, 0, 1, 2), 0, JW, held([P, 4, JW], F32, "dd1_1")[:])
         second = [held([P, PIECE, 4], BF16, "habs1_0_0", "v_c1_0"), held([P, PIECE, 4], BF16, "habs1_0_1", "v_c1_1")]
         square_on_scalar(second[0][:], diffs[1, 0, 0][:, :, :PIECE])
-        third = held([P, JW, 4], BF16, "habs0_1", "wp_c1")
+        third = placed([P, JW, 4], BF16, "habs0_1", WP_ORDERED_AT)
         square_on_scalar(third[:], diffs[0, 1, 0])
         square_on_scalar(second[1][:], diffs[1, 0, 0][:, :, PIECE:])
         last = {}
@@ -340,7 +357,7 @@ def tile_list_phase_match_families_kernel(
             last[j0] = held([P, width, 4], BF16, "habs1_1_%d" % j0)
             square_on_scalar(last[j0][:], diffs[1, 1, 0][:, :, j0 : j0 + width])
 
-        signed_first = sign(0, first[:], None)
+        signed_first = sign(0, first, None)
         signed_second = sign(0, second[0][:], placed([P, 8, P], BF16, "hs_second", FIRST_DIFFS_AT))
         quantise_h(0, 0, 0, signed_first)
         for j0, width in halves:
@@ -352,9 +369,12 @@ def tile_list_phase_match_families_kernel(
         quantise_h(0, 1, 0, signed_third)
         for j0, width in halves:
             scores(0, 1, j0, width)
+        signed_last = [sign(1, last[0][:])]
         quantise_h(1, 0, PIECE, signed_rest)
         for j0, width in pieces[1:]:
             scores(1, 0, j0, width)
-        for j0, width in pieces:
-            quantise_h(1, 1, j0, sign(1, last[j0][:]))
+        for number, (j0, width) in enumerate(pieces):
+            if j0 + width < JW:
+                signed_last.append(sign(1, last[j0 + width][:]))
+            quantise_h(1, 1, j0, signed_last[number])
             scores(1, 1, j0, width, nc.vector.tensor_copy if j0 + width == JW else nc.scalar.copy)

@@ -196,23 +196,33 @@ def tile_list_phase_match_families_kernel(
                 moduli[half, blk][:, t, :], sq[:], ACT.Sqrt, bias=gbias[:, col : col + 1], scale=gabs[:, col : col + 1]
             )
 
-        def modulus(half, blk, banks, tiles=range(4)):
+        def modulus(half, blk, banks, tiles=range(4), ahead=0):
             if 0 in tiles:
                 moduli[half, blk] = held([P, 4, JW], F32, "f%d_%d" % (half, blk))
+            accs = {}
+
+            def product(t, kp):
+                if kp == 0:
+                    accs[t] = psum_bank(banks[t])
+                word0 = kp * RB + t * P
+                scale0 = JW + blk * RB + t * P
+                nc.tensor.matmul_mx(
+                    out=accs[t][:],
+                    lhsT=wp_c[blk][:, 2 * word0 : 2 * (word0 + P)].bitcast(FP4X4),
+                    lhsT_scale=plane[:, kp, scale0 : scale0 + P],
+                    rhs=v_c[half, kp][:].bitcast(FP8X4),
+                    rhs_scale=v_s[half][:, kp, :JW],
+                    start=(kp == 0),
+                    stop=(kp == 1),
+                )
+
+            for t in range(ahead):
+                product(t, 0)
             for t in tiles:
-                acc = psum_bank(banks[t])
-                for kp in range(2):
-                    word0 = kp * RB + t * P
-                    scale0 = JW + blk * RB + t * P
-                    nc.tensor.matmul_mx(
-                        out=acc[:],
-                        lhsT=wp_c[blk][:, 2 * word0 : 2 * (word0 + P)].bitcast(FP4X4),
-                        lhsT_scale=plane[:, kp, scale0 : scale0 + P],
-                        rhs=v_c[half, kp][:].bitcast(FP8X4),
-                        rhs_scale=v_s[half][:, kp, :JW],
-                        start=(kp == 0),
-                        stop=(kp == 1),
-                    )
+                if t >= ahead:
+                    product(t, 0)
+                product(t, 1)
+                acc = accs[t]
                 sq = sqp.tile([P, JW], F32, name="sq")
                 nc.scalar.activation(sq[:], acc[:], ACT.Square)
                 if waiting_root:
@@ -296,7 +306,7 @@ def tile_list_phase_match_families_kernel(
                 c0 = half * JW + j0
                 nc.sync.dma_start(out[:, c0 : c0 + width].rearrange("(n p) c -> p n c", n=2), res[:])
 
-        modulus(0, 0, (0, 1, 2, 3))
+        modulus(0, 0, (0, 1, 2, 3), ahead=2)
         gather_v(1, 1, held([P, JW], U32, "v_c1_1"))
         gather_v(1, 0, placed([P, JW], U32, "v_c_late", LATE_PICKS_AT))
         wr_raw[1] = placed([P, 4, RB], F32, "wr_raw1", WR_SECOND_AT)

@@ -29,7 +29,8 @@ WR_SECOND_AT = WP_ORDERED_AT + 4 * RB
 SECOND_PICKS_AT = WR_SECOND_AT - JW // 2
 FIRST_PICKS_END = SECOND_PICKS_AT + 64
 WR_AT = WR_SECOND_AT + 16 * RB
-TAB2_SCALES_AT = WR_AT + 16 * RB
+TAB_SCALES_AT = WR_AT + 16 * RB - T // 2
+TAB2_SCALES_AT = TAB_SCALES_AT + T
 SHARED_AT = TAB2_SCALES_AT + T - 64
 LATE_PICKS_AT = SHARED_AT + 24 * JW
 FIRST_DIFFS_AT = LATE_PICKS_AT + 4 * JW
@@ -58,10 +59,10 @@ def tile_list_phase_match_families_kernel(
 
         lists = keep.tile([P, S // 16], U16, name="lists")
         lists2 = keep.tile([P, S // 16], U16, name="lists2")
-        g_raw = keep.tile([P, 2, 4], F32, name="g_raw")
-        ts_raw = placed([P, T], U8, "ts_raw", TAB2_SCALES_AT - T // 2)
+        g_raw = placed([P, 2, 4], F32, "g_raw", FIRST_PICKS_END)
+        ts_raw = placed([P, T], U8, "ts_raw", TAB_SCALES_AT)
         wps_raw = held([P, H], U8, "wps_raw")
-        tw = [held([P, T], I32, "tw%d" % kp) for kp in range(2)]
+        tw = [held([P, T], I32, "tw0"), placed([P, T], I32, "tw1", TAB2_SCALES_AT)]
 
         nc.vector.memset(ts_raw[:, :VECTOR_CLEARS].bitcast(I32), 0)
         nc.gpsimd.memset(ts_raw[:, VECTOR_CLEARS:].bitcast(I32), 0)
@@ -81,12 +82,13 @@ def tile_list_phase_match_families_kernel(
         wp_raw0 = held([P, RB], I32, "wp_raw0")
         nc.sync.dma_start(lists[:], offs)
         load_wp(0, wp_raw0)
-        nc.sync.dma_start(g_raw[:], gain.rearrange("(blk p t) -> p blk t", blk=2, t=4))
         nc.sync.dma_start(lists2[:], offs2)
         nc.sync.dma_start(ts_raw[0:P:4, :].bitcast(I32), tab_scales.rearrange("kp q c -> q kp c").bitcast(I32))
         nc.sync.dma_start(wps_raw[0:P:4, :].bitcast(I32), wp_scales.rearrange("kp q c -> q kp c").bitcast(I32))
         for kp in range(2):
             nc.sync.dma_start(tw[kp][:], tab_words[kp].rearrange("p c i -> p (c i)").bitcast(I32))
+            if kp == 0:
+                nc.sync.dma_start(g_raw[:], gain.rearrange("(blk p t) -> p blk t", blk=2, t=4))
 
         def gather_bytes(half, picks):
             nc.vector.tensor_copy(picks, ts_raw[:].indirect(lists[:, half * JW // 16 : (half + 1) * JW // 16]))
@@ -114,10 +116,11 @@ def tile_list_phase_match_families_kernel(
         groot = keep.tile([P, 8], F32, name="groot")
         gbias = keep.tile([P, 8], F32, name="gbias")
         nc.scalar.activation(gabs[:], gains, ACT.Abs)
-        nc.scalar.activation(groot[:], gabs[:], ACT.Sqrt)
-        nc.scalar.activation(gbias[:], gabs[:], ACT.Copy, scale=0.1)
         signs = held([P, 2, P // 4, 4], BF16, "signs")
         nc.scalar.activation(signs[:], g_raw[:].unsqueeze(2).to_broadcast([P, 2, P // 4, 4]), ACT.Sign)
+
+        nc.scalar.activation(groot[:], gabs[:], ACT.Sqrt)
+        nc.scalar.activation(gbias[:], gabs[:], ACT.Copy, scale=0.1)
 
         wp_c = {0: held([P, 2 * 2 * RB], U8, "wp_c0")}
 
@@ -149,13 +152,6 @@ def tile_list_phase_match_families_kernel(
         v_s = (plane, late_plane)
         wr_raw = {0: placed([P, 4, RB], F32, "wr_raw0", WR_AT)}
         load_wr(0)
-        t2s_raw = placed([P, T], U8, "t2s_raw", TAB2_SCALES_AT)
-        nc.gpsimd.memset(t2s_raw[:].bitcast(I32), 0)
-        for quad in range(4):
-            nc.sync.dma_start(
-                t2s_raw[32 * quad : 32 * quad + 4, :].bitcast(I32),
-                tab2_scales[0, 4 * quad : 4 * quad + 4, :].bitcast(I32),
-            )
 
         v2_c = {}
         v2_s = {}
@@ -308,8 +304,15 @@ def tile_list_phase_match_families_kernel(
 
         modulus(0, 0, (0, 1, 2, 3), ahead=2)
         gather_v(1, 1, held([P, JW], U32, "v_c1_1"))
+        t2s_raw = placed([P, T], U8, "t2s_raw", TAB2_SCALES_AT)
+        nc.gpsimd.memset(t2s_raw[:].bitcast(I32), 0)
+        for quad in range(4):
+            nc.sync.dma_start(
+                t2s_raw[32 * quad : 32 * quad + 4, :].bitcast(I32),
+                tab2_scales[0, 4 * quad : 4 * quad + 4, :].bitcast(I32),
+            )
         gather_v(1, 0, placed([P, JW], U32, "v_c_late", LATE_PICKS_AT))
-        wr_raw[1] = placed([P, 4, RB], F32, "wr_raw1", WR_SECOND_AT)
+        wr_raw[1] = held([P, 4, RB], F32, "wr_raw1", "tw0")
         load_wr(1)
         modulus(1, 0, (4, 5, 6, 7))
         picks2 = held([P, S], U32, "v2_c")

@@ -45,7 +45,7 @@ def tile_list_phase_match_families_kernel(
         keep = ctx.enter_context(tc.tile_pool(name="keep", bufs=1))
         reuse = ctx.enter_context(tc.tile_pool(name="reuse", bufs=1))
         sqp = ctx.enter_context(tc.tile_pool(name="sqp", bufs=3))
-        stage = ctx.enter_context(tc.tile_pool(name="stage", bufs=5))
+        stage = ctx.enter_context(tc.tile_pool(name="stage", bufs=2))
         psr = ctx.enter_context(tc.psum_pool(name="psr", bufs=1))
 
         def held(shape, dtype, name, buffer=None):
@@ -281,7 +281,7 @@ def tile_list_phase_match_families_kernel(
 
         def scores(half, blk, j0, width, copy=nc.scalar.copy):
             if blk == 0:
-                sums[half, j0] = psum_bank((4, 5, 6, 3, 7)[len(sums)])[:, : 2 * width].rearrange("p (n c) -> p n c", n=2)
+                sums[half, j0] = psum_bank(6 if j0 == 0 else 3)[:, : 2 * width].rearrange("p (n c) -> p n c", n=2)
             acc = sums[half, j0]
             h_c, h_s, h_first = fields[half, blk]
             entries = slice(j0 - h_first, j0 - h_first + width)
@@ -301,6 +301,28 @@ def tile_list_phase_match_families_kernel(
                 copy(res[:], acc)
                 c0 = half * JW + j0
                 nc.sync.dma_start(out[:, c0 : c0 + width].rearrange("(n p) c -> p n c", n=2), res[:])
+
+        def row_scores(half, j0, width, banks, blk, copies=None, queues=None):
+            h_c, h_s, h_first = fields[half, blk]
+            entries = slice(j0 - h_first, j0 - h_first + width)
+            for n in range(2):
+                if blk == 0:
+                    sums[half, j0, n] = psum_bank(banks[n])[:, :width]
+                columns = slice(blk * N + n * P, blk * N + (n + 1) * P)
+                nc.tensor.matmul_mx(
+                    out=sums[half, j0, n],
+                    lhsT=wf_c[:, columns].bitcast(FP8X4),
+                    lhsT_scale=wf_s.bitcast(U8)[:, columns],
+                    rhs=h_c[:, entries].bitcast(FP8X4),
+                    rhs_scale=h_s[:, entries],
+                    start=blk == 0,
+                    stop=blk == 1,
+                )
+                if blk == 1:
+                    res = held([P, width], F32, "res%d_%d" % (half, n))
+                    copies[n](res[:], sums[half, j0, n])
+                    c0 = half * JW + j0
+                    queues[n].dma_start(out[n * P : (n + 1) * P, c0 : c0 + width], res[:])
 
         modulus(0, 0, (0, 1, 2, 3), ahead=2)
         gather_v(1, 1, held([P, JW], U32, "v_c1_1"))
@@ -355,7 +377,6 @@ def tile_list_phase_match_families_kernel(
         take_root()
         residual(0, 1, (7, 0, 1, 2), 0, JW, held([P, 4, JW], F32, "dd0_1")[:])
 
-        halves = ((0, PIECE), (PIECE, PIECE))
         pieces = ((0, PIECE), (PIECE, PIECE // 2), (PIECE + PIECE // 2, PIECE // 2))
         first = shared[:, 4 * JW :].bitcast(BF16).rearrange("p (j t) -> p j t", t=4)
         square_on_gpsimd(first, diffs[0, 0, 0])
@@ -373,21 +394,27 @@ def tile_list_phase_match_families_kernel(
         signed_first = sign(0, first, None)
         signed_second = sign(0, second[0][:], placed([P, 8, P], BF16, "hs_second", FIRST_DIFFS_AT))
         quantise_h(0, 0, 0, signed_first)
-        for j0, width in halves:
-            scores(0, 0, j0, width)
+        row_scores(0, 0, JW, (4, 5), 0)
         quantise_h(1, 0, 0, signed_second)
         scores(1, 0, 0, PIECE)
         signed_third = sign(1, third[:], placed([P, 16, P], BF16, "hs_third", FIRST_DIFFS_AT + 8 * JW))
         signed_rest = sign(0, second[1][:], placed([P, 8, P], BF16, "hs_rest", FIRST_DIFFS_AT + 8 * PIECE))
         quantise_h(0, 1, 0, signed_third)
-        for j0, width in halves:
-            scores(0, 1, j0, width)
+        row_scores(0, 0, JW, (4, 5), 1, (nc.scalar.copy, nc.scalar.copy), (nc.sync, nc.sync))
         signed_last = [sign(1, last[0][:])]
         quantise_h(1, 0, PIECE, signed_rest)
-        for j0, width in pieces[1:]:
-            scores(1, 0, j0, width)
+        scores(1, 0, *pieces[1])
+        row_scores(1, *pieces[2], (7, 0), 0)
         for number, (j0, width) in enumerate(pieces):
             if j0 + width < JW:
                 signed_last.append(sign(1, last[j0 + width][:]))
             quantise_h(1, 1, j0, signed_last[number])
-            scores(1, 1, j0, width, nc.vector.tensor_copy if j0 + width == JW else nc.scalar.copy)
+            if number == 0:
+                scores(1, 1, j0, width)
+            elif number == 1:
+                waiting = fields[1, 1]
+        newest = fields[1, 1]
+        fields[1, 1] = waiting
+        scores(1, 1, *pieces[1], nc.vector.tensor_copy)
+        fields[1, 1] = newest
+        row_scores(1, *pieces[2], (7, 0), 1, (nc.vector.tensor_copy, nc.scalar.copy), (nc.sync, nc.scalar))

@@ -182,6 +182,7 @@ def tile_list_phase_match_families_kernel(
         diffs = {}
         fields = {}
         sums = {}
+        results = []
         waiting_root = []
         signed_tiles = []
 
@@ -281,7 +282,7 @@ def tile_list_phase_match_families_kernel(
 
         def scores(half, blk, j0, width, copy=nc.scalar.copy):
             if blk == 0:
-                sums[half, j0] = psum_bank(6 if j0 == 0 else 3)[:, : 2 * width].rearrange("p (n c) -> p n c", n=2)
+                sums[half, j0] = psum_bank({0: 6, PIECE: 3}.get(j0, 7))[:, : 2 * width].rearrange("p (n c) -> p n c", n=2)
             acc = sums[half, j0]
             h_c, h_s, h_first = fields[half, blk]
             entries = slice(j0 - h_first, j0 - h_first + width)
@@ -297,10 +298,12 @@ def tile_list_phase_match_families_kernel(
                     stop=(blk, n) == (1, 1),
                 )
             if blk == 1:
-                res = stage.tile([P, 2, width], F32, name="res")
-                copy(res[:], acc)
-                c0 = half * JW + j0
-                nc.sync.dma_start(out[:, c0 : c0 + width].rearrange("(n p) c -> p n c", n=2), res[:])
+                if j0 % PIECE == 0:
+                    results.append(stage.tile([P, 2, PIECE], F32, name="res"))
+                copy(results[-1][:, :, j0 % PIECE : j0 % PIECE + width], acc)
+                if (j0 + width) % PIECE == 0:
+                    c0 = half * JW + j0 + width - PIECE
+                    nc.sync.dma_start(out[:, c0 : c0 + PIECE].rearrange("(n p) c -> p n c", n=2), results[-1][:])
 
         def row_scores(half, j0, width, banks, blk, copies=None, queues=None):
             h_c, h_s, h_first = fields[half, blk]
@@ -403,18 +406,10 @@ def tile_list_phase_match_families_kernel(
         row_scores(0, 0, JW, (4, 5), 1, (nc.scalar.copy, nc.scalar.copy), (nc.sync, nc.sync))
         signed_last = [sign(1, last[0][:])]
         quantise_h(1, 0, PIECE, signed_rest)
-        scores(1, 0, *pieces[1])
-        row_scores(1, *pieces[2], (7, 0), 0)
+        for j0, width in pieces[1:]:
+            scores(1, 0, j0, width)
         for number, (j0, width) in enumerate(pieces):
             if j0 + width < JW:
                 signed_last.append(sign(1, last[j0 + width][:]))
             quantise_h(1, 1, j0, signed_last[number])
-            if number == 0:
-                scores(1, 1, j0, width)
-            elif number == 1:
-                waiting = fields[1, 1]
-        newest = fields[1, 1]
-        fields[1, 1] = waiting
-        scores(1, 1, *pieces[1], nc.vector.tensor_copy)
-        fields[1, 1] = newest
-        row_scores(1, *pieces[2], (7, 0), 1, (nc.vector.tensor_copy, nc.scalar.copy), (nc.sync, nc.scalar))
+            scores(1, 1, j0, width, nc.vector.tensor_copy if j0 + width == JW else nc.scalar.copy)

@@ -45,7 +45,7 @@ def tile_list_phase_match_families_kernel(
         keep = ctx.enter_context(tc.tile_pool(name="keep", bufs=1))
         reuse = ctx.enter_context(tc.tile_pool(name="reuse", bufs=1))
         sqp = ctx.enter_context(tc.tile_pool(name="sqp", bufs=3))
-        stage = ctx.enter_context(tc.tile_pool(name="stage", bufs=2))
+        stage = ctx.enter_context(tc.tile_pool(name="stage", bufs=4))
         psr = ctx.enter_context(tc.psum_pool(name="psr", bufs=1))
 
         def held(shape, dtype, name, buffer=None):
@@ -282,7 +282,7 @@ def tile_list_phase_match_families_kernel(
 
         def scores(half, blk, j0, width, copy=nc.scalar.copy):
             if blk == 0:
-                sums[half, j0] = psum_bank({0: 6, PIECE: 3}.get(j0, 7))[:, : 2 * width].rearrange("p (n c) -> p n c", n=2)
+                sums[half, j0] = psum_bank((4, 5, 6, 3, 7)[len(sums)])[:, : 2 * width].rearrange("p (n c) -> p n c", n=2)
             acc = sums[half, j0]
             h_c, h_s, h_first = fields[half, blk]
             entries = slice(j0 - h_first, j0 - h_first + width)
@@ -386,24 +386,32 @@ def tile_list_phase_match_families_kernel(
         residual(1, 1, (7, 0, 1, 2), 0, JW, held([P, 4, JW], F32, "dd1_1")[:])
         second = [held([P, PIECE, 4], BF16, "habs1_0_0", "v_c1_0"), held([P, PIECE, 4], BF16, "habs1_0_1", "v_c1_1")]
         square_on_scalar(second[0][:], diffs[1, 0, 0][:, :, :PIECE])
-        third = placed([P, JW, 4], BF16, "habs0_1", WP_ORDERED_AT)
-        square_on_scalar(third[:], diffs[0, 1, 0])
+        third = [placed([P, PIECE, 4], BF16, "habs0_1_%d" % u, WP_ORDERED_AT + 8 * PIECE * u) for u in range(2)]
+        for u in range(2):
+            square_on_scalar(third[u][:], diffs[0, 1, 0][:, :, u * PIECE : (u + 1) * PIECE])
         square_on_scalar(second[1][:], diffs[1, 0, 0][:, :, PIECE:])
-        last = {}
-        for j0, width in pieces:
-            last[j0] = held([P, width, 4], BF16, "habs1_1_%d" % j0)
-            square_on_scalar(last[j0][:], diffs[1, 1, 0][:, :, j0 : j0 + width])
 
         signed_first = sign(0, first, None)
         signed_second = sign(0, second[0][:], placed([P, 8, P], BF16, "hs_second", FIRST_DIFFS_AT))
         quantise_h(0, 0, 0, signed_first)
-        row_scores(0, 0, JW, (4, 5), 0)
+        for u in range(2):
+            scores(0, 0, u * PIECE, PIECE)
+        signed_third = [
+            placed([P, 8, P], BF16, "hs_third%d" % u, FIRST_DIFFS_AT + 8 * JW + 8 * PIECE * u) for u in range(2)
+        ]
+        sign(1, third[0][:], signed_third[0])
         quantise_h(1, 0, 0, signed_second)
         scores(1, 0, 0, PIECE)
-        signed_third = sign(1, third[:], placed([P, 16, P], BF16, "hs_third", FIRST_DIFFS_AT + 8 * JW))
+        sign(1, third[1][:], signed_third[1])
+        quantise_h(0, 1, 0, signed_third[0])
+        scores(0, 1, 0, PIECE)
         signed_rest = sign(0, second[1][:], placed([P, 8, P], BF16, "hs_rest", FIRST_DIFFS_AT + 8 * PIECE))
-        quantise_h(0, 1, 0, signed_third)
-        row_scores(0, 0, JW, (4, 5), 1, (nc.scalar.copy, nc.scalar.copy), (nc.sync, nc.sync))
+        quantise_h(0, 1, PIECE, signed_third[1])
+        scores(0, 1, PIECE, PIECE)
+        last = {}
+        for j0, width in pieces:
+            last[j0] = held([P, width, 4], BF16, "habs1_1_%d" % j0)
+            square_on_scalar(last[j0][:], diffs[1, 1, 0][:, :, j0 : j0 + width])
         signed_last = [sign(1, last[0][:])]
         quantise_h(1, 0, PIECE, signed_rest)
         for j0, width in pieces[1:]:

@@ -45,7 +45,6 @@ def tile_list_phase_match_families_kernel(
         keep = ctx.enter_context(tc.tile_pool(name="keep", bufs=1))
         reuse = ctx.enter_context(tc.tile_pool(name="reuse", bufs=1))
         sqp = ctx.enter_context(tc.tile_pool(name="sqp", bufs=3))
-        stage = ctx.enter_context(tc.tile_pool(name="stage", bufs=4))
         psr = ctx.enter_context(tc.psum_pool(name="psr", bufs=1))
 
         def held(shape, dtype, name, buffer=None):
@@ -298,12 +297,13 @@ def tile_list_phase_match_families_kernel(
                     stop=(blk, n) == (1, 1),
                 )
             if blk == 1:
-                if j0 % PIECE == 0:
-                    results.append(stage.tile([P, 2, PIECE], F32, name="res"))
-                copy(results[-1][:, :, j0 % PIECE : j0 % PIECE + width], acc)
-                if (j0 + width) % PIECE == 0:
-                    c0 = half * JW + j0 + width - PIECE
-                    nc.sync.dma_start(out[:, c0 : c0 + PIECE].rearrange("(n p) c -> p n c", n=2), results[-1][:])
+                stored = (PIECE, JW)[half]
+                if j0 % stored == 0:
+                    results.append(held([P, 2, stored], F32, "res%d" % len(results)))
+                copy(results[-1][:, :, j0 % stored : j0 % stored + width], acc)
+                if (j0 + width) % stored == 0:
+                    c0 = half * JW + j0 + width - stored
+                    nc.sync.dma_start(out[:, c0 : c0 + stored].rearrange("(n p) c -> p n c", n=2), results[-1][:])
 
         def row_scores(half, j0, width, banks, blk, copies=None, queues=None):
             h_c, h_s, h_first = fields[half, blk]

@@ -22,6 +22,8 @@ RB = 512
 PIECE = 256
 VECTOR_CLEARS = T // 4
 
+GPSIMD_SQUARES = 7 * JW // 8
+
 TAB2_WORDS_AT = 0
 WP_SECOND_AT = TAB2_WORDS_AT + 4 * T
 WP_ORDERED_AT = WP_SECOND_AT + 4 * RB
@@ -382,7 +384,8 @@ def tile_list_phase_match_families_kernel(
 
         pieces = ((0, PIECE), (PIECE, PIECE // 2), (PIECE + PIECE // 2, PIECE // 2))
         first = shared[:, 4 * JW :].bitcast(BF16).rearrange("p (j t) -> p j t", t=4)
-        square_on_gpsimd(first, diffs[0, 0, 0])
+        square_on_gpsimd(first[:, :GPSIMD_SQUARES, :], diffs[0, 0, 0][:, :, :GPSIMD_SQUARES])
+        square_on_scalar(first[:, GPSIMD_SQUARES:, :], diffs[0, 0, 0][:, :, GPSIMD_SQUARES:])
         residual(1, 1, (7, 0, 1, 2), 0, JW, held([P, 4, JW], F32, "dd1_1")[:])
         second = [held([P, PIECE, 4], BF16, "habs1_0_0", "v_c1_0"), held([P, PIECE, 4], BF16, "habs1_0_1", "v_c1_1")]
         square_on_scalar(second[0][:], diffs[1, 0, 0][:, :, :PIECE])

@@ -305,7 +305,11 @@ def tile_list_phase_match_families_kernel(
                 copy(results[-1][:, :, j0 % stored : j0 % stored + width], acc)
                 if (j0 + width) % stored == 0:
                     c0 = half * JW + j0 + width - stored
-                    nc.sync.dma_start(out[:, c0 : c0 + stored].rearrange("(n p) c -> p n c", n=2), results[-1][:])
+                    if half == 0:
+                        nc.sync.dma_start(out[:, c0 : c0 + stored].rearrange("(n p) c -> p n c", n=2), results[-1][:])
+                    else:
+                        for n, queue in enumerate((nc.sync, nc.scalar)):
+                            queue.dma_start(out[n * P : (n + 1) * P, c0 : c0 + stored], results[-1][:, n, :])
 
         def row_scores(half, j0, width, banks, blk, copies=None, queues=None):
             h_c, h_s, h_first = fields[half, blk]

@@ -24,18 +24,15 @@ VECTOR_CLEARS = T // 4
 
 GPSIMD_SQUARES = 7 * JW // 8
 
-TAB2_WORDS_AT = 0
-WP_SECOND_AT = TAB2_WORDS_AT + 4 * T
-WP_ORDERED_AT = WP_SECOND_AT + 4 * RB
-WR_SECOND_AT = WP_ORDERED_AT + 4 * RB
-SECOND_PICKS_AT = WR_SECOND_AT - JW // 2
-FIRST_PICKS_END = SECOND_PICKS_AT + 64
-WR_AT = WR_SECOND_AT + 16 * RB
-TAB_SCALES_AT = WR_AT + 16 * RB - T // 2
-TAB2_SCALES_AT = TAB_SCALES_AT + T
-SHARED_AT = TAB2_SCALES_AT + T - 64
-LATE_PICKS_AT = SHARED_AT + 24 * JW
-FIRST_DIFFS_AT = LATE_PICKS_AT + 4 * JW
+WR_AT = 0
+SECOND_PICKS_AT = WR_AT + 16 * RB
+TAB2_WORDS_AT = SECOND_PICKS_AT + JW
+FIRST_PICKS_AT = TAB2_WORDS_AT - 64
+SHARED_AT = TAB2_WORDS_AT + 4 * T - 64
+STAGED_AT = SHARED_AT + 40 * JW
+WR_SECOND_AT = STAGED_AT + S + 4 * JW
+FIRST_DIFFS_AT = WR_SECOND_AT + 16 * RB
+WP_ORDERED_AT = FIRST_DIFFS_AT + 16 * JW
 
 
 def tile_list_phase_match_families_kernel(
@@ -60,36 +57,35 @@ def tile_list_phase_match_families_kernel(
 
         lists = keep.tile([P, S // 16], U16, name="lists")
         lists2 = keep.tile([P, S // 16], U16, name="lists2")
-        g_raw = placed([P, 2, 4], F32, "g_raw", FIRST_PICKS_END)
-        ts_raw = placed([P, T], U8, "ts_raw", TAB_SCALES_AT)
+        g_raw = held([P, 2, 4], F32, "g_raw")
+        ts_raw = placed([P, T], U8, "ts_raw", WR_AT)
+        t2s_raw = placed([P, T], U8, "t2s_raw", WR_SECOND_AT)
         wps_raw = held([P, H], U8, "wps_raw")
-        tw = [held([P, T], I32, "tw0"), placed([P, T], I32, "tw1", TAB2_SCALES_AT)]
+        wp_raw = held([P, 2, RB], I32, "wp_raw")
+        tw = [held([P, T], I32, "tw%d" % kp) for kp in range(2)]
 
         nc.vector.memset(ts_raw[:, :VECTOR_CLEARS].bitcast(I32), 0)
         nc.gpsimd.memset(ts_raw[:, VECTOR_CLEARS:].bitcast(I32), 0)
         nc.vector.memset(wps_raw[:].bitcast(I32), 0)
-
-        def load_wp(blk, raw):
-            nc.sync.dma_start(
-                raw[:].rearrange("p (kp c) -> p kp c", kp=2),
-                wp_words[:, :, 2 * RB * blk : 2 * RB * (blk + 1)].rearrange("kp p c -> p kp c").bitcast(I32),
-            )
+        nc.gpsimd.memset(t2s_raw[:].bitcast(I32), 0)
 
         def load_wr(blk):
             nc.sync.dma_start(
                 wr_raw[blk][:], wr[:, RB * blk : RB * (blk + 1)].rearrange("(p i) c -> p i c", i=4)
             )
 
-        wp_raw0 = held([P, RB], I32, "wp_raw0")
+        def load_table(kp):
+            nc.sync.dma_start(tw[kp][:], tab_words[kp].rearrange("p c i -> p (c i)").bitcast(I32))
+
         nc.sync.dma_start(lists[:], offs)
-        load_wp(0, wp_raw0)
         nc.sync.dma_start(lists2[:], offs2)
+        nc.sync.dma_start(g_raw[:], gain.rearrange("(blk p t) -> p blk t", blk=2, t=4))
         nc.sync.dma_start(ts_raw[0:P:4, :].bitcast(I32), tab_scales.rearrange("kp q c -> q kp c").bitcast(I32))
         nc.sync.dma_start(wps_raw[0:P:4, :].bitcast(I32), wp_scales.rearrange("kp q c -> q kp c").bitcast(I32))
-        for kp in range(2):
-            nc.sync.dma_start(tw[kp][:], tab_words[kp].rearrange("p c i -> p (c i)").bitcast(I32))
-            if kp == 0:
-                nc.sync.dma_start(g_raw[:], gain.rearrange("(blk p t) -> p blk t", blk=2, t=4))
+        nc.sync.dma_start(wp_raw[:], wp_words.rearrange("kp p c -> p kp c").bitcast(I32))
+        load_table(0)
+        nc.sync.dma_start(t2s_raw[0:P:8, :].bitcast(I32), tab2_scales[0].bitcast(I32))
+        load_table(1)
 
         def gather_bytes(half, picks):
             nc.vector.tensor_copy(picks, ts_raw[:].indirect(lists[:, half * JW // 16 : (half + 1) * JW // 16]))
@@ -101,8 +97,8 @@ def tile_list_phase_match_families_kernel(
                     rows[32 * quad : 32 * quad + 32 : 4, :].bitcast(I32),
                 )
 
-        first_got = placed([P, FIRST_PICKS_END], U8, "first_got", 0)[:, :JW]
-        staged = placed([P, JW + H], U8, "staged", LATE_PICKS_AT)
+        first_got = placed([P, JW], U8, "first_got", FIRST_PICKS_AT)[:]
+        staged = placed([P, JW + H], U8, "staged", STAGED_AT)
         plane = held([P, 2, JW + H], U8, "plane")
         gather_bytes(0, first_got)
         nc.vector.tensor_copy(
@@ -123,31 +119,30 @@ def tile_list_phase_match_families_kernel(
         nc.scalar.activation(groot[:], gabs[:], ACT.Sqrt)
         nc.scalar.activation(gbias[:], gabs[:], ACT.Copy, scale=0.1)
 
-        wp_c = {0: held([P, 2 * 2 * RB], U8, "wp_c0")}
-
-        def order_wp(blk, raw):
-            nc.vector.tensor_copy(
+        wp_c = [held([P, 2 * 2 * RB], U8, "wp_c0"), placed([P, 2 * 2 * RB], U8, "wp_c1", WP_ORDERED_AT)]
+        for blk in range(2):
+            nc.scalar.copy(
                 wp_c[blk][:].bitcast(U16).rearrange("p (kp t c) -> p kp t c", kp=2, t=4),
-                raw[:].bitcast(U16).rearrange("p (kp c t) -> p kp t c", kp=2, t=4),
+                wp_raw[:].bitcast(U16)[:, :, blk * RB : (blk + 1) * RB].rearrange("p kp (c t) -> p kp t c", t=4),
             )
 
         v_c = {}
 
-        def gather_v(half, kp, picks):
-            v_c[half, kp] = picks
-            entries = lists[:, half * JW // 16 : (half + 1) * JW // 16]
-            nc.vector.tensor_copy(picks[:], tw[kp][:].bitcast(U32).indirect(entries))
+        def gather_words(picks, words, offsets, j0):
+            width = picks.shape[1]
+            nc.vector.tensor_copy(picks, words[:].bitcast(U32).indirect(offsets[:, j0 // 16 : (j0 + width) // 16]))
 
-        order_wp(0, wp_raw0)
-        gather_v(0, 0, held([P, JW], U32, "v_c0_0"))
         second_got = placed([P, JW], U8, "second_got", SECOND_PICKS_AT)
         gather_bytes(1, second_got[:])
-        gather_v(0, 1, held([P, JW], U32, "v_c1_0"))
+        for half in range(2):
+            v_c[half, 0] = held([P, JW], U32, "v_c0_%d" % half)
+            gather_words(v_c[half, 0][:], tw[0], lists, half * JW)
+        v_c[0, 1] = held([P, JW], U32, "v_c1_0")
+        for j0 in (0, PIECE):
+            gather_words(v_c[0, 1][:, j0 : j0 + PIECE], tw[1], lists, j0)
 
         t2w = placed([P, T], I32, "t2w", TAB2_WORDS_AT)
         nc.sync.dma_start(t2w[:], tab2_words[0].rearrange("p c i -> p (c i)").bitcast(I32))
-        wp_raw1 = placed([P, RB], I32, "wp_raw1", WP_SECOND_AT)
-        load_wp(1, wp_raw1)
         late_plane = held([P, 2, JW], U8, "late_plane")
         move_rows(late_plane, second_got)
         v_s = (plane, late_plane)
@@ -155,7 +150,6 @@ def tile_list_phase_match_families_kernel(
         load_wr(0)
 
         v2_c = {}
-        v2_s = {}
 
         wr_g = {}
         wr_c = {}
@@ -188,28 +182,30 @@ def tile_list_phase_match_families_kernel(
         signed_tiles = []
 
         def take_root():
-            half, blk, t, sq = waiting_root.pop()
+            half, blk, t, entries, sq = waiting_root.pop()
             col = 4 * blk + t
             nc.scalar.activation(
-                moduli[half, blk][:, t, :], sq[:], ACT.Sqrt, bias=gbias[:, col : col + 1], scale=gabs[:, col : col + 1]
+                moduli[half, blk][:, t, entries], sq, ACT.Sqrt,
+                bias=gbias[:, col : col + 1], scale=gabs[:, col : col + 1],
             )
 
-        def modulus(half, blk, banks, tiles=range(4), ahead=0):
-            if 0 in tiles:
+        def modulus(half, blk, banks, tiles=range(4), ahead=0, j0=0, width=JW):
+            if (half, blk) not in moduli:
                 moduli[half, blk] = held([P, 4, JW], F32, "f%d_%d" % (half, blk))
             accs = {}
+            entries = slice(j0, j0 + width)
 
             def product(t, kp):
                 if kp == 0:
-                    accs[t] = psum_bank(banks[t])
+                    accs[t] = psum_bank(banks[t])[:, :width]
                 word0 = kp * RB + t * P
                 scale0 = JW + blk * RB + t * P
                 nc.tensor.matmul_mx(
-                    out=accs[t][:],
+                    out=accs[t],
                     lhsT=wp_c[blk][:, 2 * word0 : 2 * (word0 + P)].bitcast(FP4X4),
                     lhsT_scale=plane[:, kp, scale0 : scale0 + P],
-                    rhs=v_c[half, kp][:].bitcast(FP8X4),
-                    rhs_scale=v_s[half][:, kp, :JW],
+                    rhs=v_c[half, kp][:, entries].bitcast(FP8X4),
+                    rhs_scale=v_s[half][:, kp, entries],
                     start=(kp == 0),
                     stop=(kp == 1),
                 )
@@ -220,12 +216,11 @@ def tile_list_phase_match_families_kernel(
                 if t >= ahead:
                     product(t, 0)
                 product(t, 1)
-                acc = accs[t]
-                sq = sqp.tile([P, JW], F32, name="sq")
-                nc.scalar.activation(sq[:], acc[:], ACT.Square)
+                sq = sqp.tile([P, JW], F32, name="sq")[:, :width]
+                nc.scalar.activation(sq, accs[t], ACT.Square)
                 if waiting_root:
                     take_root()
-                waiting_root.append((half, blk, t, sq))
+                waiting_root.append((half, blk, t, entries, sq))
 
         def residual(half, blk, banks, j0, width, tile, steps=range(4)):
             diffs[half, blk, j0] = tile
@@ -240,7 +235,7 @@ def tile_list_phase_match_families_kernel(
                         lhsT=wr_c[blk][:, t * P : (t + 1) * P].bitcast(FP8X4),
                         lhsT_scale=wr_s[blk][:, t * P : (t + 1) * P],
                         rhs=v2_c[half][:, entries].bitcast(FP8X4),
-                        rhs_scale=v2_s[half][:, entries],
+                        rhs_scale=v2_s[:, half * JW + j0 : half * JW + j0 + width],
                         start=True,
                         stop=True,
                     )
@@ -283,7 +278,7 @@ def tile_list_phase_match_families_kernel(
 
         def scores(half, blk, j0, width, copy=nc.scalar.copy):
             if blk == 0:
-                sums[half, j0] = psum_bank((4, 5, 6, 3, 7)[len(sums)])[:, : 2 * width].rearrange("p (n c) -> p n c", n=2)
+                sums[half, j0] = psum_bank((6, 7, 2, 3, 4)[len(sums)])[:, : 2 * width].rearrange("p (n c) -> p n c", n=2)
             acc = sums[half, j0]
             h_c, h_s, h_first = fields[half, blk]
             entries = slice(j0 - h_first, j0 - h_first + width)
@@ -311,57 +306,28 @@ def tile_list_phase_match_families_kernel(
                         for n, queue in enumerate((nc.sync, nc.scalar)):
                             queue.dma_start(out[n * P : (n + 1) * P, c0 : c0 + stored], results[-1][:, n, :])
 
-        def row_scores(half, j0, width, banks, blk, copies=None, queues=None):
-            h_c, h_s, h_first = fields[half, blk]
-            entries = slice(j0 - h_first, j0 - h_first + width)
-            for n in range(2):
-                if blk == 0:
-                    sums[half, j0, n] = psum_bank(banks[n])[:, :width]
-                columns = slice(blk * N + n * P, blk * N + (n + 1) * P)
-                nc.tensor.matmul_mx(
-                    out=sums[half, j0, n],
-                    lhsT=wf_c[:, columns].bitcast(FP8X4),
-                    lhsT_scale=wf_s.bitcast(U8)[:, columns],
-                    rhs=h_c[:, entries].bitcast(FP8X4),
-                    rhs_scale=h_s[:, entries],
-                    start=blk == 0,
-                    stop=blk == 1,
-                )
-                if blk == 1:
-                    res = held([P, width], F32, "res%d_%d" % (half, n))
-                    copies[n](res[:], sums[half, j0, n])
-                    c0 = half * JW + j0
-                    queues[n].dma_start(out[n * P : (n + 1) * P, c0 : c0 + width], res[:])
-
-        modulus(0, 0, (0, 1, 2, 3), ahead=2)
-        gather_v(1, 1, held([P, JW], U32, "v_c1_1"))
-        t2s_raw = placed([P, T], U8, "t2s_raw", TAB2_SCALES_AT)
-        nc.gpsimd.memset(t2s_raw[:].bitcast(I32), 0)
-        for quad in range(4):
+        modulus(0, 0, (0, 1, 2, 3), ahead=2, width=PIECE)
+        modulus(0, 0, (4, 5, 6, 7), j0=PIECE, width=PIECE)
+        t2_got = placed([P, S], U8, "t2_got", STAGED_AT)
+        nc.vector.tensor_copy(t2_got[:], t2s_raw[:].indirect(lists2[:]))
+        v_c[1, 1] = placed([P, JW], U32, "v_c1_1", STAGED_AT + S)
+        gather_words(v_c[1, 1][:], tw[1], lists, JW)
+        v2_s = held([P, S], U8, "v2_s")
+        for quad in (0, 2, 1, 3):
             nc.sync.dma_start(
-                t2s_raw[32 * quad : 32 * quad + 4, :].bitcast(I32),
-                tab2_scales[0, 4 * quad : 4 * quad + 4, :].bitcast(I32),
+                v2_s[32 * quad : 32 * quad + 4, :].bitcast(I32), t2_got[32 * quad : 32 * quad + 32 : 8, :].bitcast(I32)
             )
-        gather_v(1, 0, placed([P, JW], U32, "v_c_late", LATE_PICKS_AT))
-        wr_raw[1] = held([P, 4, RB], F32, "wr_raw1", "tw0")
+        wr_raw[1] = placed([P, 4, RB], F32, "wr_raw1", WR_SECOND_AT)
         load_wr(1)
-        modulus(1, 0, (4, 5, 6, 7))
-        picks2 = held([P, S], U32, "v2_c")
-        nc.vector.tensor_copy(picks2[:], t2w[:].bitcast(U32).indirect(lists2[:]))
-        wp_c[1] = placed([P, 2 * 2 * RB], U8, "wp_c1", WP_ORDERED_AT)
-        order_wp(1, wp_raw1)
+        modulus(1, 0, (0, 1, 2, 3))
+        v2_c[0] = held([P, JW], U32, "v2_c0")
+        gather_words(v2_c[0][:], t2w, lists2, 0)
         round_wr(0, held([P, 4 * RB], BF16, "wr_g0")[:], False)
-
-        def gather_bytes2(half):
-            v2_c[half] = picks2[:, half * JW : (half + 1) * JW]
-            v2_s[half] = held([P, JW], U8, "v2_s%d" % half)
-            entries = lists2[:, half * JW // 16 : (half + 1) * JW // 16]
-            nc.vector.tensor_copy(v2_s[half][:], t2s_raw[:].indirect(entries))
-
-        gather_bytes2(0)
+        v2_c[1] = placed([P, JW], U32, "v2_c1", WR_AT)
+        gather_words(v2_c[1][:, :PIECE], t2w, lists2, JW)
         quantise_wr(0, held([P, RB], U32, "wr_c0"))
-        gather_bytes2(1)
-        wf_all = placed([P, 2 * N + N // 2], I32, "wf_all", WR_AT)
+        gather_words(v2_c[1][:, PIECE:], t2w, lists2, JW + PIECE)
+        wf_all = placed([P, 2 * N + N // 2], I32, "wf_all", WR_AT + 4 * JW)
         wf_c = wf_all[:, : 2 * N]
         wf_s = wf_all[:, 2 * N :]
         nc.sync.dma_start(
@@ -372,33 +338,34 @@ def tile_list_phase_match_families_kernel(
                 wf_s[32 * quad : 32 * quad + 4, :].rearrange("p (kp c) -> p kp c", kp=2),
                 wf_scales[:, 4 * quad : 4 * quad + 4, :].rearrange("kp q c -> q kp c").bitcast(I32),
             )
-        shared = placed([P, 6 * JW], F32, "shared", SHARED_AT)
+        shared = placed([P, 10 * JW], F32, "shared", SHARED_AT)
         round_wr(1, shared[:, 3 * JW - 16 : 5 * JW - 16].bitcast(BF16), True)
         take_root()
-        modulus(0, 1, (0, 1, 2, 3), (0, 1, 2))
-        residual(0, 0, (3, 4, 5, 6), 0, JW, placed([P, 4, JW], F32, "dd0_0", FIRST_DIFFS_AT)[:])
+        modulus(0, 1, (0, 1, 4, 5), (0, 1))
+        residual(0, 0, (4, 5, 6, 7), 0, JW, placed([P, 4, JW], F32, "dd0_0", FIRST_DIFFS_AT)[:])
+        modulus(0, 1, (0, 1, 4, 5), (2, 3))
         second_diffs = shared[:, : 4 * JW].rearrange("p (t j) -> p t j", t=4)
-        residual(1, 0, (7, 0, 1, 2), 0, JW, second_diffs, (0, 1))
+        residual(1, 0, (2, 3, 0, 1), 0, JW, second_diffs, (0, 1))
         quantise_wr(1, held([P, RB], U32, "wr_c1"))
-        modulus(0, 1, (0, 1, 2, 3), (3,))
-        residual(1, 0, (7, 0, 1, 2), 0, JW, second_diffs, (2, 3))
-        modulus(1, 1, (4, 5, 6, 3))
+        residual(1, 0, (2, 3, 0, 1), 0, JW, second_diffs, (2, 3))
+        modulus(1, 1, (3, 6, 7, 2), (1, 2, 3, 0))
         take_root()
-        residual(0, 1, (7, 0, 1, 2), 0, JW, held([P, 4, JW], F32, "dd0_1")[:])
+        residual(0, 1, (4, 0, 1, 5), 0, JW, held([P, 4, JW], F32, "dd0_1")[:])
 
         pieces = ((0, PIECE), (PIECE, PIECE // 2), (PIECE + PIECE // 2, PIECE // 2))
-        first = shared[:, 4 * JW :].bitcast(BF16).rearrange("p (j t) -> p j t", t=4)
-        square_on_gpsimd(first[:, :GPSIMD_SQUARES, :], diffs[0, 0, 0][:, :, :GPSIMD_SQUARES])
-        square_on_scalar(first[:, GPSIMD_SQUARES:, :], diffs[0, 0, 0][:, :, GPSIMD_SQUARES:])
-        residual(1, 1, (7, 0, 1, 2), 0, JW, held([P, 4, JW], F32, "dd1_1")[:])
-        second = [held([P, PIECE, 4], BF16, "habs1_0_0", "v_c1_0"), held([P, PIECE, 4], BF16, "habs1_0_1", "v_c1_1")]
+        first = shared[:, 4 * JW : 6 * JW].bitcast(BF16).rearrange("p (j t) -> p j t", t=4)
+        square_on_gpsimd(first, diffs[0, 0, 0])
+        last_diffs = shared[:, 6 * JW - 16 : 10 * JW - 16].rearrange("p (t j) -> p t j", t=4)
+        residual(1, 1, (5, 4, 0, 1), 0, JW, last_diffs, (1, 2, 3))
+        signed_first = sign(0, first, None)
+        residual(1, 1, (5, 4, 0, 1), 0, JW, last_diffs, (0,))
+        second = [held([P, PIECE, 4], BF16, "habs1_0_0", "v_c1_0"), placed([P, PIECE, 4], BF16, "habs1_0_1", STAGED_AT + S)]
         square_on_scalar(second[0][:], diffs[1, 0, 0][:, :, :PIECE])
         third = [placed([P, PIECE, 4], BF16, "habs0_1_%d" % u, WP_ORDERED_AT + 8 * PIECE * u) for u in range(2)]
         for u in range(2):
             square_on_scalar(third[u][:], diffs[0, 1, 0][:, :, u * PIECE : (u + 1) * PIECE])
         square_on_scalar(second[1][:], diffs[1, 0, 0][:, :, PIECE:])
 
-        signed_first = sign(0, first, None)
         signed_second = sign(0, second[0][:], placed([P, 8, P], BF16, "hs_second", FIRST_DIFFS_AT))
         quantise_h(0, 0, 0, signed_first)
         for u in range(2):

@@ -61,29 +61,36 @@ def tile_list_phase_match_families_kernel(
         ts_raw = placed([P, T], U8, "ts_raw", WR_AT)
         t2s_raw = placed([P, T], U8, "t2s_raw", WR_SECOND_AT)
         wps_raw = held([P, H], U8, "wps_raw")
-        wp_raw = held([P, 2, RB], I32, "wp_raw")
+        wp_raw = [held([P, 2, RB // 2], I32, "wp_raw%d" % blk) for blk in range(2)]
         tw = [held([P, T], I32, "tw%d" % kp) for kp in range(2)]
 
         nc.vector.memset(ts_raw[:, :VECTOR_CLEARS].bitcast(I32), 0)
         nc.gpsimd.memset(ts_raw[:, VECTOR_CLEARS:].bitcast(I32), 0)
         nc.vector.memset(wps_raw[:].bitcast(I32), 0)
-        nc.gpsimd.memset(t2s_raw[:].bitcast(I32), 0)
+        nc.vector.memset(t2s_raw[:].bitcast(I32), 0)
 
         def load_wr(blk):
             nc.sync.dma_start(
                 wr_raw[blk][:], wr[:, RB * blk : RB * (blk + 1)].rearrange("(p i) c -> p i c", i=4)
             )
 
+        def load_wp(blk):
+            nc.sync.dma_start(
+                wp_raw[blk][:],
+                wp_words[:, :, 2 * RB * blk : 2 * RB * (blk + 1)].rearrange("kp p c -> p kp c").bitcast(I32),
+            )
+
         def load_table(kp):
             nc.sync.dma_start(tw[kp][:], tab_words[kp].rearrange("p c i -> p (c i)").bitcast(I32))
 
         nc.sync.dma_start(lists[:], offs)
+        load_wp(0)
         nc.sync.dma_start(lists2[:], offs2)
-        nc.sync.dma_start(g_raw[:], gain.rearrange("(blk p t) -> p blk t", blk=2, t=4))
         nc.sync.dma_start(ts_raw[0:P:4, :].bitcast(I32), tab_scales.rearrange("kp q c -> q kp c").bitcast(I32))
         nc.sync.dma_start(wps_raw[0:P:4, :].bitcast(I32), wp_scales.rearrange("kp q c -> q kp c").bitcast(I32))
-        nc.sync.dma_start(wp_raw[:], wp_words.rearrange("kp p c -> p kp c").bitcast(I32))
+        load_wp(1)
         load_table(0)
+        nc.sync.dma_start(g_raw[:], gain.rearrange("(blk p t) -> p blk t", blk=2, t=4))
         nc.sync.dma_start(t2s_raw[0:P:8, :].bitcast(I32), tab2_scales[0].bitcast(I32))
         load_table(1)
 
@@ -123,7 +130,7 @@ def tile_list_phase_match_families_kernel(
         for blk in range(2):
             nc.scalar.copy(
                 wp_c[blk][:].bitcast(U16).rearrange("p (kp t c) -> p kp t c", kp=2, t=4),
-                wp_raw[:].bitcast(U16)[:, :, blk * RB : (blk + 1) * RB].rearrange("p kp (c t) -> p kp t c", t=4),
+                wp_raw[blk][:].bitcast(U16).rearrange("p kp (c t) -> p kp t c", t=4),
             )
 
         v_c = {}

@@ -25,9 +25,9 @@ VECTOR_CLEARS = T // 4
 GPSIMD_SQUARES = 7 * JW // 8
 
 WR_AT = 0
-SECOND_PICKS_AT = WR_AT + 16 * RB
-TAB2_WORDS_AT = SECOND_PICKS_AT + JW
-FIRST_PICKS_AT = TAB2_WORDS_AT - 64
+TAB2_WORDS_AT = WR_AT + 16 * RB
+SECOND_PICKS_AT = TAB2_WORDS_AT - (S - PIECE) // 2
+FIRST_PICKS_AT = SECOND_PICKS_AT - PIECE + 64
 SHARED_AT = TAB2_WORDS_AT + 4 * T - 64
 STAGED_AT = SHARED_AT + 40 * JW
 WR_SECOND_AT = STAGED_AT + S + 4 * JW
@@ -94,8 +94,6 @@ def tile_list_phase_match_families_kernel(
         nc.sync.dma_start(t2s_raw[0:P:8, :].bitcast(I32), tab2_scales[0].bitcast(I32))
         load_table(1)
 
-        def gather_bytes(half, picks):
-            nc.vector.tensor_copy(picks, ts_raw[:].indirect(lists[:, half * JW // 16 : (half + 1) * JW // 16]))
 
         def move_rows(planes, rows):
             for quad in (0, 2, 1, 3):
@@ -104,16 +102,31 @@ def tile_list_phase_match_families_kernel(
                     rows[32 * quad : 32 * quad + 32 : 4, :].bitcast(I32),
                 )
 
-        first_got = placed([P, JW], U8, "first_got", FIRST_PICKS_AT)[:]
-        staged = placed([P, JW + H], U8, "staged", STAGED_AT)
-        plane = held([P, 2, JW + H], U8, "plane")
-        gather_bytes(0, first_got)
-        nc.vector.tensor_copy(
-            staged[:, JW:].rearrange("p (blk t c) -> p blk t c", blk=2, t=4),
-            wps_raw[:].rearrange("p (blk c t) -> p blk t c", blk=2, t=4),
+        def make_planes(blk, j0, picks, staged):
+            width = picks.shape[1]
+            planes = held([P, 2, width + RB], U8, "planes%d" % blk)
+            nc.vector.tensor_copy(picks[:], ts_raw[:].indirect(lists[:, j0 // 16 : (j0 + width) // 16]))
+            nc.vector.tensor_copy(
+                staged[:, width:].rearrange("p (t c) -> p t c", t=4),
+                wps_raw[:, blk * RB : (blk + 1) * RB].rearrange("p (c t) -> p t c", t=4),
+            )
+            nc.vector.tensor_copy(staged[:, :width].bitcast(I32), picks[:].bitcast(I32))
+            move_rows(planes, staged)
+            return planes
+
+        early = make_planes(
+            0, 0, placed([P, PIECE], U8, "first_got", FIRST_PICKS_AT), held([P, PIECE + RB], U8, "staged0")
         )
-        nc.vector.tensor_copy(staged[:, :JW].bitcast(I32), first_got.bitcast(I32))
-        move_rows(plane, staged)
+        late = make_planes(
+            1, PIECE, placed([P, S - PIECE], U8, "second_got", SECOND_PICKS_AT),
+            placed([P, S - PIECE + RB], U8, "staged1", STAGED_AT),
+        )
+        wp_s = (early[:, :, PIECE:], late[:, :, S - PIECE :])
+
+        def picked_scales(kp, entry, width):
+            if entry < PIECE:
+                return early[:, kp, entry : entry + width]
+            return late[:, kp, entry - PIECE : entry - PIECE + width]
 
         gains = g_raw[:].rearrange("p blk t -> p (blk t)")
         gabs = keep.tile([P, 8], F32, name="gabs")
@@ -139,8 +152,6 @@ def tile_list_phase_match_families_kernel(
             width = picks.shape[1]
             nc.vector.tensor_copy(picks, words[:].bitcast(U32).indirect(offsets[:, j0 // 16 : (j0 + width) // 16]))
 
-        second_got = placed([P, JW], U8, "second_got", SECOND_PICKS_AT)
-        gather_bytes(1, second_got[:])
         for half in range(2):
             v_c[half, 0] = held([P, JW], U32, "v_c0_%d" % half)
             gather_words(v_c[half, 0][:], tw[0], lists, half * JW)
@@ -150,9 +161,6 @@ def tile_list_phase_match_families_kernel(
 
         t2w = placed([P, T], I32, "t2w", TAB2_WORDS_AT)
         nc.sync.dma_start(t2w[:], tab2_words[0].rearrange("p c i -> p (c i)").bitcast(I32))
-        late_plane = held([P, 2, JW], U8, "late_plane")
-        move_rows(late_plane, second_got)
-        v_s = (plane, late_plane)
         wr_raw = {0: placed([P, 4, RB], F32, "wr_raw0", WR_AT)}
         load_wr(0)
 
@@ -206,16 +214,17 @@ def tile_list_phase_match_families_kernel(
                 if kp == 0:
                     accs[t] = psum_bank(banks[t])[:, :width]
                 word0 = kp * RB + t * P
-                scale0 = JW + blk * RB + t * P
-                nc.tensor.matmul_mx(
-                    out=accs[t],
-                    lhsT=wp_c[blk][:, 2 * word0 : 2 * (word0 + P)].bitcast(FP4X4),
-                    lhsT_scale=plane[:, kp, scale0 : scale0 + P],
-                    rhs=v_c[half, kp][:, entries].bitcast(FP8X4),
-                    rhs_scale=v_s[half][:, kp, entries],
-                    start=(kp == 0),
-                    stop=(kp == 1),
-                )
+                cuts = (j0, PIECE, j0 + width) if half == 0 and j0 < PIECE < j0 + width else (j0, j0 + width)
+                for first, end in zip(cuts, cuts[1:]):
+                    nc.tensor.matmul_mx(
+                        out=accs[t][:, first - j0 : end - j0],
+                        lhsT=wp_c[blk][:, 2 * word0 : 2 * (word0 + P)].bitcast(FP4X4),
+                        lhsT_scale=wp_s[blk][:, kp, t * P : (t + 1) * P],
+                        rhs=v_c[half, kp][:, first:end].bitcast(FP8X4),
+                        rhs_scale=picked_scales(kp, half * JW + first, end - first),
+                        start=(kp == 0 and first == j0),
+                        stop=(kp == 1 and end == j0 + width),
+                    )
 
             for t in range(ahead):
                 product(t, 0)
@@ -313,12 +322,12 @@ def tile_list_phase_match_families_kernel(
                         for n, queue in enumerate((nc.sync, nc.scalar)):
                             queue.dma_start(out[n * P : (n + 1) * P, c0 : c0 + stored], results[-1][:, n, :])
 
-        modulus(0, 0, (0, 1, 2, 3), ahead=2, width=PIECE)
+        modulus(0, 0, (0, 1, 2, 3), width=PIECE)
         modulus(0, 0, (4, 5, 6, 7), j0=PIECE, width=PIECE)
-        t2_got = placed([P, S], U8, "t2_got", STAGED_AT)
-        nc.vector.tensor_copy(t2_got[:], t2s_raw[:].indirect(lists2[:]))
         v_c[1, 1] = placed([P, JW], U32, "v_c1_1", STAGED_AT + S)
         gather_words(v_c[1, 1][:], tw[1], lists, JW)
+        t2_got = placed([P, S], U8, "t2_got", STAGED_AT)
+        nc.vector.tensor_copy(t2_got[:], t2s_raw[:].indirect(lists2[:]))
         v2_s = held([P, S], U8, "v2_s")
         for quad in (0, 2, 1, 3):
             nc.sync.dma_start(

from contextlib import ExitStack

import concourse.mybir as mybir

K, K2, H, N, T, S = 1024, 512, 1024, 256, 2048, 1024
FLOPS = 2 * S * (K * H + K2 * H + H * N)

F32 = mybir.dt.float32
BF16 = mybir.dt.bfloat16
I32 = mybir.dt.int32
U32 = mybir.dt.uint32
U16 = mybir.dt.uint16
U8 = mybir.dt.uint8
FP8X4 = mybir.dt.float8_e4m3fn_x4
FP4X4 = mybir.dt.float4_e2m1fn_x4
ALU = mybir.AluOpType
ACT = mybir.ActivationFunctionType

P = 128
JW = 512
RB = 512
PIECE = 256
VECTOR_CLEARS = T // 4

GPSIMD_SQUARES = 7 * JW // 8

WR_AT = 0
TAB2_WORDS_AT = WR_AT + 16 * RB
SECOND_PICKS_AT = TAB2_WORDS_AT - (S - PIECE) // 2
FIRST_PICKS_AT = SECOND_PICKS_AT - PIECE + 64
SHARED_AT = TAB2_WORDS_AT + 4 * T - 64
STAGED_AT = SHARED_AT + 40 * JW
WR_SECOND_AT = STAGED_AT + S + 4 * JW
FIRST_DIFFS_AT = WR_SECOND_AT + 16 * RB
WP_ORDERED_AT = FIRST_DIFFS_AT + 16 * JW


def tile_list_phase_match_families_kernel(
    tc, tab_words, tab_scales, offs, tab2_words, tab2_scales, offs2,
    wp_words, wp_scales, wr, gain, wf_words, wf_scales, out,
):
    nc = tc.nc
    with ExitStack() as ctx:
        keep = ctx.enter_context(tc.tile_pool(name="keep", bufs=1))
        reuse = ctx.enter_context(tc.tile_pool(name="reuse", bufs=1))
        sqp = ctx.enter_context(tc.tile_pool(name="sqp", bufs=3))
        psr = ctx.enter_context(tc.psum_pool(name="psr", bufs=1))

        def held(shape, dtype, name, buffer=None):
            return keep.tile(shape, dtype, name=name, tag=buffer or name, align_bytes=64)

        def placed(shape, dtype, name, offset):
            return reuse.tile(shape, dtype, name=name, offset=offset, align_bytes=64)

        def psum_bank(number):
            return psr.tile([P, JW], F32, name="bank", tag="bank%d" % number)

        lists = keep.tile([P, S // 16], U16, name="lists")
        lists2 = keep.tile([P, S // 16], U16, name="lists2")
        g_raw = held([P, 2, 4], F32, "g_raw")
        ts_raw = placed([P, T], U8, "ts_raw", WR_AT)
        t2s_raw = placed([P, T], U8, "t2s_raw", WR_SECOND_AT)
        wps_raw = held([P, H], U8, "wps_raw")
        wp_raw = [held([P, 2, RB // 2], I32, "wp_raw%d" % blk) for blk in range(2)]
        tw = [held([P, T], I32, "tw%d" % kp) for kp in range(2)]

        nc.vector.memset(ts_raw[:, :VECTOR_CLEARS].bitcast(I32), 0)
        nc.gpsimd.memset(ts_raw[:, VECTOR_CLEARS:].bitcast(I32), 0)
        nc.vector.memset(wps_raw[:].bitcast(I32), 0)
        nc.vector.memset(t2s_raw[:].bitcast(I32), 0)

        def load_wr(blk):
            nc.sync.dma_start(
                wr_raw[blk][:], wr[:, RB * blk : RB * (blk + 1)].rearrange("(p i) c -> p i c", i=4)
            )

        def load_wp(blk):
            nc.sync.dma_start(
                wp_raw[blk][:],
                wp_words[:, :, 2 * RB * blk : 2 * RB * (blk + 1)].rearrange("kp p c -> p kp c").bitcast(I32),
            )

        def load_table(kp):
            nc.sync.dma_start(tw[kp][:], tab_words[kp].rearrange("p c i -> p (c i)").bitcast(I32))

        nc.sync.dma_start(lists[:], offs)
        load_wp(0)
        nc.sync.dma_start(lists2[:], offs2)
        nc.sync.dma_start(ts_raw[0:P:4, :].bitcast(I32), tab_scales.rearrange("kp q c -> q kp c").bitcast(I32))
        nc.sync.dma_start(wps_raw[0:P:4, :].bitcast(I32), wp_scales.rearrange("kp q c -> q kp c").bitcast(I32))
        load_wp(1)
        load_table(0)
        nc.sync.dma_start(g_raw[:], gain.rearrange("(blk p t) -> p blk t", blk=2, t=4))
        nc.sync.dma_start(t2s_raw[0:P:8, :].bitcast(I32), tab2_scales[0].bitcast(I32))
        load_table(1)


        def move_rows(planes, rows):
            for quad in (0, 2, 1, 3):
                nc.sync.dma_start(
                    planes[32 * quad : 32 * quad + 4, :, :].rearrange("p kp c -> p (kp c)").bitcast(I32),
                    rows[32 * quad : 32 * quad + 32 : 4, :].bitcast(I32),
                )

        def make_planes(blk, j0, picks, staged):
            width = picks.shape[1]
            planes = held([P, 2, width + RB], U8, "planes%d" % blk)
            nc.vector.tensor_copy(picks[:], ts_raw[:].indirect(lists[:, j0 // 16 : (j0 + width) // 16]))
            nc.vector.tensor_copy(
                staged[:, width:].rearrange("p (t c) -> p t c", t=4),
                wps_raw[:, blk * RB : (blk + 1) * RB].rearrange("p (c t) -> p t c", t=4),
            )
            nc.vector.tensor_copy(staged[:, :width].bitcast(I32), picks[:].bitcast(I32))
            move_rows(planes, staged)
            return planes

        early = make_planes(
            0, 0, placed([P, PIECE], U8, "first_got", FIRST_PICKS_AT), held([P, PIECE + RB], U8, "staged0")
        )
        late = make_planes(
            1, PIECE, placed([P, S - PIECE], U8, "second_got", SECOND_PICKS_AT),
            placed([P, S - PIECE + RB], U8, "staged1", STAGED_AT),
        )
        wp_s = (early[:, :, PIECE:], late[:, :, S - PIECE :])

        def picked_scales(kp, entry, width):
            if entry < PIECE:
                return early[:, kp, entry : entry + width]
            return late[:, kp, entry - PIECE : entry - PIECE + width]

        gains = g_raw[:].rearrange("p blk t -> p (blk t)")
        gabs = keep.tile([P, 8], F32, name="gabs")
        groot = keep.tile([P, 8], F32, name="groot")
        gbias = keep.tile([P, 8], F32, name="gbias")
        nc.scalar.activation(gabs[:], gains, ACT.Abs)
        signs = held([P, 2, P // 4, 4], BF16, "signs")
        nc.scalar.activation(signs[:], g_raw[:].unsqueeze(2).to_broadcast([P, 2, P // 4, 4]), ACT.Sign)

        nc.scalar.activation(groot[:], gabs[:], ACT.Sqrt)
        nc.scalar.activation(gbias[:], gabs[:], ACT.Copy, scale=0.1)

        wp_c = [held([P, 2 * 2 * RB], U8, "wp_c0"), placed([P, 2 * 2 * RB], U8, "wp_c1", WP_ORDERED_AT)]
        for blk in range(2):
            nc.scalar.copy(
                wp_c[blk][:].bitcast(U16).rearrange("p (kp t c) -> p kp t c", kp=2, t=4),
                wp_raw[blk][:].bitcast(U16).rearrange("p kp (c t) -> p kp t c", t=4),
            )

        v_c = {}

        def gather_words(picks, words, offsets, j0):
            width = picks.shape[1]
            nc.vector.tensor_copy(picks, words[:].bitcast(U32).indirect(offsets[:, j0 // 16 : (j0 + width) // 16]))

        for half in range(2):
            v_c[half, 0] = held([P, JW], U32, "v_c0_%d" % half)
            gather_words(v_c[half, 0][:], tw[0], lists, half * JW)
        v_c[0, 1] = held([P, JW], U32, "v_c1_0")
        for j0 in (0, PIECE):
            gather_words(v_c[0, 1][:, j0 : j0 + PIECE], tw[1], lists, j0)

        t2w = placed([P, T], I32, "t2w", TAB2_WORDS_AT)
        nc.sync.dma_start(t2w[:], tab2_words[0].rearrange("p c i -> p (c i)").bitcast(I32))
        wr_raw = {0: placed([P, 4, RB], F32, "wr_raw0", WR_AT)}
        load_wr(0)

        v2_c = {}

        wr_g = {}
        wr_c = {}
        wr_s = [held([P, RB], U8, "wr_s%d" % blk) for blk in range(2)]

        def round_wr(blk, rounded, on_gpsimd):
            wr_g[blk] = rounded
            if on_gpsimd:
                nc.gpsimd.tensor_scalar(
                    rounded.rearrange("p (t c i) -> p c t i", t=4, i=4),
                    wr_raw[blk][:].rearrange("p i (c t) -> p c t i", t=4),
                    1.0, 0.0, ALU.mult, ALU.add,
                )
            else:
                nc.vector.tensor_copy(
                    rounded.rearrange("p (t c i) -> p c i t", t=4, i=4),
                    wr_raw[blk][:].rearrange("p i (c t) -> p c i t", t=4),
                )

        def quantise_wr(blk, codes):
            wr_c[blk] = codes
            nc.vector.quantize_mx(out=wr_c[blk][:].bitcast(FP8X4), scales=wr_s[blk][:], in_=wr_g[blk])

        moduli = {}
        diffs = {}
        fields = {}
        sums = {}
        results = []
        waiting_root = []
        signed_tiles = []

        def take_root():
            half, blk, t, entries, sq = waiting_root.pop()
            col = 4 * blk + t
            nc.scalar.activation(
                moduli[half, blk][:, t, entries], sq, ACT.Sqrt,
                bias=gbias[:, col : col + 1], scale=gabs[:, col : col + 1],
            )

        def modulus(half, blk, banks, tiles=range(4), ahead=0, j0=0, width=JW):
            if (half, blk) not in moduli:
                moduli[half, blk] = held([P, 4, JW], F32, "f%d_%d" % (half, blk))
            accs = {}
            entries = slice(j0, j0 + width)

            def product(t, kp):
                if kp == 0:
                    accs[t] = psum_bank(banks[t])[:, :width]
                word0 = kp * RB + t * P
                cuts = (j0, PIECE, j0 + width) if half == 0 and j0 < PIECE < j0 + width else (j0, j0 + width)
                for first, end in zip(cuts, cuts[1:]):
                    nc.tensor.matmul_mx(
                        out=accs[t][:, first - j0 : end - j0],
                        lhsT=wp_c[blk][:, 2 * word0 : 2 * (word0 + P)].bitcast(FP4X4),
                        lhsT_scale=wp_s[blk][:, kp, t * P : (t + 1) * P],
                        rhs=v_c[half, kp][:, first:end].bitcast(FP8X4),
                        rhs_scale=picked_scales(kp, half * JW + first, end - first),
                        start=(kp == 0 and first == j0),
                        stop=(kp == 1 and end == j0 + width),
                    )

            for t in range(ahead):
                product(t, 0)
            for t in tiles:
                if t >= ahead:
                    product(t, 0)
                product(t, 1)
                sq = sqp.tile([P, JW], F32, name="sq")[:, :width]
                nc.scalar.activation(sq, accs[t], ACT.Square)
                if waiting_root:
                    take_root()
                waiting_root.append((half, blk, t, entries, sq))

        def residual(half, blk, banks, j0, width, tile, steps=range(4)):
            diffs[half, blk, j0] = tile
            in_bank = JW // width
            entries = slice(j0, j0 + width)
            for step in steps:
                acc = psum_bank(banks[step])
                for place in range(in_bank):
                    t = step * in_bank + place
                    nc.tensor.matmul_mx(
                        out=acc[:, place * width : (place + 1) * width],
                        lhsT=wr_c[blk][:, t * P : (t + 1) * P].bitcast(FP8X4),
                        lhsT_scale=wr_s[blk][:, t * P : (t + 1) * P],
                        rhs=v2_c[half][:, entries].bitcast(FP8X4),
                        rhs_scale=v2_s[:, half * JW + j0 : half * JW + j0 + width],
                        start=True,
                        stop=True,
                    )
                for place in range(in_bank):
                    t = step * in_bank + place
                    col = 4 * blk + t
                    nc.vector.scalar_tensor_tensor(
                        tile[:, t, :], acc[:, place * width : (place + 1) * width],
                        groot[:, col : col + 1], moduli[half, blk][:, t, entries], ALU.mult, ALU.subtract,
                    )

        def square_on_gpsimd(habs, rows):
            woven = rows.rearrange("p t j -> p j t")
            nc.gpsimd.tensor_tensor(habs, woven, woven, ALU.mult)

        def square_on_scalar(habs, rows):
            nc.scalar.activation(
                habs.rearrange("p (c j) t -> p c t j", j=2), rows.rearrange("p t (c j) -> p c t j", j=2), ACT.Square
            )

        def sign(blk, habs, hs=None):
            runs = habs.shape[1] * 4 // P
            if hs is None:
                hs = held([P, runs, P], BF16, "hs%d" % len(signed_tiles))
                signed_tiles.append(hs)
            nc.vector.tensor_tensor(
                hs[:],
                habs.rearrange("p (c j) t -> p c (j t)", c=runs),
                signs[:, blk, :, :].rearrange("p j t -> p (j t)").unsqueeze(1).to_broadcast([P, runs, P]),
                ALU.mult,
            )
            return hs

        def quantise_h(half, blk, j0, hs, buffer=None):
            width = hs.shape[1] * P // 4
            h_c = held([P, width], U32, "h_c%d_%d_%d" % (half, blk, j0), buffer)
            h_s = held([P, width], U8, "h_s%d_%d_%d" % (half, blk, j0))
            nc.vector.quantize_mx(out=h_c[:].bitcast(FP8X4), scales=h_s[:], in_=hs[:].rearrange("p c x -> p (c x)"))
            fields[half, blk] = (h_c, h_s, j0)

        def scores(half, blk, j0, width, copy=nc.scalar.copy):
            if blk == 0:
                sums[half, j0] = psum_bank((6, 7, 2, 3, 4)[len(sums)])[:, : 2 * width].rearrange("p (n c) -> p n c", n=2)
            acc = sums[half, j0]
            h_c, h_s, h_first = fields[half, blk]
            entries = slice(j0 - h_first, j0 - h_first + width)
            for n in range(2):
                columns = slice(blk * N + n * P, blk * N + (n + 1) * P)
                nc.tensor.matmul_mx(
                    out=acc[:, n, :],
                    lhsT=wf_c[:, columns].bitcast(FP8X4),
                    lhsT_scale=wf_s.bitcast(U8)[:, columns],
                    rhs=h_c[:, entries].bitcast(FP8X4),
                    rhs_scale=h_s[:, entries],
                    start=(blk, n) == (0, 0),
                    stop=(blk, n) == (1, 1),
                )
            if blk == 1:
                stored = (PIECE, JW)[half]
                if j0 % stored == 0:
                    results.append(held([P, 2, stored], F32, "res%d" % len(results)))
                copy(results[-1][:, :, j0 % stored : j0 % stored + width], acc)
                if (j0 + width) % stored == 0:
                    c0 = half * JW + j0 + width - stored
                    if half == 0:
                        nc.sync.dma_start(out[:, c0 : c0 + stored].rearrange("(n p) c -> p n c", n=2), results[-1][:])
                    else:
                        for n, queue in enumerate((nc.sync, nc.scalar)):
                            queue.dma_start(out[n * P : (n + 1) * P, c0 : c0 + stored], results[-1][:, n, :])

        modulus(0, 0, (0, 1, 2, 3), width=PIECE)
        modulus(0, 0, (4, 5, 6, 7), j0=PIECE, width=PIECE)
        v_c[1, 1] = placed([P, JW], U32, "v_c1_1", STAGED_AT + S)
        gather_words(v_c[1, 1][:], tw[1], lists, JW)
        t2_got = placed([P, S], U8, "t2_got", STAGED_AT)
        nc.vector.tensor_copy(t2_got[:], t2s_raw[:].indirect(lists2[:]))
        v2_s = held([P, S], U8, "v2_s")
        for quad in (0, 2, 1, 3):
            nc.sync.dma_start(
                v2_s[32 * quad : 32 * quad + 4, :].bitcast(I32), t2_got[32 * quad : 32 * quad + 32 : 8, :].bitcast(I32)
            )
        wr_raw[1] = placed([P, 4, RB], F32, "wr_raw1", WR_SECOND_AT)
        load_wr(1)
        modulus(1, 0, (0, 1, 2, 3))
        v2_c[0] = held([P, JW], U32, "v2_c0")
        gather_words(v2_c[0][:], t2w, lists2, 0)
        round_wr(0, held([P, 4 * RB], BF16, "wr_g0")[:], False)
        v2_c[1] = placed([P, JW], U32, "v2_c1", WR_AT)
        gather_words(v2_c[1][:, :PIECE], t2w, lists2, JW)
        quantise_wr(0, held([P, RB], U32, "wr_c0"))
        gather_words(v2_c[1][:, PIECE:], t2w, lists2, JW + PIECE)
        wf_all = placed([P, 2 * N + N // 2], I32, "wf_all", WR_AT + 4 * JW)
        wf_c = wf_all[:, : 2 * N]
        wf_s = wf_all[:, 2 * N :]
        nc.sync.dma_start(
            wf_c.rearrange("p (kp c) -> p kp c", kp=2), wf_words.rearrange("kp p c i -> p kp (c i)").bitcast(I32)
        )
        for quad in range(4):
            nc.sync.dma_start(
                wf_s[32 * quad : 32 * quad + 4, :].rearrange("p (kp c) -> p kp c", kp=2),
                wf_scales[:, 4 * quad : 4 * quad + 4, :].rearrange("kp q c -> q kp c").bitcast(I32),
            )
        shared = placed([P, 10 * JW], F32, "shared", SHARED_AT)
        round_wr(1, shared[:, 3 * JW - 16 : 5 * JW - 16].bitcast(BF16), True)
        take_root()
        modulus(0, 1, (0, 1, 4, 5), (0, 1))
        residual(0, 0, (4, 5, 6, 7), 0, JW, placed([P, 4, JW], F32, "dd0_0", FIRST_DIFFS_AT)[:])
        modulus(0, 1, (0, 1, 4, 5), (2, 3))
        second_diffs = shared[:, : 4 * JW].rearrange("p (t j) -> p t j", t=4)
        residual(1, 0, (2, 3, 0, 1), 0, JW, second_diffs, (0, 1))
        quantise_wr(1, held([P, RB], U32, "wr_c1"))
        residual(1, 0, (2, 3, 0, 1), 0, JW, second_diffs, (2, 3))
        modulus(1, 1, (3, 6, 7, 2), (1, 2, 3, 0))
        take_root()
        residual(0, 1, (4, 0, 1, 5), 0, JW, held([P, 4, JW], F32, "dd0_1")[:])

        pieces = ((0, PIECE), (PIECE, PIECE // 2), (PIECE + PIECE // 2, PIECE // 2))
        first = shared[:, 4 * JW : 6 * JW].bitcast(BF16).rearrange("p (j t) -> p j t", t=4)
        square_on_gpsimd(first, diffs[0, 0, 0])
        last_diffs = shared[:, 6 * JW - 16 : 10 * JW - 16].rearrange("p (t j) -> p t j", t=4)
        residual(1, 1, (5, 4, 0, 1), 0, JW, last_diffs, (1, 2, 3))
        signed_first = sign(0, first, None)
        residual(1, 1, (5, 4, 0, 1), 0, JW, last_diffs, (0,))
        second = [held([P, PIECE, 4], BF16, "habs1_0_0", "v_c1_0"), placed([P, PIECE, 4], BF16, "habs1_0_1", STAGED_AT + S)]
        square_on_scalar(second[0][:], diffs[1, 0, 0][:, :, :PIECE])
        third = [placed([P, PIECE, 4], BF16, "habs0_1_%d" % u, WP_ORDERED_AT + 8 * PIECE * u) for u in range(2)]
        for u in range(2):
            square_on_scalar(third[u][:], diffs[0, 1, 0][:, :, u * PIECE : (u + 1) * PIECE])
        square_on_scalar(second[1][:], diffs[1, 0, 0][:, :, PIECE:])

        signed_second = sign(0, second[0][:], placed([P, 8, P], BF16, "hs_second", FIRST_DIFFS_AT))
        quantise_h(0, 0, 0, signed_first)
        for u in range(2):
            scores(0, 0, u * PIECE, PIECE)
        signed_third = [
            placed([P, 8, P], BF16, "hs_third%d" % u, FIRST_DIFFS_AT + 8 * JW + 8 * PIECE * u) for u in range(2)
        ]
        sign(1, third[0][:], signed_third[0])
        quantise_h(1, 0, 0, signed_second)
        scores(1, 0, 0, PIECE)
        sign(1, third[1][:], signed_third[1])
        quantise_h(0, 1, 0, signed_third[0])
        scores(0, 1, 0, PIECE)
        signed_rest = sign(0, second[1][:], placed([P, 8, P], BF16, "hs_rest", FIRST_DIFFS_AT + 8 * PIECE))
        quantise_h(0, 1, PIECE, signed_third[1])
        scores(0, 1, PIECE, PIECE)
        last = {}
        for j0, width in pieces:
            last[j0] = held([P, width, 4], BF16, "habs1_1_%d" % j0)
            square_on_scalar(last[j0][:], diffs[1, 1, 0][:, :, j0 : j0 + width])
        signed_last = [sign(1, last[0][:])]
        quantise_h(1, 0, PIECE, signed_rest)
        for j0, width in pieces[1:]:
            scores(1, 0, j0, width)
        for number, (j0, width) in enumerate(pieces):
            if j0 + width < JW:
                signed_last.append(sign(1, last[j0 + width][:]))
            quantise_h(1, 1, j0, signed_last[number])
            scores(1, 1, j0, width, nc.vector.tensor_copy if j0 + width == JW else nc.scalar.copy)
